import numpy as np
import ml_dtypes


def mxq(x, axis, fmt="e4m3"):
    dtype, down = {"e4m3": (ml_dtypes.float8_e4m3fn, 7), "e5m2": (ml_dtypes.float8_e5m2, 14)}[fmt]
    v = np.moveaxis(np.asarray(x, np.float32).astype(ml_dtypes.bfloat16).astype(np.float64), axis, -1)
    blocks = v.reshape(v.shape[:-1] + (-1, 32))
    amax = np.abs(blocks).max(-1, keepdims=True)
    byte = np.maximum(np.where(amax > 0, np.frexp(amax)[1] - 1 + 127, 0) - down, 1)
    scale = np.exp2(byte - 127.0)
    codes = (blocks / scale).astype(np.float32).astype(dtype).astype(np.float64)
    return np.moveaxis((codes * scale).reshape(v.shape), -1, axis)


WIDE = False


def mx_kscale(k):
    if not WIDE:
        return np.ones(k)
    levels = np.array([10, -10, 5, -5, 0])
    if k % 512:
        return np.exp2(np.random.permutation(np.resize(levels, k // 32))).repeat(32)
    a = np.empty((k // 512, 16))
    for p in range(k // 512):
        a[p, :8] = np.random.permutation(np.resize(levels, 8))
        for g in range(8):
            far = levels[np.abs(levels - a[p, g]) >= 10]
            a[p, g + 8] = far[np.random.randint(len(far))]
    return np.exp2(a.ravel()).repeat(32)


def f64(x):
    return np.asarray(x).astype(np.float64)


def striped(idx):
    return np.tile(idx.reshape(-1, 16).T, (8, 1)).astype(np.uint16)


def unstriped(offs):
    return offs[:16].T.reshape(-1).astype(np.int64)


E2M1 = np.array([0.0, 0.5, 1.0, 1.5, 2.0, 3.0, 4.0, 6.0, -0.0, -0.5, -1.0, -1.5, -2.0, -3.0, -4.0, -6.0])


def pack_weight(w, fmt):
    k, n = w.shape
    w = f64(np.asarray(w, np.float32).astype(ml_dtypes.bfloat16)).reshape(k // 32, 32, n)
    amax = np.abs(w).max(1)
    if fmt == "e4m3":
        byte = np.frexp(amax)[1] - 1 + 127 - 7
    else:
        mant, ex = np.frexp(amax / 6.0)
        byte = np.where(mant > 0.5, ex, ex - 1) + 127
    byte = np.clip(np.where(amax > 0, byte, 1), 1, 254)
    scaled = (w * np.exp2(127.0 - byte)[:, None, :]).reshape(k, n).astype(np.float32)
    by_word = np.ascontiguousarray(scaled.reshape(k // 512, 128, 4, n).transpose(0, 1, 3, 2))
    if fmt == "e4m3":
        words = by_word.astype(ml_dtypes.float8_e4m3fn).view(np.uint8)
    else:
        c = by_word.astype(ml_dtypes.float4_e2m1fn).view(np.uint8) & 0xF
        words = (c[..., 0::2] | (c[..., 1::2] << 4)).reshape(k // 512, 128, 2 * n)
    return np.ascontiguousarray(words), np.ascontiguousarray(byte.astype(np.uint8).reshape(k // 512, 16, n))


def unpack_weight(words, scales, fmt):
    g, _, n = scales.shape
    words = np.ascontiguousarray(words).reshape(g, 128, n, -1)
    if fmt == "e4m3":
        vals = words.view(ml_dtypes.float8_e4m3fn).astype(np.float64)
    else:
        nib = np.empty((g, 128, n, 4), np.uint8)
        nib[..., 0::2] = words & 0xF
        nib[..., 1::2] = words >> 4
        vals = E2M1[nib]
    vals = vals * np.repeat(np.exp2(scales.astype(np.float64) - 127.0), 8, axis=1)[..., None]
    return vals.transpose(0, 1, 3, 2).reshape(g * 512, n)


def gelu(v):
    return 0.5 * v * (1.0 + np.tanh(np.sqrt(2.0 / np.pi) * (v + 0.044715 * v**3)))


K, T, S, T2, S2, N = 1536, 4096, 1024, 2048, 512, 512

def setup_inputs():
    n = np.random.standard_normal
    s = mx_kscale(K)[:, None]
    u = mx_kscale(S)[:, None]
    tab_words, tab_scales = pack_weight(n((K, T)) * s / np.sqrt(K), "e4m3")
    tab2_words, tab2_scales = pack_weight(n((K, T2)) / s, "e4m3")
    w4_words, w4_scales = pack_weight(n((S, N)) / np.sqrt(S) / u, "e2m1")
    return {
        "tab_words": tab_words, "tab_scales": tab_scales,
        "tab2_words": tab2_words, "tab2_scales": tab2_scales,
        "offs": striped(np.random.permutation(T)[:S]),
        "offs2": striped(np.random.permutation(T2)[:S2]),
        "size": (np.exp(0.3 * n(S)) * u[:, 0]).astype(np.float32),
        "wd": (n((S, N)) / np.sqrt(S) / u).astype(np.float32),
        "w4_words": w4_words, "w4_scales": w4_scales,
    }

def reference(tab_words, tab_scales, tab2_words, tab2_scales, offs, offs2, size, wd, w4_words, w4_scales):
    v = unpack_weight(tab_words, tab_scales, "e4m3")[:, unstriped(offs)]
    v2 = unpack_weight(tab2_words, tab2_scales, "e4m3")[:, unstriped(offs2)]
    c = v.T @ v2
    r = np.abs(c)
    d = f64(size)[:, None] / (1.0 + r)
    h = mxq(c * d, 0, "e4m3")
    g = mxq(r * d, 0, "e4m3")
    w4 = unpack_weight(w4_words, w4_scales, "e2m1")
    wdq = mxq(f64(wd), 0, "e4m3")
    return wdq.T @ h + w4.T @ g

@@ -1,0 +1,259 @@
+from contextlib import ExitStack
+
+import concourse.mybir as mybir
+
+K, T, S, T2, S2, N = 1536, 4096, 1024, 2048, 512, 512
+FLOPS = 2 * K * S * S2 + 2 * 2 * S * N * S2
+
+F32 = mybir.dt.float32
+BF16 = mybir.dt.bfloat16
+I32 = mybir.dt.int32
+U32 = mybir.dt.uint32
+U16 = mybir.dt.uint16
+U8 = mybir.dt.uint8
+FP8X4 = mybir.dt.float8_e4m3fn_x4
+FP4X4 = mybir.dt.float4_e2m1fn_x4
+ACT = mybir.ActivationFunctionType
+MULT = mybir.AluOpType.mult
+
+P = 128
+PACK = 4
+PASS = P * PACK
+KP = K // PASS
+IB = S // PASS
+JW = 128
+JB = S2 // JW
+NT = N // P
+C_BANKS = 6
+NW = 256
+
+
+def tile_list_desk_stress_results_kernel(tc, tab_words, tab_scales, tab2_words, tab2_scales, offs, offs2, size, wd, w4_words, w4_scales, out):
+    nc = tc.nc
+    with ExitStack() as ctx:
+        keep = ctx.enter_context(tc.tile_pool(name="keep", bufs=1))
+        ring = ctx.enter_context(tc.tile_pool(name="ring", bufs=3))
+        cps = ctx.enter_context(tc.psum_pool(name="cps", bufs=C_BANKS))
+        ops = ctx.enter_context(tc.psum_pool(name="ops", bufs=2))
+
+        idx = keep.tile([P, S // 16], U16, name="idx")
+        idx2 = keep.tile([P, S2 // 16], U16, name="idx2")
+        tabw = [keep.tile([P, T], I32, name="tabw%d" % a, align_bytes=64) for a in range(KP)]
+        tab2w = [keep.tile([P, T2], I32, name="tab2w%d" % a, align_bytes=64) for a in range(KP)]
+        tabs = keep.tile([P, T], U8, name="tabs", align_bytes=64)
+        tab2s = keep.tile([P, T2], U8, name="tab2s", align_bytes=64)
+        w4s = keep.tile([P, IB, N], U8, name="w4s", align_bytes=64)
+        w4w = keep.tile([P, IB, 2 * N], U8, name="w4w", align_bytes=64)
+        sz = keep.tile([P, IB, PACK], F32, name="sz")
+        chunks = [(b, u) for b in range(IB) for u in range(N // NW)]
+        wdraw = {c: keep.tile([P, PACK, NW], F32, name="wdraw%d_%d" % c, align_bytes=64) for c in chunks}
+        wdbf = {c: keep.tile([P, NW, PACK], BF16, name="wdbf%d_%d" % c, align_bytes=64) for c in chunks}
+        wdw = {c: keep.tile([P, NW], U32, name="wdw%d_%d" % c, align_bytes=64) for c in chunks}
+        wds = {c: keep.tile([P, NW], U8, name="wds%d_%d" % c, align_bytes=64) for c in chunks}
+        vw = [[keep.tile([P, PASS], U32, name="vw%d_%d" % (a, b), align_bytes=64) for b in range(IB)] for a in range(KP)]
+        v2w = [[keep.tile([P, 2 * JW], U32, name="v2w%d_%d" % (a, u), align_bytes=64) for u in range(2)] for a in range(KP)]
+        vs_list = keep.tile([P, S], U8, name="vs_list", align_bytes=64)
+        vs = keep.tile([P, S], U8, name="vs", align_bytes=64)
+        v2s = keep.tile([P, S2], U8, name="v2s", align_bytes=64)
+        warm = keep.tile([P, 8], F32, name="warm")
+        warm_out = keep.tile([P, 8], F32, name="warm_out")
+
+        nc.vector.memset(tabs[:].bitcast(I32), 0)
+        nc.vector.memset(tab2s[:].bitcast(I32), 0)
+        nc.vector.memset(w4s[:].rearrange("p b n -> p (b n)").bitcast(I32), 0)
+        nc.vector.memset(warm[:], 1.0)
+        nc.scalar.activation(warm_out[:], warm[:], ACT.Abs_reciprocal_sqrt)
+
+        def load_words(dst, words, a):
+            nc.sync.dma_start(dst[a][:], words[a].rearrange("p t i -> p (t i)").bitcast(I32))
+
+        load_words(tabw, tab_words, 0)
+        nc.sync.dma_start(idx[:], offs)
+        nc.sync.dma_start(idx2[:], offs2)
+        load_words(tab2w, tab2_words, 0)
+        load_words(tab2w, tab2_words, 1)
+        load_words(tabw, tab_words, 2)
+        load_words(tabw, tab_words, 1)
+        load_words(tab2w, tab2_words, 2)
+        nc.sync.dma_start(sz[:], size.rearrange("(b p t) -> p b t", b=IB, t=PACK))
+        for b, u in chunks:
+            nc.sync.dma_start(wdraw[b, u][:], wd[b * PASS : (b + 1) * PASS, u * NW : (u + 1) * NW].rearrange("(p t) n -> p t n", t=PACK))
+        nc.sync.dma_start(w4w[:].bitcast(I32), w4_words.rearrange("b p e -> p b e").bitcast(I32))
+
+        for q in range(4):
+            nc.gpsimd.dma_start(tabs[32 * q : 32 * q + 4 * KP, :].bitcast(I32), tab_scales[:, 4 * q : 4 * q + 4, :].bitcast(I32))
+        for q in range(4):
+            nc.gpsimd.dma_start(tab2s[32 * q : 32 * q + 4 * KP, :].bitcast(I32), tab2_scales[:, 4 * q : 4 * q + 4, :].bitcast(I32))
+        for q in range(4):
+            nc.gpsimd.dma_start(w4s[32 * q : 32 * q + 4, :, :].bitcast(I32), w4_scales[:, 4 * q : 4 * q + 4, :].rearrange("b r n -> r b n").bitcast(I32))
+
+        def gather_v(a, b):
+            cols = PASS // 16
+            nc.vector.tensor_copy(
+                vw[a][b][:].rearrange("p (t m) -> p m t", t=PACK),
+                tabw[a][:].bitcast(U32).indirect(idx[:, b * cols : (b + 1) * cols]),
+            )
+
+        def gather_v2(a, u):
+            cols = 2 * JW // 16
+            nc.vector.tensor_copy(v2w[a][u][:], tab2w[a][:].bitcast(U32).indirect(idx2[:, u * cols : (u + 1) * cols]))
+
+        gather_v(0, 0)
+        gather_v(0, 1)
+        for a in (0, 1):
+            gather_v2(a, 0)
+            gather_v2(a, 1)
+        nc.vector.tensor_copy(vs_list[:], tabs[:].indirect(idx[:]))
+        nc.vector.tensor_copy(v2s[:], tab2s[:].indirect(idx2[:]))
+        nc.vector.tensor_copy(
+            vs[:].rearrange("p (b t m) -> p b m t", b=IB, t=PACK),
+            vs_list[:].rearrange("p (b m t) -> p b m t", b=IB, t=PACK),
+        )
+        for a in (2, 1):
+            gather_v(a, 0)
+            gather_v(a, 1)
+
+        units = [(jb, b) for jb in range(JB) for b in range(IB)]
+        order = (1, 0, 2)
+
+        def c_pass(bank, unit, t, a):
+            jb, b = unit
+            jcols = slice((jb % 2) * JW, (jb % 2 + 1) * JW)
+            nc.tensor.matmul_mx(
+                out=bank[:, t, :],
+                lhsT=vw[a][b][:, t * P : (t + 1) * P].bitcast(FP8X4),
+                lhsT_scale=vs[4 * a :, b * PASS + t * P : b * PASS + (t + 1) * P],
+                rhs=v2w[a][jb // 2][:, jcols].bitcast(FP8X4),
+                rhs_scale=v2s[4 * a :, jb * JW : (jb + 1) * JW],
+                start=(a == order[0]),
+                stop=(a == order[-1]),
+            )
+
+        banks = {}
+        for k in range(C_BANKS):
+            banks[k] = cps.tile([P, PACK, JW], F32, name="cbank", tag="c")
+        for k in sorted(range(C_BANKS), key=lambda k: units[k][1]):
+            for a in order[:-1]:
+                c_pass(banks[k], units[k], 0, a)
+
+        gather_v2(2, 0)
+        gather_v2(2, 1)
+
+        def c_unit(k):
+            if k >= C_BANKS:
+                banks[k] = cps.tile([P, PACK, JW], F32, name="cbank", tag="c")
+            for t in range(PACK):
+                for a in order:
+                    if k < C_BANKS and t == 0 and a != order[-1]:
+                        continue
+                    c_pass(banks[k], units[k], t, a)
+
+        r_t, y_t, w_t, d_t, hg_t, hgw, hgs = {}, {}, {}, {}, {}, {}, {}
+
+        def s_abs(k):
+            r_t[k] = ring.tile([P, PACK, JW], F32, name="r", tag="r", bufs=4)
+            nc.scalar.activation(r_t[k][:], banks[k][:], ACT.Abs)
+
+        def s_rsqrt(k):
+            y_t[k] = ring.tile([P, PACK, JW], F32, name="y", tag="y")
+            nc.scalar.activation(y_t[k][:], r_t[k][:], ACT.Abs_reciprocal_sqrt, bias=1.0)
+
+        def s_square(k):
+            w_t[k] = ring.tile([P, PACK, JW], F32, name="w", tag="w")
+            nc.scalar.activation(w_t[k][:], y_t[k][:], ACT.Square)
+
+        def v_damp(k):
+            b = units[k][1]
+            d_t[k] = ring.tile([P, PACK, JW], F32, name="d", tag="d")
+            for t in range(PACK):
+                nc.vector.tensor_scalar_mul(d_t[k][:, t, :], w_t[k][:, t, :], sz[:, b, t : t + 1])
+
+        def v_hg(k):
+            hg_t[k] = ring.tile([P, 2, JW * PACK], BF16, name="hg", tag="hg", align_bytes=64)
+            d4 = d_t[k][:].rearrange("p t (c i) -> p c t i", i=4)
+            for which, src in enumerate((banks[k], r_t[k])):
+                nc.vector.tensor_tensor(
+                    hg_t[k][:, which, :].rearrange("p (c i t) -> p c t i", i=4, t=PACK),
+                    src[:].rearrange("p t (c i) -> p c t i", i=4),
+                    d4,
+                    MULT,
+                )
+
+        def v_quant(k):
+            hgw[k] = ring.tile([P, 2 * JW], U32, name="hgw", tag="hgw", bufs=4, align_bytes=64)
+            hgs[k] = ring.tile([P, 2 * JW], U8, name="hgs", tag="hgs", bufs=4, align_bytes=64)
+            nc.vector.quantize_mx(out=hgw[k][:].bitcast(FP8X4), scales=hgs[k][:], in_=hg_t[k][:].rearrange("p w c -> p (w c)"))
+
+        def wd_cast(c):
+            nc.vector.tensor_copy(
+                wdbf[c][:].rearrange("p (c i) t -> p c t i", i=4),
+                wdraw[c][:].rearrange("p t (c i) -> p c t i", i=4),
+            )
+
+        def wd_quant(c):
+            nc.vector.quantize_mx(out=wdw[c][:].bitcast(FP8X4), scales=wds[c][:], in_=wdbf[c][:].rearrange("p n t -> p (n t)"))
+
+        def out_passes(dst, q, k):
+            b = units[k][1]
+            ncols = slice(q * P, (q + 1) * P)
+            c = (b, q * P // NW)
+            wcols = slice(q * P % NW, q * P % NW + P)
+            nc.tensor.matmul_mx(
+                out=dst, lhsT=wdw[c][:, wcols].bitcast(FP8X4), lhsT_scale=wds[c][:, wcols],
+                rhs=hgw[k][:, 0:JW].bitcast(FP8X4), rhs_scale=hgs[k][:, 0:JW], start=(b == 0), stop=False,
+            )
+            nc.tensor.matmul_mx(
+                out=dst, lhsT=w4w[:, b, 2 * q * P : 2 * (q + 1) * P].bitcast(FP4X4), lhsT_scale=w4s[:, b, ncols],
+                rhs=hgw[k][:, JW : 2 * JW].bitcast(FP8X4), rhs_scale=hgs[k][:, JW : 2 * JW], start=False, stop=(b == IB - 1),
+            )
+
+        out_v = out.rearrange("(q p) j -> p q j", p=P)
+
+        def out_block(jb):
+            acc = ops.tile([P, NT, JW], F32, name="acc", tag="acc")
+            for q in range(NT):
+                for b in range(IB):
+                    out_passes(acc[:, q, :], q, jb * IB + b)
+            res = ring.tile([P, NT, JW], F32, name="res", tag="res")
+            nc.scalar.copy(res[:], acc[:])
+            nc.sync.dma_start(out_v[:, :, jb * JW : (jb + 1) * JW], res[:])
+
+        def last_block():
+            jb = JB - 1
+            accs = [cps.tile([P, PACK, JW], F32, name="cbank", tag="c") for q in range(NT)]
+            for b in range(IB):
+                for q in range(NT):
+                    out_passes(accs[q][:, 0, :], q, jb * IB + b)
+            for half in range(2):
+                res = ring.tile([P, 2, JW], F32, name="tail", tag="tail")
+                nc.vector.tensor_copy(res[:, 0, :], accs[2 * half][:, 0, :])
+                nc.scalar.copy(res[:, 1, :], accs[2 * half + 1][:, 0, :])
+                nc.sync.dma_start(out_v[:, 2 * half : 2 * half + 2, jb * JW : (jb + 1) * JW], res[:])
+
+        n_units = len(units)
+        wd_cast(chunks[0])
+        for n in range(1, len(chunks)):
+            wd_cast(chunks[n])
+            wd_quant(chunks[n - 1])
+        c_unit(0)
+        s_abs(0)
+        for k in range(n_units + 1):
+            if k + 1 < n_units:
+                c_unit(k + 1)
+            if k < n_units:
+                s_rsqrt(k)
+                if k + 1 < n_units:
+                    s_abs(k + 1)
+                s_square(k)
+                v_damp(k)
+            if k == 0:
+                wd_quant(chunks[-1])
+            else:
+                v_quant(k - 1)
+            if k < n_units:
+                v_hg(k)
+            if k > 0 and k % IB == 0:
+                if k == n_units:
+                    last_block()
+                else:
+                    out_block(k // IB - 1)

@@ -46,7 +46,7 @@ def tile_list_desk_stress_results_kernel(tc, tab_words, tab_scales, tab2_words, 
         w4w = keep.tile([P, IB, 2 * N], U8, name="w4w", align_bytes=64)
         sz = keep.tile([P, IB, PACK], F32, name="sz")
         chunks = [(b, u) for b in range(IB) for u in range(N // NW)]
-        wdraw = {c: keep.tile([P, PACK, NW], F32, name="wdraw%d_%d" % c, align_bytes=64) for c in chunks}
+        wdraw = [keep.tile([P, PACK, N], F32, name="wdraw%d" % b, align_bytes=64) for b in range(IB)]
         wdbf = {c: keep.tile([P, NW, PACK], BF16, name="wdbf%d_%d" % c, align_bytes=64) for c in chunks}
         wdw = {c: keep.tile([P, NW], U32, name="wdw%d_%d" % c, align_bytes=64) for c in chunks}
         wds = {c: keep.tile([P, NW], U8, name="wds%d_%d" % c, align_bytes=64) for c in chunks}
@@ -59,33 +59,35 @@ def tile_list_desk_stress_results_kernel(tc, tab_words, tab_scales, tab2_words, 
         warm_out = keep.tile([P, 8], F32, name="warm_out")
 
         nc.vector.memset(tabs[:].bitcast(I32), 0)
-        nc.vector.memset(tab2s[:].bitcast(I32), 0)
+        nc.gpsimd.memset(tab2s[:].bitcast(I32), 0)
         nc.vector.memset(w4s[:].rearrange("p b n -> p (b n)").bitcast(I32), 0)
         nc.vector.memset(warm[:], 1.0)
         nc.scalar.activation(warm_out[:], warm[:], ACT.Abs_reciprocal_sqrt)
 
-        def load_words(dst, words, a):
-            nc.sync.dma_start(dst[a][:], words[a].rearrange("p t i -> p (t i)").bitcast(I32))
+        def load_words(dst, words, a, lo=0, hi=None):
+            nc.sync.dma_start(dst[a][:, lo:hi], words[a, :, lo:hi, :].rearrange("p t i -> p (t i)").bitcast(I32))
 
-        load_words(tabw, tab_words, 0)
-        nc.sync.dma_start(idx[:], offs)
+        load_words(tab2w, tab2_words, 0, 0, T2 // 2)
         nc.sync.dma_start(idx2[:], offs2)
-        load_words(tab2w, tab2_words, 0)
-        load_words(tab2w, tab2_words, 1)
-        load_words(tabw, tab_words, 2)
-        load_words(tabw, tab_words, 1)
-        load_words(tab2w, tab2_words, 2)
+        nc.sync.dma_start(idx[:], offs)
         nc.sync.dma_start(sz[:], size.rearrange("(b p t) -> p b t", b=IB, t=PACK))
-        for b, u in chunks:
-            nc.sync.dma_start(wdraw[b, u][:], wd[b * PASS : (b + 1) * PASS, u * NW : (u + 1) * NW].rearrange("(p t) n -> p t n", t=PACK))
+        load_words(tab2w, tab2_words, 0, T2 // 2, T2)
+        load_words(tabw, tab_words, 0, 0, 1024)
+        load_words(tabw, tab_words, 0, 1024, 2560)
+        load_words(tabw, tab_words, 0, 2560, T)
+        for q in range(4):
+            nc.sync.dma_start(tabs[32 * q : 32 * q + 4 * KP, :].bitcast(I32), tab_scales[:, 4 * q : 4 * q + 4, :].bitcast(I32))
+        for q in range(4):
+            nc.sync.dma_start(tab2s[32 * q : 32 * q + 4 * KP, :].bitcast(I32), tab2_scales[:, 4 * q : 4 * q + 4, :].bitcast(I32))
+        load_words(tabw, tab_words, 1)
+        load_words(tabw, tab_words, 2)
+        load_words(tab2w, tab2_words, 1)
+        load_words(tab2w, tab2_words, 2)
+        for b, lo, hi in ((0, 0, NW), (0, NW, N), (1, 0, N)):
+            nc.sync.dma_start(wdraw[b][:, :, lo:hi], wd[b * PASS : (b + 1) * PASS, lo:hi].rearrange("(p t) n -> p t n", t=PACK))
         nc.sync.dma_start(w4w[:].bitcast(I32), w4_words.rearrange("b p e -> p b e").bitcast(I32))
-
         for q in range(4):
-            nc.gpsimd.dma_start(tabs[32 * q : 32 * q + 4 * KP, :].bitcast(I32), tab_scales[:, 4 * q : 4 * q + 4, :].bitcast(I32))
-        for q in range(4):
-            nc.gpsimd.dma_start(tab2s[32 * q : 32 * q + 4 * KP, :].bitcast(I32), tab2_scales[:, 4 * q : 4 * q + 4, :].bitcast(I32))
-        for q in range(4):
-            nc.gpsimd.dma_start(w4s[32 * q : 32 * q + 4, :, :].bitcast(I32), w4_scales[:, 4 * q : 4 * q + 4, :].rearrange("b r n -> r b n").bitcast(I32))
+            nc.sync.dma_start(w4s[32 * q : 32 * q + 4, :, :].bitcast(I32), w4_scales[:, 4 * q : 4 * q + 4, :].rearrange("b r n -> r b n").bitcast(I32))
 
         def gather_v(a, b):
             cols = PASS // 16
@@ -98,20 +100,21 @@ def tile_list_desk_stress_results_kernel(tc, tab_words, tab_scales, tab2_words, 
             cols = 2 * JW // 16
             nc.vector.tensor_copy(v2w[a][u][:], tab2w[a][:].bitcast(U32).indirect(idx2[:, u * cols : (u + 1) * cols]))
 
+        gather_v2(0, 0)
+        gather_v2(0, 1)
         gather_v(0, 0)
         gather_v(0, 1)
-        for a in (0, 1):
-            gather_v2(a, 0)
-            gather_v2(a, 1)
         nc.vector.tensor_copy(vs_list[:], tabs[:].indirect(idx[:]))
         nc.vector.tensor_copy(v2s[:], tab2s[:].indirect(idx2[:]))
         nc.vector.tensor_copy(
             vs[:].rearrange("p (b t m) -> p b m t", b=IB, t=PACK),
             vs_list[:].rearrange("p (b m t) -> p b m t", b=IB, t=PACK),
         )
-        for a in (2, 1):
+        for a in (1, 2):
             gather_v(a, 0)
             gather_v(a, 1)
+        gather_v2(1, 0)
+        gather_v2(1, 1)
 
         units = [(jb, b) for jb in range(JB) for b in range(IB)]
         order = (1, 0, 2)
@@ -132,7 +135,7 @@ def tile_list_desk_stress_results_kernel(tc, tab_words, tab_scales, tab2_words, 
         banks = {}
         for k in range(C_BANKS):
             banks[k] = cps.tile([P, PACK, JW], F32, name="cbank", tag="c")
-        for k in sorted(range(C_BANKS), key=lambda k: units[k][1]):
+        for k in range(C_BANKS):
             for a in order[:-1]:
                 c_pass(banks[k], units[k], 0, a)
 
@@ -180,30 +183,37 @@ def tile_list_desk_stress_results_kernel(tc, tab_words, tab_scales, tab2_words, 
                 )
 
         def v_quant(k):
-            hgw[k] = ring.tile([P, 2 * JW], U32, name="hgw", tag="hgw", bufs=4, align_bytes=64)
-            hgs[k] = ring.tile([P, 2 * JW], U8, name="hgs", tag="hgs", bufs=4, align_bytes=64)
-            nc.vector.quantize_mx(out=hgw[k][:].bitcast(FP8X4), scales=hgs[k][:], in_=hg_t[k][:].rearrange("p w c -> p (w c)"))
+            hgw[k] = ring.tile([P, 2 * JW], U32, name="hgw", tag="hgw", bufs=6, align_bytes=64)
+            hgs[k] = ring.tile([P, 2 * JW], U8, name="hgs", tag="hgs", bufs=6, align_bytes=64)
+            if k < len(units) - 1:
+                nc.vector.quantize_mx(out=hgw[k][:].bitcast(FP8X4), scales=hgs[k][:], in_=hg_t[k][:].rearrange("p w c -> p (w c)"))
+            else:
+                for which in range(2):
+                    cols = slice(which * JW, (which + 1) * JW)
+                    nc.vector.quantize_mx(out=hgw[k][:, cols].bitcast(FP8X4), scales=hgs[k][:, cols], in_=hg_t[k][:, which, :])
 
         def wd_cast(c):
             nc.vector.tensor_copy(
                 wdbf[c][:].rearrange("p (c i) t -> p c t i", i=4),
-                wdraw[c][:].rearrange("p t (c i) -> p c t i", i=4),
+                wdraw[c[0]][:, :, c[1] * NW : (c[1] + 1) * NW].rearrange("p t (c i) -> p c t i", i=4),
             )
 
         def wd_quant(c):
             nc.vector.quantize_mx(out=wdw[c][:].bitcast(FP8X4), scales=wds[c][:], in_=wdbf[c][:].rearrange("p n t -> p (n t)"))
 
-        def out_passes(dst, q, k):
+        def linear_pass(dst, q, k):
             b = units[k][1]
-            ncols = slice(q * P, (q + 1) * P)
             c = (b, q * P // NW)
             wcols = slice(q * P % NW, q * P % NW + P)
             nc.tensor.matmul_mx(
                 out=dst, lhsT=wdw[c][:, wcols].bitcast(FP8X4), lhsT_scale=wds[c][:, wcols],
                 rhs=hgw[k][:, 0:JW].bitcast(FP8X4), rhs_scale=hgs[k][:, 0:JW], start=(b == 0), stop=False,
             )
+
+        def option_pass(dst, q, k):
+            b = units[k][1]
             nc.tensor.matmul_mx(
-                out=dst, lhsT=w4w[:, b, 2 * q * P : 2 * (q + 1) * P].bitcast(FP4X4), lhsT_scale=w4s[:, b, ncols],
+                out=dst, lhsT=w4w[:, b, 2 * q * P : 2 * (q + 1) * P].bitcast(FP4X4), lhsT_scale=w4s[:, b, q * P : (q + 1) * P],
                 rhs=hgw[k][:, JW : 2 * JW].bitcast(FP8X4), rhs_scale=hgs[k][:, JW : 2 * JW], start=False, stop=(b == IB - 1),
             )
 
@@ -213,7 +223,8 @@ def tile_list_desk_stress_results_kernel(tc, tab_words, tab_scales, tab2_words, 
             acc = ops.tile([P, NT, JW], F32, name="acc", tag="acc")
             for q in range(NT):
                 for b in range(IB):
-                    out_passes(acc[:, q, :], q, jb * IB + b)
+                    linear_pass(acc[:, q, :], q, jb * IB + b)
+                    option_pass(acc[:, q, :], q, jb * IB + b)
             res = ring.tile([P, NT, JW], F32, name="res", tag="res")
             nc.scalar.copy(res[:], acc[:])
             nc.sync.dma_start(out_v[:, :, jb * JW : (jb + 1) * JW], res[:])
@@ -222,8 +233,9 @@ def tile_list_desk_stress_results_kernel(tc, tab_words, tab_scales, tab2_words, 
             jb = JB - 1
             accs = [cps.tile([P, PACK, JW], F32, name="cbank", tag="c") for q in range(NT)]
             for b in range(IB):
-                for q in range(NT):
-                    out_passes(accs[q][:, 0, :], q, jb * IB + b)
+                for one_pass in (linear_pass, option_pass):
+                    for q in range(NT):
+                        one_pass(accs[q][:, 0, :], q, jb * IB + b)
             for half in range(2):
                 res = ring.tile([P, 2, JW], F32, name="tail", tag="tail")
                 nc.vector.tensor_copy(res[:, 0, :], accs[2 * half][:, 0, :])
@@ -232,9 +244,8 @@ def tile_list_desk_stress_results_kernel(tc, tab_words, tab_scales, tab2_words, 
 
         n_units = len(units)
         wd_cast(chunks[0])
-        for n in range(1, len(chunks)):
-            wd_cast(chunks[n])
-            wd_quant(chunks[n - 1])
+        wd_cast(chunks[1])
+        wd_quant(chunks[0])
         c_unit(0)
         s_abs(0)
         for k in range(n_units + 1):
@@ -247,11 +258,17 @@ def tile_list_desk_stress_results_kernel(tc, tab_words, tab_scales, tab2_words, 
                 s_square(k)
                 v_damp(k)
             if k == 0:
-                wd_quant(chunks[-1])
+                wd_quant(chunks[1])
             else:
                 v_quant(k - 1)
             if k < n_units:
                 v_hg(k)
+            if k < 2:
+                wd_cast(chunks[2 + k])
+            if k == 1:
+                wd_quant(chunks[2])
+            if k == 2:
+                wd_quant(chunks[3])
             if k > 0 and k % IB == 0:
                 if k == n_units:
                     last_block()

@@ -24,7 +24,8 @@ IB = S // PASS
 JW = 128
 JB = S2 // JW
 NT = N // P
-C_BANKS = 6
+C_BANKS = 8
+AHEAD = 2
 NW = 256
 
 
@@ -34,7 +35,6 @@ def tile_list_desk_stress_results_kernel(tc, tab_words, tab_scales, tab2_words, 
         keep = ctx.enter_context(tc.tile_pool(name="keep", bufs=1))
         ring = ctx.enter_context(tc.tile_pool(name="ring", bufs=3))
         cps = ctx.enter_context(tc.psum_pool(name="cps", bufs=C_BANKS))
-        ops = ctx.enter_context(tc.psum_pool(name="ops", bufs=2))
 
         idx = keep.tile([P, S // 16], U16, name="idx")
         idx2 = keep.tile([P, S2 // 16], U16, name="idx2")
@@ -77,9 +77,9 @@ def tile_list_desk_stress_results_kernel(tc, tab_words, tab_scales, tab2_words, 
         load_words(tabw, tab_words, 0, 2560, T)
         for q in range(4):
             nc.sync.dma_start(tabs[32 * q : 32 * q + 4 * KP, :].bitcast(I32), tab_scales[:, 4 * q : 4 * q + 4, :].bitcast(I32))
+        load_words(tabw, tab_words, 1)
         for q in range(4):
             nc.sync.dma_start(tab2s[32 * q : 32 * q + 4 * KP, :].bitcast(I32), tab2_scales[:, 4 * q : 4 * q + 4, :].bitcast(I32))
-        load_words(tabw, tab_words, 1)
         load_words(tabw, tab_words, 2)
         load_words(tab2w, tab2_words, 1)
         load_words(tab2w, tab2_words, 2)
@@ -105,19 +105,19 @@ def tile_list_desk_stress_results_kernel(tc, tab_words, tab_scales, tab2_words, 
         gather_v(0, 0)
         gather_v(0, 1)
         nc.vector.tensor_copy(vs_list[:], tabs[:].indirect(idx[:]))
-        nc.vector.tensor_copy(v2s[:], tab2s[:].indirect(idx2[:]))
         nc.vector.tensor_copy(
             vs[:].rearrange("p (b t m) -> p b m t", b=IB, t=PACK),
             vs_list[:].rearrange("p (b m t) -> p b m t", b=IB, t=PACK),
         )
-        for a in (1, 2):
-            gather_v(a, 0)
-            gather_v(a, 1)
+        gather_v(1, 0)
+        gather_v(1, 1)
+        nc.vector.tensor_copy(v2s[:], tab2s[:].indirect(idx2[:]))
+        gather_v(2, 0)
+        gather_v(2, 1)
         gather_v2(1, 0)
         gather_v2(1, 1)
 
         units = [(jb, b) for jb in range(JB) for b in range(IB)]
-        order = (1, 0, 2)
 
         def c_pass(bank, unit, t, a):
             jb, b = unit
@@ -128,27 +128,26 @@ def tile_list_desk_stress_results_kernel(tc, tab_words, tab_scales, tab2_words, 
                 lhsT_scale=vs[4 * a :, b * PASS + t * P : b * PASS + (t + 1) * P],
                 rhs=v2w[a][jb // 2][:, jcols].bitcast(FP8X4),
                 rhs_scale=v2s[4 * a :, jb * JW : (jb + 1) * JW],
-                start=(a == order[0]),
-                stop=(a == order[-1]),
+                start=(a == 0 and t == 0),
+                stop=(a == KP - 1 and t == PACK - 1),
             )
 
         banks = {}
         for k in range(C_BANKS):
             banks[k] = cps.tile([P, PACK, JW], F32, name="cbank", tag="c")
         for k in range(C_BANKS):
-            for a in order[:-1]:
-                c_pass(banks[k], units[k], 0, a)
+            for t in range(PACK):
+                c_pass(banks[k], units[k], t, 0)
+        for k in range(AHEAD):
+            for t in range(PACK):
+                c_pass(banks[k], units[k], t, 1)
 
         gather_v2(2, 0)
         gather_v2(2, 1)
 
         def c_unit(k):
-            if k >= C_BANKS:
-                banks[k] = cps.tile([P, PACK, JW], F32, name="cbank", tag="c")
-            for t in range(PACK):
-                for a in order:
-                    if k < C_BANKS and t == 0 and a != order[-1]:
-                        continue
+            for a in range(2 if k < AHEAD else 1, KP):
+                for t in range(PACK):
                     c_pass(banks[k], units[k], t, a)
 
         r_t, y_t, w_t, d_t, hg_t, hgw, hgs = {}, {}, {}, {}, {}, {}, {}
@@ -201,46 +200,47 @@ def tile_list_desk_stress_results_kernel(tc, tab_words, tab_scales, tab2_words, 
         def wd_quant(c):
             nc.vector.quantize_mx(out=wdw[c][:].bitcast(FP8X4), scales=wds[c][:], in_=wdbf[c][:].rearrange("p n t -> p (n t)"))
 
-        def linear_pass(dst, q, k):
+        def linear_pass(dst, q, k, first):
             b = units[k][1]
             c = (b, q * P // NW)
             wcols = slice(q * P % NW, q * P % NW + P)
             nc.tensor.matmul_mx(
                 out=dst, lhsT=wdw[c][:, wcols].bitcast(FP8X4), lhsT_scale=wds[c][:, wcols],
-                rhs=hgw[k][:, 0:JW].bitcast(FP8X4), rhs_scale=hgs[k][:, 0:JW], start=(b == 0), stop=False,
+                rhs=hgw[k][:, 0:JW].bitcast(FP8X4), rhs_scale=hgs[k][:, 0:JW], start=first, stop=False,
             )
 
-        def option_pass(dst, q, k):
+        def option_pass(dst, q, k, last):
             b = units[k][1]
             nc.tensor.matmul_mx(
                 out=dst, lhsT=w4w[:, b, 2 * q * P : 2 * (q + 1) * P].bitcast(FP4X4), lhsT_scale=w4s[:, b, q * P : (q + 1) * P],
-                rhs=hgw[k][:, JW : 2 * JW].bitcast(FP8X4), rhs_scale=hgs[k][:, JW : 2 * JW], start=False, stop=(b == IB - 1),
+                rhs=hgw[k][:, JW : 2 * JW].bitcast(FP8X4), rhs_scale=hgs[k][:, JW : 2 * JW], start=False, stop=last,
             )
 
         out_v = out.rearrange("(q p) j -> p q j", p=P)
 
         def out_block(jb):
-            acc = ops.tile([P, NT, JW], F32, name="acc", tag="acc")
-            for q in range(NT):
-                for b in range(IB):
-                    linear_pass(acc[:, q, :], q, jb * IB + b)
-                    option_pass(acc[:, q, :], q, jb * IB + b)
+            acc = cps.tile([P, NT, JW], F32, name="cbank", tag="c")
+            for b in range(IB):
+                for q in range(NT):
+                    linear_pass(acc[:, q, :], q, jb * IB + b, b == 0 and q == 0)
+                for q in range(NT):
+                    option_pass(acc[:, q, :], q, jb * IB + b, b == IB - 1 and q == NT - 1)
             res = ring.tile([P, NT, JW], F32, name="res", tag="res")
             nc.scalar.copy(res[:], acc[:])
             nc.sync.dma_start(out_v[:, :, jb * JW : (jb + 1) * JW], res[:])
 
         def last_block():
             jb = JB - 1
-            accs = [cps.tile([P, PACK, JW], F32, name="cbank", tag="c") for q in range(NT)]
+            accs = [cps.tile([P, PACK, JW], F32, name="cbank", tag="c") for half in range(2)]
             for b in range(IB):
-                for one_pass in (linear_pass, option_pass):
-                    for q in range(NT):
-                        one_pass(accs[q][:, 0, :], q, jb * IB + b)
-            for half in range(2):
-                res = ring.tile([P, 2, JW], F32, name="tail", tag="tail")
-                nc.vector.tensor_copy(res[:, 0, :], accs[2 * half][:, 0, :])
-                nc.scalar.copy(res[:, 1, :], accs[2 * half + 1][:, 0, :])
-                nc.sync.dma_start(out_v[:, 2 * half : 2 * half + 2, jb * JW : (jb + 1) * JW], res[:])
+                for q in range(NT):
+                    linear_pass(accs[q // 2][:, q % 2, :], q, jb * IB + b, b == 0 and q % 2 == 0)
+                for q in range(NT):
+                    option_pass(accs[q // 2][:, q % 2, :], q, jb * IB + b, b == IB - 1 and q % 2 == 1)
+            res = ring.tile([P, NT, JW], F32, name="res", tag="res")
+            nc.vector.tensor_copy(res[:, 0:2, :], accs[0][:, 0:2, :])
+            nc.scalar.copy(res[:, 2:4, :], accs[1][:, 0:2, :])
+            nc.sync.dma_start(out_v[:, :, jb * JW : (jb + 1) * JW], res[:])
 
         n_units = len(units)
         wd_cast(chunks[0])

@@ -77,9 +77,9 @@ def tile_list_desk_stress_results_kernel(tc, tab_words, tab_scales, tab2_words, 
         load_words(tabw, tab_words, 0, 2560, T)
         for q in range(4):
             nc.sync.dma_start(tabs[32 * q : 32 * q + 4 * KP, :].bitcast(I32), tab_scales[:, 4 * q : 4 * q + 4, :].bitcast(I32))
-        load_words(tabw, tab_words, 1)
         for q in range(4):
             nc.sync.dma_start(tab2s[32 * q : 32 * q + 4 * KP, :].bitcast(I32), tab2_scales[:, 4 * q : 4 * q + 4, :].bitcast(I32))
+        load_words(tabw, tab_words, 1)
         load_words(tabw, tab_words, 2)
         load_words(tab2w, tab2_words, 1)
         load_words(tab2w, tab2_words, 2)
@@ -109,9 +109,9 @@ def tile_list_desk_stress_results_kernel(tc, tab_words, tab_scales, tab2_words, 
             vs[:].rearrange("p (b t m) -> p b m t", b=IB, t=PACK),
             vs_list[:].rearrange("p (b m t) -> p b m t", b=IB, t=PACK),
         )
+        nc.vector.tensor_copy(v2s[:], tab2s[:].indirect(idx2[:]))
         gather_v(1, 0)
         gather_v(1, 1)
-        nc.vector.tensor_copy(v2s[:], tab2s[:].indirect(idx2[:]))
         gather_v(2, 0)
         gather_v(2, 1)
         gather_v2(1, 0)

@@ -38,96 +38,105 @@ def tile_list_desk_stress_results_kernel(tc, tab_words, tab_scales, tab2_words, 
 
         idx = keep.tile([P, S // 16], U16, name="idx")
         idx2 = keep.tile([P, S2 // 16], U16, name="idx2")
-        tabw = [keep.tile([P, T], I32, name="tabw%d" % a, align_bytes=64) for a in range(KP)]
-        tab2w = [keep.tile([P, T2], I32, name="tab2w%d" % a, align_bytes=64) for a in range(KP)]
         tabs = keep.tile([P, T], U8, name="tabs", align_bytes=64)
         tab2s = keep.tile([P, T2], U8, name="tab2s", align_bytes=64)
-        w4s = keep.tile([P, IB, N], U8, name="w4s", align_bytes=64)
-        w4w = keep.tile([P, IB, 2 * N], U8, name="w4w", align_bytes=64)
+        picked = keep.tile([P, S + S2], U8, name="picked", tag="picked", align_bytes=64)
+        staged = keep.tile([P, S + S2], U8, name="staged", tag="staged", align_bytes=64)
+        planes = keep.tile([P, S + S2], U8, name="planes", align_bytes=64)
         sz = keep.tile([P, IB, PACK], F32, name="sz")
         chunks = [(b, u) for b in range(IB) for u in range(N // NW)]
-        wdraw = [keep.tile([P, PACK, N], F32, name="wdraw%d" % b, align_bytes=64) for b in range(IB)]
         wdbf = {c: keep.tile([P, NW, PACK], BF16, name="wdbf%d_%d" % c, align_bytes=64) for c in chunks}
         wdw = {c: keep.tile([P, NW], U32, name="wdw%d_%d" % c, align_bytes=64) for c in chunks}
         wds = {c: keep.tile([P, NW], U8, name="wds%d_%d" % c, align_bytes=64) for c in chunks}
-        vw = [[keep.tile([P, PASS], U32, name="vw%d_%d" % (a, b), align_bytes=64) for b in range(IB)] for a in range(KP)]
-        v2w = [[keep.tile([P, 2 * JW], U32, name="v2w%d_%d" % (a, u), align_bytes=64) for u in range(2)] for a in range(KP)]
-        vs_list = keep.tile([P, S], U8, name="vs_list", align_bytes=64)
-        vs = keep.tile([P, S], U8, name="vs", align_bytes=64)
-        v2s = keep.tile([P, S2], U8, name="v2s", align_bytes=64)
+        tabw, tab2w, vw, v2w, wdraw = {}, {}, {}, {}, {}
         warm = keep.tile([P, 8], F32, name="warm")
         warm_out = keep.tile([P, 8], F32, name="warm_out")
 
+        nc.vector.memset(tab2s[:].bitcast(I32), 0)
         nc.vector.memset(tabs[:].bitcast(I32), 0)
-        nc.gpsimd.memset(tab2s[:].bitcast(I32), 0)
-        nc.vector.memset(w4s[:].rearrange("p b n -> p (b n)").bitcast(I32), 0)
+        nc.vector.memset(planes[:].bitcast(I32), 0)
         nc.vector.memset(warm[:], 1.0)
         nc.scalar.activation(warm_out[:], warm[:], ACT.Abs_reciprocal_sqrt)
 
-        def load_words(dst, words, a, lo=0, hi=None):
-            nc.sync.dma_start(dst[a][:, lo:hi], words[a, :, lo:hi, :].rearrange("p t i -> p (t i)").bitcast(I32))
+        def load_words(dst, words, a, tag, cuts):
+            dst[a] = keep.tile([P, cuts[-1]], I32, name="words_%d_%d" % (a, cuts[-1]), tag=tag, align_bytes=64)
+            for lo, hi in zip(cuts[:-1], cuts[1:]):
+                nc.sync.dma_start(dst[a][:, lo:hi], words[a, :, lo:hi, :].rearrange("p t i -> p (t i)").bitcast(I32))
 
-        load_words(tab2w, tab2_words, 0, 0, T2 // 2)
+        first_row = (0, 16, 64)
+
+        def load_scale_rows(dst, scales):
+            nc.sync.dma_start(dst[0:32, :].bitcast(I32), scales[0:2].rearrange("a r t -> (a r) t").bitcast(I32))
+            nc.sync.dma_start(dst[64:80, :].bitcast(I32), scales[2].bitcast(I32))
+
+        def place_rows(a, q):
+            src = first_row[a] + 4 * q
+            dst = 32 * q + 4 * a
+            nc.sync.dma_start(planes[dst : dst + 4, :].bitcast(I32), staged[src : src + 4, :].bitcast(I32))
+
+        def gather_v(a):
+            vw[a] = keep.tile([P, S], U32, name="vw%d" % a, align_bytes=64)
+            nc.vector.tensor_copy(
+                vw[a][:].rearrange("p (b t m) -> p b m t", b=IB, t=PACK),
+                tabw[a][:].bitcast(U32).indirect(idx[:]),
+            )
+
+        def gather_v2(a, parts):
+            v2w[a] = keep.tile([P, S2], U32, name="v2w%d" % a, align_bytes=64)
+            width = S2 // parts
+            for u in range(parts):
+                nc.vector.tensor_copy(
+                    v2w[a][:, u * width : (u + 1) * width],
+                    tab2w[a][:].bitcast(U32).indirect(idx2[:, u * width // 16 : (u + 1) * width // 16]),
+                )
+
         nc.sync.dma_start(idx2[:], offs2)
         nc.sync.dma_start(idx[:], offs)
         nc.sync.dma_start(sz[:], size.rearrange("(b p t) -> p b t", b=IB, t=PACK))
-        load_words(tab2w, tab2_words, 0, T2 // 2, T2)
-        load_words(tabw, tab_words, 0, 0, 1024)
-        load_words(tabw, tab_words, 0, 1024, 2560)
-        load_words(tabw, tab_words, 0, 2560, T)
-        for q in range(4):
-            nc.sync.dma_start(tabs[32 * q : 32 * q + 4 * KP, :].bitcast(I32), tab_scales[:, 4 * q : 4 * q + 4, :].bitcast(I32))
-        for q in range(4):
-            nc.sync.dma_start(tab2s[32 * q : 32 * q + 4 * KP, :].bitcast(I32), tab2_scales[:, 4 * q : 4 * q + 4, :].bitcast(I32))
-        load_words(tabw, tab_words, 1)
-        load_words(tabw, tab_words, 2)
-        load_words(tab2w, tab2_words, 1)
-        load_words(tab2w, tab2_words, 2)
-        for b, lo, hi in ((0, 0, NW), (0, NW, N), (1, 0, N)):
-            nc.sync.dma_start(wdraw[b][:, :, lo:hi], wd[b * PASS : (b + 1) * PASS, lo:hi].rearrange("(p t) n -> p t n", t=PACK))
-        nc.sync.dma_start(w4w[:].bitcast(I32), w4_words.rearrange("b p e -> p b e").bitcast(I32))
-        for q in range(4):
-            nc.sync.dma_start(w4s[32 * q : 32 * q + 4, :, :].bitcast(I32), w4_scales[:, 4 * q : 4 * q + 4, :].rearrange("b r n -> r b n").bitcast(I32))
+        load_words(tab2w, tab2_words, 0, "tab2w0", (0, 384, 768, 1152, 1536, T2))
+        load_scale_rows(tab2s, tab2_scales)
+        load_scale_rows(tabs, tab_scales)
+        load_words(tabw, tab_words, 0, "tabw0", (0, T))
+        load_words(tabw, tab_words, 1, "tabw1", (0, T))
 
-        def gather_v(a, b):
-            cols = PASS // 16
-            nc.vector.tensor_copy(
-                vw[a][b][:].rearrange("p (t m) -> p m t", t=PACK),
-                tabw[a][:].bitcast(U32).indirect(idx[:, b * cols : (b + 1) * cols]),
-            )
-
-        def gather_v2(a, u):
-            cols = 2 * JW // 16
-            nc.vector.tensor_copy(v2w[a][u][:], tab2w[a][:].bitcast(U32).indirect(idx2[:, u * cols : (u + 1) * cols]))
-
-        gather_v2(0, 0)
         gather_v2(0, 1)
-        gather_v(0, 0)
-        gather_v(0, 1)
-        nc.vector.tensor_copy(vs_list[:], tabs[:].indirect(idx[:]))
+        nc.vector.tensor_copy(picked[:, S:], tab2s[:].indirect(idx2[:]))
+        nc.vector.tensor_copy(picked[:, :S], tabs[:].indirect(idx[:]))
+        nc.vector.tensor_copy(staged[:, S:].bitcast(I32), picked[:, S:].bitcast(I32))
         nc.vector.tensor_copy(
-            vs[:].rearrange("p (b t m) -> p b m t", b=IB, t=PACK),
-            vs_list[:].rearrange("p (b m t) -> p b m t", b=IB, t=PACK),
+            staged[:, :S].rearrange("p (b t m) -> p b m t", b=IB, t=PACK),
+            picked[:, :S].rearrange("p (b m t) -> p b m t", b=IB, t=PACK),
         )
-        nc.vector.tensor_copy(v2s[:], tab2s[:].indirect(idx2[:]))
-        gather_v(1, 0)
-        gather_v(1, 1)
-        gather_v(2, 0)
-        gather_v(2, 1)
-        gather_v2(1, 0)
-        gather_v2(1, 1)
+        moves = [(a, q) for a in (1, 2, 0) for q in range(4)]
+        for a, q in moves[:6]:
+            place_rows(a, q)
+        load_words(tabw, tab_words, 2, "picked", (0, T))
+        for a, q in moves[6:]:
+            place_rows(a, q)
+        gather_v(0)
+        load_words(tab2w, tab2_words, 1, "tabw0", (0, T2))
+        gather_v(1)
+        load_words(tab2w, tab2_words, 2, "tabw1", (0, T2))
+        gather_v(2)
+        for b, tag, cuts in ((0, "staged", (0, NW, N)), (1, "picked", (0, N))):
+            wdraw[b] = keep.tile([P, PACK, N], F32, name="wdraw%d" % b, tag=tag, align_bytes=64)
+            for lo, hi in zip(cuts[:-1], cuts[1:]):
+                nc.sync.dma_start(wdraw[b][:, :, lo:hi], wd[b * PASS : (b + 1) * PASS, lo:hi].rearrange("(p t) n -> p t n", t=PACK))
+        gather_v2(1, 2)
+        w4w = keep.tile([P, IB, 2 * N], U8, name="w4w", tag="tabw0", align_bytes=64)
+        nc.sync.dma_start(w4w[:].bitcast(I32), w4_words.rearrange("b p e -> p b e").bitcast(I32))
 
         units = [(jb, b) for jb in range(JB) for b in range(IB)]
 
         def c_pass(bank, unit, t, a):
             jb, b = unit
-            jcols = slice((jb % 2) * JW, (jb % 2 + 1) * JW)
+            jcols = slice(jb * JW, (jb + 1) * JW)
             nc.tensor.matmul_mx(
                 out=bank[:, t, :],
-                lhsT=vw[a][b][:, t * P : (t + 1) * P].bitcast(FP8X4),
-                lhsT_scale=vs[4 * a :, b * PASS + t * P : b * PASS + (t + 1) * P],
-                rhs=v2w[a][jb // 2][:, jcols].bitcast(FP8X4),
-                rhs_scale=v2s[4 * a :, jb * JW : (jb + 1) * JW],
+                lhsT=vw[a][:, b * PASS + t * P : b * PASS + (t + 1) * P].bitcast(FP8X4),
+                lhsT_scale=planes[4 * a :, b * PASS + t * P : b * PASS + (t + 1) * P],
+                rhs=v2w[a][:, jcols].bitcast(FP8X4),
+                rhs_scale=planes[4 * a :, S + jb * JW : S + (jb + 1) * JW],
                 start=(a == 0 and t == 0),
                 stop=(a == KP - 1 and t == PACK - 1),
             )
@@ -142,8 +151,11 @@ def tile_list_desk_stress_results_kernel(tc, tab_words, tab_scales, tab2_words, 
             for t in range(PACK):
                 c_pass(banks[k], units[k], t, 1)
 
-        gather_v2(2, 0)
-        gather_v2(2, 1)
+        gather_v2(2, 2)
+        w4s = keep.tile([P, IB, N], U8, name="w4s", tag="tabw1", align_bytes=64)
+        nc.vector.memset(w4s[:].rearrange("p b n -> p (b n)").bitcast(I32), 0)
+        for q in range(4):
+            nc.sync.dma_start(w4s[32 * q : 32 * q + 4, :, :].bitcast(I32), w4_scales[:, 4 * q : 4 * q + 4, :].rearrange("b r n -> r b n").bitcast(I32))
 
         def c_unit(k):
             for a in range(2 if k < AHEAD else 1, KP):

@@ -24,9 +24,16 @@ IB = S // PASS
 JW = 128
 JB = S2 // JW
 NT = N // P
-C_BANKS = 8
-AHEAD = 2
+UNITS = JB * IB
 NW = 256
+QUADRANTS = 4
+LIST_ROWS = 16
+RUN = 4
+FIRST_ROW = (0, 16, 64)
+FIRST_CUTS = (0, 384, 768, 1152, 1536, T2)
+PLACED_FIRST = 6
+AHEAD = 2
+ON_SCALAR = 2
 
 
 def tile_list_desk_stress_results_kernel(tc, tab_words, tab_scales, tab2_words, tab2_scales, offs, offs2, size, wd, w4_words, w4_scales, out):
@@ -34,45 +41,43 @@ def tile_list_desk_stress_results_kernel(tc, tab_words, tab_scales, tab2_words, 
     with ExitStack() as ctx:
         keep = ctx.enter_context(tc.tile_pool(name="keep", bufs=1))
         ring = ctx.enter_context(tc.tile_pool(name="ring", bufs=3))
-        cps = ctx.enter_context(tc.psum_pool(name="cps", bufs=C_BANKS))
+        psum = ctx.enter_context(tc.psum_pool(name="psum", bufs=UNITS))
 
-        idx = keep.tile([P, S // 16], U16, name="idx")
-        idx2 = keep.tile([P, S2 // 16], U16, name="idx2")
+        idx = keep.tile([P, S // LIST_ROWS], U16, name="idx")
+        idx2 = keep.tile([P, S2 // LIST_ROWS], U16, name="idx2")
         tabs = keep.tile([P, T], U8, name="tabs", align_bytes=64)
         tab2s = keep.tile([P, T2], U8, name="tab2s", align_bytes=64)
         picked = keep.tile([P, S + S2], U8, name="picked", tag="picked", align_bytes=64)
         staged = keep.tile([P, S + S2], U8, name="staged", tag="staged", align_bytes=64)
-        planes = keep.tile([P, S + S2], U8, name="planes", align_bytes=64)
+        planes = [keep.tile([P, S + S2], U8, name="planes%d" % a, align_bytes=64) for a in range(KP)]
         sz = keep.tile([P, IB, PACK], F32, name="sz")
         chunks = [(b, u) for b in range(IB) for u in range(N // NW)]
         wdbf = {c: keep.tile([P, NW, PACK], BF16, name="wdbf%d_%d" % c, align_bytes=64) for c in chunks}
         wdw = {c: keep.tile([P, NW], U32, name="wdw%d_%d" % c, align_bytes=64) for c in chunks}
         wds = {c: keep.tile([P, NW], U8, name="wds%d_%d" % c, align_bytes=64) for c in chunks}
         tabw, tab2w, vw, v2w, wdraw = {}, {}, {}, {}, {}
-        warm = keep.tile([P, 8], F32, name="warm")
-        warm_out = keep.tile([P, 8], F32, name="warm_out")
+        one_in = keep.tile([P, 1], F32, name="one_in")
+        one = keep.tile([P, 1], F32, name="one")
 
         nc.vector.memset(tab2s[:].bitcast(I32), 0)
         nc.vector.memset(tabs[:].bitcast(I32), 0)
-        nc.vector.memset(planes[:].bitcast(I32), 0)
-        nc.vector.memset(warm[:], 1.0)
-        nc.scalar.activation(warm_out[:], warm[:], ACT.Abs_reciprocal_sqrt)
+        for a in range(KP):
+            nc.vector.memset(planes[a][:].bitcast(I32), 0)
+        nc.vector.memset(one_in[:], 1.0)
+        nc.scalar.activation(one[:], one_in[:], ACT.Abs_reciprocal_sqrt)
 
         def load_words(dst, words, a, tag, cuts):
             dst[a] = keep.tile([P, cuts[-1]], I32, name="words_%d_%d" % (a, cuts[-1]), tag=tag, align_bytes=64)
             for lo, hi in zip(cuts[:-1], cuts[1:]):
                 nc.sync.dma_start(dst[a][:, lo:hi], words[a, :, lo:hi, :].rearrange("p t i -> p (t i)").bitcast(I32))
 
-        first_row = (0, 16, 64)
-
         def load_scale_rows(dst, scales):
             nc.sync.dma_start(dst[0:32, :].bitcast(I32), scales[0:2].rearrange("a r t -> (a r) t").bitcast(I32))
             nc.sync.dma_start(dst[64:80, :].bitcast(I32), scales[2].bitcast(I32))
 
-        def place_rows(a, q):
-            src = first_row[a] + 4 * q
-            dst = 32 * q + 4 * a
-            nc.sync.dma_start(planes[dst : dst + 4, :].bitcast(I32), staged[src : src + 4, :].bitcast(I32))
+        def place_rows(a, quadrant):
+            src = FIRST_ROW[a] + 4 * quadrant
+            nc.sync.dma_start(planes[a][32 * quadrant : 32 * quadrant + 4, :].bitcast(I32), staged[src : src + 4, :].bitcast(I32))
 
         def gather_v(a):
             vw[a] = keep.tile([P, S], U32, name="vw%d" % a, align_bytes=64)
@@ -81,25 +86,22 @@ def tile_list_desk_stress_results_kernel(tc, tab_words, tab_scales, tab2_words, 
                 tabw[a][:].bitcast(U32).indirect(idx[:]),
             )
 
-        def gather_v2(a, parts):
-            v2w[a] = keep.tile([P, S2], U32, name="v2w%d" % a, align_bytes=64)
-            width = S2 // parts
-            for u in range(parts):
-                nc.vector.tensor_copy(
-                    v2w[a][:, u * width : (u + 1) * width],
-                    tab2w[a][:].bitcast(U32).indirect(idx2[:, u * width // 16 : (u + 1) * width // 16]),
-                )
+        def gather_v2(a, lo, hi, tag):
+            picks = keep.tile([P, hi - lo], U32, name="v2w%d_%d" % (a, lo), tag=tag, align_bytes=64)
+            nc.vector.tensor_copy(picks[:], tab2w[a][:].bitcast(U32).indirect(idx2[:, lo // LIST_ROWS : hi // LIST_ROWS]))
+            for jb in range(lo // JW, hi // JW):
+                v2w[a, jb] = picks[:, jb * JW - lo : (jb + 1) * JW - lo]
 
         nc.sync.dma_start(idx2[:], offs2)
         nc.sync.dma_start(idx[:], offs)
         nc.sync.dma_start(sz[:], size.rearrange("(b p t) -> p b t", b=IB, t=PACK))
-        load_words(tab2w, tab2_words, 0, "tab2w0", (0, 384, 768, 1152, 1536, T2))
+        load_words(tab2w, tab2_words, 0, "tab2w0", FIRST_CUTS)
         load_scale_rows(tab2s, tab2_scales)
         load_scale_rows(tabs, tab_scales)
         load_words(tabw, tab_words, 0, "tabw0", (0, T))
         load_words(tabw, tab_words, 1, "tabw1", (0, T))
 
-        gather_v2(0, 1)
+        gather_v2(0, 0, S2, "v2w0")
         nc.vector.tensor_copy(picked[:, S:], tab2s[:].indirect(idx2[:]))
         nc.vector.tensor_copy(picked[:, :S], tabs[:].indirect(idx[:]))
         nc.vector.tensor_copy(staged[:, S:].bitcast(I32), picked[:, S:].bitcast(I32))
@@ -107,60 +109,54 @@ def tile_list_desk_stress_results_kernel(tc, tab_words, tab_scales, tab2_words, 
             staged[:, :S].rearrange("p (b t m) -> p b m t", b=IB, t=PACK),
             picked[:, :S].rearrange("p (b m t) -> p b m t", b=IB, t=PACK),
         )
-        moves = [(a, q) for a in (1, 2, 0) for q in range(4)]
-        for a, q in moves[:6]:
-            place_rows(a, q)
+        moves = [(a, quadrant) for a in range(KP) for quadrant in range(QUADRANTS)]
+        for a, quadrant in moves[:PLACED_FIRST]:
+            place_rows(a, quadrant)
         load_words(tabw, tab_words, 2, "picked", (0, T))
-        for a, q in moves[6:]:
-            place_rows(a, q)
+        for a, quadrant in moves[PLACED_FIRST:]:
+            place_rows(a, quadrant)
         gather_v(0)
         load_words(tab2w, tab2_words, 1, "tabw0", (0, T2))
         gather_v(1)
         load_words(tab2w, tab2_words, 2, "tabw1", (0, T2))
         gather_v(2)
-        for b, tag, cuts in ((0, "staged", (0, NW, N)), (1, "picked", (0, N))):
+        for b, tag in enumerate(("staged", "picked")):
             wdraw[b] = keep.tile([P, PACK, N], F32, name="wdraw%d" % b, tag=tag, align_bytes=64)
-            for lo, hi in zip(cuts[:-1], cuts[1:]):
-                nc.sync.dma_start(wdraw[b][:, :, lo:hi], wd[b * PASS : (b + 1) * PASS, lo:hi].rearrange("(p t) n -> p t n", t=PACK))
-        gather_v2(1, 2)
-        w4w = keep.tile([P, IB, 2 * N], U8, name="w4w", tag="tabw0", align_bytes=64)
-        nc.sync.dma_start(w4w[:].bitcast(I32), w4_words.rearrange("b p e -> p b e").bitcast(I32))
+            for lo in range(0, N, NW):
+                nc.sync.dma_start(wdraw[b][:, :, lo : lo + NW], wd[b * PASS : (b + 1) * PASS, lo : lo + NW].rearrange("(p t) n -> p t n", t=PACK))
+        gather_v2(1, 0, S2 // 2, "v2w1")
 
         units = [(jb, b) for jb in range(JB) for b in range(IB)]
 
-        def c_pass(bank, unit, t, a):
-            jb, b = unit
-            jcols = slice(jb * JW, (jb + 1) * JW)
-            nc.tensor.matmul_mx(
-                out=bank[:, t, :],
-                lhsT=vw[a][:, b * PASS + t * P : b * PASS + (t + 1) * P].bitcast(FP8X4),
-                lhsT_scale=planes[4 * a :, b * PASS + t * P : b * PASS + (t + 1) * P],
-                rhs=v2w[a][:, jcols].bitcast(FP8X4),
-                rhs_scale=planes[4 * a :, S + jb * JW : S + (jb + 1) * JW],
-                start=(a == 0 and t == 0),
-                stop=(a == KP - 1 and t == PACK - 1),
-            )
-
-        banks = {}
-        for k in range(C_BANKS):
-            banks[k] = cps.tile([P, PACK, JW], F32, name="cbank", tag="c")
-        for k in range(C_BANKS):
+        def c_pass(k, a):
+            jb, b = units[k]
             for t in range(PACK):
-                c_pass(banks[k], units[k], t, 0)
+                icols = slice(b * PASS + t * P, b * PASS + (t + 1) * P)
+                nc.tensor.matmul_mx(
+                    out=banks[k][:, t, :],
+                    lhsT=vw[a][:, icols].bitcast(FP8X4),
+                    lhsT_scale=planes[a][:, icols],
+                    rhs=v2w[a, jb].bitcast(FP8X4),
+                    rhs_scale=planes[a][:, S + jb * JW : S + (jb + 1) * JW],
+                    start=(a == 0 and t == 0),
+                    stop=(a == KP - 1 and t == PACK - 1),
+                )
+
+        banks = [psum.tile([P, PACK, JW], F32, name="bank", tag="bank") for k in range(UNITS)]
+        for k in range(UNITS):
+            c_pass(k, 0)
         for k in range(AHEAD):
-            for t in range(PACK):
-                c_pass(banks[k], units[k], t, 1)
+            c_pass(k, 1)
 
-        gather_v2(2, 2)
-        w4s = keep.tile([P, IB, N], U8, name="w4s", tag="tabw1", align_bytes=64)
-        nc.vector.memset(w4s[:].rearrange("p b n -> p (b n)").bitcast(I32), 0)
-        for q in range(4):
-            nc.sync.dma_start(w4s[32 * q : 32 * q + 4, :, :].bitcast(I32), w4_scales[:, 4 * q : 4 * q + 4, :].rearrange("b r n -> r b n").bitcast(I32))
+        gather_v2(2, 0, S2 // 2, "v2w2")
+        gather_v2(2, S2 // 2, S2, "v2w2_late")
+        gather_v2(1, S2 // 2, S2, "tabw1")
+        w4w = keep.tile([P, IB, 2 * N], U8, name="w4w", tag="tabw0", align_bytes=64)
+        nc.sync.dma_start(w4w[:].bitcast(I32), w4_words.rearrange("b p e -> p b e").bitcast(I32))
 
-        def c_unit(k):
+        def c_finish(k):
             for a in range(2 if k < AHEAD else 1, KP):
-                for t in range(PACK):
-                    c_pass(banks[k], units[k], t, a)
+                c_pass(k, a)
 
         r_t, y_t, w_t, d_t, hg_t, hgw, hgs = {}, {}, {}, {}, {}, {}, {}
 
@@ -168,35 +164,40 @@ def tile_list_desk_stress_results_kernel(tc, tab_words, tab_scales, tab2_words, 
             r_t[k] = ring.tile([P, PACK, JW], F32, name="r", tag="r", bufs=4)
             nc.scalar.activation(r_t[k][:], banks[k][:], ACT.Abs)
 
-        def s_rsqrt(k):
+        def s_root(k):
             y_t[k] = ring.tile([P, PACK, JW], F32, name="y", tag="y")
-            nc.scalar.activation(y_t[k][:], r_t[k][:], ACT.Abs_reciprocal_sqrt, bias=1.0)
+            nc.scalar.activation(y_t[k][:], r_t[k][:], ACT.Abs_reciprocal_sqrt, bias=one[:])
 
         def s_square(k):
             w_t[k] = ring.tile([P, PACK, JW], F32, name="w", tag="w")
             nc.scalar.activation(w_t[k][:], y_t[k][:], ACT.Square)
 
-        def v_damp(k):
+        def size_product(k):
             b = units[k][1]
             d_t[k] = ring.tile([P, PACK, JW], F32, name="d", tag="d")
             for t in range(PACK):
-                nc.vector.tensor_scalar_mul(d_t[k][:, t, :], w_t[k][:, t, :], sz[:, b, t : t + 1])
+                if k < UNITS - ON_SCALAR:
+                    nc.vector.tensor_scalar_mul(d_t[k][:, t, :], w_t[k][:, t, :], sz[:, b, t : t + 1])
+                else:
+                    nc.scalar.activation(d_t[k][:, t, :], w_t[k][:, t, :], ACT.Copy, scale=sz[:, b, t : t + 1])
 
-        def v_hg(k):
+        def by_runs(src):
+            return src.rearrange("p t (c i) -> p c t i", i=RUN)
+
+        def v_products(k):
             hg_t[k] = ring.tile([P, 2, JW * PACK], BF16, name="hg", tag="hg", align_bytes=64)
-            d4 = d_t[k][:].rearrange("p t (c i) -> p c t i", i=4)
             for which, src in enumerate((banks[k], r_t[k])):
                 nc.vector.tensor_tensor(
-                    hg_t[k][:, which, :].rearrange("p (c i t) -> p c t i", i=4, t=PACK),
-                    src[:].rearrange("p t (c i) -> p c t i", i=4),
-                    d4,
+                    hg_t[k][:, which, :].rearrange("p (c i t) -> p c t i", i=RUN, t=PACK),
+                    by_runs(src[:]),
+                    by_runs(d_t[k][:]),
                     MULT,
                 )
 
         def v_quant(k):
             hgw[k] = ring.tile([P, 2 * JW], U32, name="hgw", tag="hgw", bufs=6, align_bytes=64)
             hgs[k] = ring.tile([P, 2 * JW], U8, name="hgs", tag="hgs", bufs=6, align_bytes=64)
-            if k < len(units) - 1:
+            if k < UNITS - 1:
                 nc.vector.quantize_mx(out=hgw[k][:].bitcast(FP8X4), scales=hgs[k][:], in_=hg_t[k][:].rearrange("p w c -> p (w c)"))
             else:
                 for which in range(2):
@@ -205,84 +206,85 @@ def tile_list_desk_stress_results_kernel(tc, tab_words, tab_scales, tab2_words, 
 
         def wd_cast(c):
             nc.vector.tensor_copy(
-                wdbf[c][:].rearrange("p (c i) t -> p c t i", i=4),
-                wdraw[c[0]][:, :, c[1] * NW : (c[1] + 1) * NW].rearrange("p t (c i) -> p c t i", i=4),
+                wdbf[c][:].rearrange("p (c i) t -> p c t i", i=RUN),
+                by_runs(wdraw[c[0]][:, :, c[1] * NW : (c[1] + 1) * NW]),
             )
 
         def wd_quant(c):
             nc.vector.quantize_mx(out=wdw[c][:].bitcast(FP8X4), scales=wds[c][:], in_=wdbf[c][:].rearrange("p n t -> p (n t)"))
 
-        def linear_pass(dst, q, k, first):
-            b = units[k][1]
-            c = (b, q * P // NW)
-            wcols = slice(q * P % NW, q * P % NW + P)
+        def linear_pass(dst, nt, k, first):
+            c = (units[k][1], nt * P // NW)
+            wcols = slice(nt * P % NW, nt * P % NW + P)
             nc.tensor.matmul_mx(
                 out=dst, lhsT=wdw[c][:, wcols].bitcast(FP8X4), lhsT_scale=wds[c][:, wcols],
                 rhs=hgw[k][:, 0:JW].bitcast(FP8X4), rhs_scale=hgs[k][:, 0:JW], start=first, stop=False,
             )
 
-        def option_pass(dst, q, k, last):
+        def option_pass(dst, nt, k, final):
             b = units[k][1]
             nc.tensor.matmul_mx(
-                out=dst, lhsT=w4w[:, b, 2 * q * P : 2 * (q + 1) * P].bitcast(FP4X4), lhsT_scale=w4s[:, b, q * P : (q + 1) * P],
-                rhs=hgw[k][:, JW : 2 * JW].bitcast(FP8X4), rhs_scale=hgs[k][:, JW : 2 * JW], start=False, stop=last,
+                out=dst, lhsT=w4w[:, b, 2 * nt * P : 2 * (nt + 1) * P].bitcast(FP4X4), lhsT_scale=w4s[:, b, nt * P : (nt + 1) * P],
+                rhs=hgw[k][:, JW : 2 * JW].bitcast(FP8X4), rhs_scale=hgs[k][:, JW : 2 * JW], start=False, stop=final,
             )
 
-        out_v = out.rearrange("(q p) j -> p q j", p=P)
+        out_v = out.rearrange("(nt p) j -> p nt j", p=P)
+
+        def out_sums(jb, per_bank):
+            accs = [psum.tile([P, NT, JW], F32, name="bank", tag="bank") for part in range(NT // per_bank)]
+            for b in range(IB):
+                for nt in range(NT):
+                    linear_pass(accs[nt // per_bank][:, nt % per_bank, :], nt, jb * IB + b, b == 0 and nt % per_bank == 0)
+                for nt in range(NT):
+                    option_pass(accs[nt // per_bank][:, nt % per_bank, :], nt, jb * IB + b, b == IB - 1 and nt % per_bank == per_bank - 1)
+            return accs
 
         def out_block(jb):
-            acc = cps.tile([P, NT, JW], F32, name="cbank", tag="c")
-            for b in range(IB):
-                for q in range(NT):
-                    linear_pass(acc[:, q, :], q, jb * IB + b, b == 0 and q == 0)
-                for q in range(NT):
-                    option_pass(acc[:, q, :], q, jb * IB + b, b == IB - 1 and q == NT - 1)
+            accs = out_sums(jb, NT)
             res = ring.tile([P, NT, JW], F32, name="res", tag="res")
-            nc.scalar.copy(res[:], acc[:])
+            nc.scalar.copy(res[:], accs[0][:])
             nc.sync.dma_start(out_v[:, :, jb * JW : (jb + 1) * JW], res[:])
 
         def last_block():
-            jb = JB - 1
-            accs = [cps.tile([P, PACK, JW], F32, name="cbank", tag="c") for half in range(2)]
-            for b in range(IB):
-                for q in range(NT):
-                    linear_pass(accs[q // 2][:, q % 2, :], q, jb * IB + b, b == 0 and q % 2 == 0)
-                for q in range(NT):
-                    option_pass(accs[q // 2][:, q % 2, :], q, jb * IB + b, b == IB - 1 and q % 2 == 1)
-            res = ring.tile([P, NT, JW], F32, name="res", tag="res")
-            nc.vector.tensor_copy(res[:, 0:2, :], accs[0][:, 0:2, :])
-            nc.scalar.copy(res[:, 2:4, :], accs[1][:, 0:2, :])
-            nc.sync.dma_start(out_v[:, :, jb * JW : (jb + 1) * JW], res[:])
+            half_nt = NT // 2
+            accs = out_sums(JB - 1, half_nt)
+            for half, copy, queue in ((0, nc.vector.tensor_copy, nc.sync), (1, nc.scalar.copy, nc.scalar)):
+                res = keep.tile([P, half_nt, JW], F32, name="res_last%d" % half)
+                copy(res[:], accs[half][:, 0:half_nt, :])
+                queue.dma_start(out_v[:, half * half_nt : (half + 1) * half_nt, (JB - 1) * JW : JB * JW], res[:])
 
-        n_units = len(units)
         wd_cast(chunks[0])
         wd_cast(chunks[1])
+        w4s = keep.tile([P, IB, N], U8, name="w4s", tag="staged", align_bytes=64)
+        nc.vector.memset(w4s[:].rearrange("p b n -> p (b n)").bitcast(I32), 0)
+        for quadrant in range(QUADRANTS):
+            nc.sync.dma_start(
+                w4s[32 * quadrant : 32 * quadrant + 4, :, :].bitcast(I32),
+                w4_scales[:, 4 * quadrant : 4 * quadrant + 4, :].rearrange("b r n -> r b n").bitcast(I32),
+            )
         wd_quant(chunks[0])
-        c_unit(0)
+        c_finish(0)
         s_abs(0)
-        for k in range(n_units + 1):
-            if k + 1 < n_units:
-                c_unit(k + 1)
-            if k < n_units:
-                s_rsqrt(k)
-                if k + 1 < n_units:
+        for k in range(UNITS + 1):
+            if k + 1 < UNITS:
+                c_finish(k + 1)
+            if k < UNITS:
+                s_root(k)
+                if k + 1 < UNITS:
                     s_abs(k + 1)
                 s_square(k)
-                v_damp(k)
+                size_product(k)
             if k == 0:
                 wd_quant(chunks[1])
             else:
                 v_quant(k - 1)
-            if k < n_units:
-                v_hg(k)
-            if k < 2:
+            if k < UNITS:
+                v_products(k)
+            if 2 + k < len(chunks):
                 wd_cast(chunks[2 + k])
-            if k == 1:
-                wd_quant(chunks[2])
-            if k == 2:
-                wd_quant(chunks[3])
-            if k > 0 and k % IB == 0:
-                if k == n_units:
-                    last_block()
-                else:
-                    out_block(k // IB - 1)
+            if 2 <= 1 + k < len(chunks):
+                wd_quant(chunks[1 + k])
+            if k == UNITS:
+                last_block()
+            elif k > 0 and k % IB == 0:
+                out_block(k // IB - 1)

@@ -29,10 +29,9 @@ NW = 256
 QUADRANTS = 4
 LIST_ROWS = 16
 RUN = 4
-FIRST_ROW = (0, 16, 64)
+FIRST_ROW = (0, 64, 33)
+ROW_STEP = 4
 FIRST_CUTS = (0, 384, 768, 1152, 1536, T2)
-PLACED_FIRST = 6
-AHEAD = 2
 ON_SCALAR = 2
 
 
@@ -72,12 +71,15 @@ def tile_list_desk_stress_results_kernel(tc, tab_words, tab_scales, tab2_words, 
                 nc.sync.dma_start(dst[a][:, lo:hi], words[a, :, lo:hi, :].rearrange("p t i -> p (t i)").bitcast(I32))
 
         def load_scale_rows(dst, scales):
-            nc.sync.dma_start(dst[0:32, :].bitcast(I32), scales[0:2].rearrange("a r t -> (a r) t").bitcast(I32))
-            nc.sync.dma_start(dst[64:80, :].bitcast(I32), scales[2].bitcast(I32))
+            nc.sync.dma_start(dst[0:P:ROW_STEP, :].bitcast(I32), scales[0:2].rearrange("a r t -> (a r) t").bitcast(I32))
+            nc.sync.dma_start(dst[FIRST_ROW[2] : FIRST_ROW[2] + 16 * ROW_STEP : ROW_STEP, :].bitcast(I32), scales[2].bitcast(I32))
 
         def place_rows(a, quadrant):
-            src = FIRST_ROW[a] + 4 * quadrant
-            nc.sync.dma_start(planes[a][32 * quadrant : 32 * quadrant + 4, :].bitcast(I32), staged[src : src + 4, :].bitcast(I32))
+            src = FIRST_ROW[a] + 4 * quadrant * ROW_STEP
+            nc.scalar.dma_start(
+                planes[a][32 * quadrant : 32 * quadrant + 4, :].bitcast(I32),
+                staged[src : src + 3 * ROW_STEP + 1 : ROW_STEP, :].bitcast(I32),
+            )
 
         def gather_v(a):
             vw[a] = keep.tile([P, S], U32, name="vw%d" % a, align_bytes=64)
@@ -99,6 +101,7 @@ def tile_list_desk_stress_results_kernel(tc, tab_words, tab_scales, tab2_words, 
         load_scale_rows(tab2s, tab2_scales)
         load_scale_rows(tabs, tab_scales)
         load_words(tabw, tab_words, 0, "tabw0", (0, T))
+        load_words(tab2w, tab2_words, 1, "tab2w1", (0, T2))
         load_words(tabw, tab_words, 1, "tabw1", (0, T))
 
         gather_v2(0, 0, S2, "v2w0")
@@ -110,21 +113,18 @@ def tile_list_desk_stress_results_kernel(tc, tab_words, tab_scales, tab2_words, 
             picked[:, :S].rearrange("p (b m t) -> p b m t", b=IB, t=PACK),
         )
         moves = [(a, quadrant) for a in range(KP) for quadrant in range(QUADRANTS)]
-        for a, quadrant in moves[:PLACED_FIRST]:
-            place_rows(a, quadrant)
-        load_words(tabw, tab_words, 2, "picked", (0, T))
-        for a, quadrant in moves[PLACED_FIRST:]:
+        for a, quadrant in moves:
             place_rows(a, quadrant)
         gather_v(0)
-        load_words(tab2w, tab2_words, 1, "tabw0", (0, T2))
+        load_words(tabw, tab_words, 2, "tabw0", (0, T))
+        gather_v2(1, 0, S2, "v2w1")
+        load_words(tab2w, tab2_words, 2, "tab2w1", (0, T2))
         gather_v(1)
-        load_words(tab2w, tab2_words, 2, "tabw1", (0, T2))
         gather_v(2)
-        for b, tag in enumerate(("staged", "picked")):
+        for b, tag in enumerate(("tabw1", "tabw0")):
             wdraw[b] = keep.tile([P, PACK, N], F32, name="wdraw%d" % b, tag=tag, align_bytes=64)
             for lo in range(0, N, NW):
                 nc.sync.dma_start(wdraw[b][:, :, lo : lo + NW], wd[b * PASS : (b + 1) * PASS, lo : lo + NW].rearrange("(p t) n -> p t n", t=PACK))
-        gather_v2(1, 0, S2 // 2, "v2w1")
 
         units = [(jb, b) for jb in range(JB) for b in range(IB)]
 
@@ -145,18 +145,16 @@ def tile_list_desk_stress_results_kernel(tc, tab_words, tab_scales, tab2_words, 
         banks = [psum.tile([P, PACK, JW], F32, name="bank", tag="bank") for k in range(UNITS)]
         for k in range(UNITS):
             c_pass(k, 0)
-        for k in range(AHEAD):
+        for k in range(UNITS):
             c_pass(k, 1)
 
         gather_v2(2, 0, S2 // 2, "v2w2")
         gather_v2(2, S2 // 2, S2, "v2w2_late")
-        gather_v2(1, S2 // 2, S2, "tabw1")
-        w4w = keep.tile([P, IB, 2 * N], U8, name="w4w", tag="tabw0", align_bytes=64)
+        w4w = keep.tile([P, IB, 2 * N], U8, name="w4w", tag="tab2w1", align_bytes=64)
         nc.sync.dma_start(w4w[:].bitcast(I32), w4_words.rearrange("b p e -> p b e").bitcast(I32))
 
         def c_finish(k):
-            for a in range(2 if k < AHEAD else 1, KP):
-                c_pass(k, a)
+            c_pass(k, KP - 1)
 
         r_t, y_t, w_t, d_t, hg_t, hgw, hgs = {}, {}, {}, {}, {}, {}, {}
 
@@ -255,7 +253,7 @@ def tile_list_desk_stress_results_kernel(tc, tab_words, tab_scales, tab2_words, 
 
         wd_cast(chunks[0])
         wd_cast(chunks[1])
-        w4s = keep.tile([P, IB, N], U8, name="w4s", tag="staged", align_bytes=64)
+        w4s = keep.tile([P, IB, N], U8, name="w4s", tag="v2w0", align_bytes=64)
         nc.vector.memset(w4s[:].rearrange("p b n -> p (b n)").bitcast(I32), 0)
         for quadrant in range(QUADRANTS):
             nc.sync.dma_start(

@@ -31,8 +31,8 @@ LIST_ROWS = 16
 RUN = 4
 FIRST_ROW = (0, 64, 33)
 ROW_STEP = 4
-FIRST_CUTS = (0, 384, 768, 1152, 1536, T2)
-ON_SCALAR = 2
+PLACED_FIRST = 6
+ON_SCALAR = (1, 3, 5, 7)
 
 
 def tile_list_desk_stress_results_kernel(tc, tab_words, tab_scales, tab2_words, tab2_scales, offs, offs2, size, wd, w4_words, w4_scales, out):
@@ -55,14 +55,14 @@ def tile_list_desk_stress_results_kernel(tc, tab_words, tab_scales, tab2_words, 
         wdw = {c: keep.tile([P, NW], U32, name="wdw%d_%d" % c, align_bytes=64) for c in chunks}
         wds = {c: keep.tile([P, NW], U8, name="wds%d_%d" % c, align_bytes=64) for c in chunks}
         tabw, tab2w, vw, v2w, wdraw = {}, {}, {}, {}, {}
-        one_in = keep.tile([P, 1], F32, name="one_in")
+        one_in = keep.tile([P, 1], F32, name="one_in", tag="tabw0", align_bytes=64)
         one = keep.tile([P, 1], F32, name="one")
 
         nc.vector.memset(tab2s[:].bitcast(I32), 0)
         nc.vector.memset(tabs[:].bitcast(I32), 0)
         for a in range(KP):
             nc.vector.memset(planes[a][:].bitcast(I32), 0)
-        nc.vector.memset(one_in[:], 1.0)
+        nc.gpsimd.memset(one_in[:], 1.0)
         nc.scalar.activation(one[:], one_in[:], ACT.Abs_reciprocal_sqrt)
 
         def load_words(dst, words, a, tag, cuts):
@@ -76,7 +76,7 @@ def tile_list_desk_stress_results_kernel(tc, tab_words, tab_scales, tab2_words, 
 
         def place_rows(a, quadrant):
             src = FIRST_ROW[a] + 4 * quadrant * ROW_STEP
-            nc.scalar.dma_start(
+            nc.sync.dma_start(
                 planes[a][32 * quadrant : 32 * quadrant + 4, :].bitcast(I32),
                 staged[src : src + 3 * ROW_STEP + 1 : ROW_STEP, :].bitcast(I32),
             )
@@ -95,16 +95,15 @@ def tile_list_desk_stress_results_kernel(tc, tab_words, tab_scales, tab2_words, 
                 v2w[a, jb] = picks[:, jb * JW - lo : (jb + 1) * JW - lo]
 
         nc.sync.dma_start(idx2[:], offs2)
+        load_words(tab2w, tab2_words, 0, "tab2w0", (0, T2))
         nc.sync.dma_start(idx[:], offs)
         nc.sync.dma_start(sz[:], size.rearrange("(b p t) -> p b t", b=IB, t=PACK))
-        load_words(tab2w, tab2_words, 0, "tab2w0", FIRST_CUTS)
         load_scale_rows(tab2s, tab2_scales)
         load_scale_rows(tabs, tab_scales)
         load_words(tabw, tab_words, 0, "tabw0", (0, T))
-        load_words(tab2w, tab2_words, 1, "tab2w1", (0, T2))
-        load_words(tabw, tab_words, 1, "tabw1", (0, T))
 
         gather_v2(0, 0, S2, "v2w0")
+        load_words(tabw, tab_words, 1, "tab2w0", (0, T))
         nc.vector.tensor_copy(picked[:, S:], tab2s[:].indirect(idx2[:]))
         nc.vector.tensor_copy(picked[:, :S], tabs[:].indirect(idx[:]))
         nc.vector.tensor_copy(staged[:, S:].bitcast(I32), picked[:, S:].bitcast(I32))
@@ -113,15 +112,18 @@ def tile_list_desk_stress_results_kernel(tc, tab_words, tab_scales, tab2_words, 
             picked[:, :S].rearrange("p (b m t) -> p b m t", b=IB, t=PACK),
         )
         moves = [(a, quadrant) for a in range(KP) for quadrant in range(QUADRANTS)]
-        for a, quadrant in moves:
+        for a, quadrant in moves[:PLACED_FIRST]:
+            place_rows(a, quadrant)
+        load_words(tab2w, tab2_words, 1, "picked", (0, T2))
+        for a, quadrant in moves[PLACED_FIRST:]:
             place_rows(a, quadrant)
         gather_v(0)
         load_words(tabw, tab_words, 2, "tabw0", (0, T))
-        gather_v2(1, 0, S2, "v2w1")
-        load_words(tab2w, tab2_words, 2, "tab2w1", (0, T2))
         gather_v(1)
+        load_words(tab2w, tab2_words, 2, "tab2w0", (0, T2))
+        gather_v2(1, 0, S2, "v2w1")
         gather_v(2)
-        for b, tag in enumerate(("tabw1", "tabw0")):
+        for b, tag in enumerate(("picked", "tabw0")):
             wdraw[b] = keep.tile([P, PACK, N], F32, name="wdraw%d" % b, tag=tag, align_bytes=64)
             for lo in range(0, N, NW):
                 nc.sync.dma_start(wdraw[b][:, :, lo : lo + NW], wd[b * PASS : (b + 1) * PASS, lo : lo + NW].rearrange("(p t) n -> p t n", t=PACK))
@@ -150,7 +152,7 @@ def tile_list_desk_stress_results_kernel(tc, tab_words, tab_scales, tab2_words, 
 
         gather_v2(2, 0, S2 // 2, "v2w2")
         gather_v2(2, S2 // 2, S2, "v2w2_late")
-        w4w = keep.tile([P, IB, 2 * N], U8, name="w4w", tag="tab2w1", align_bytes=64)
+        w4w = keep.tile([P, IB, 2 * N], U8, name="w4w", tag="tab2w0", align_bytes=64)
         nc.sync.dma_start(w4w[:].bitcast(I32), w4_words.rearrange("b p e -> p b e").bitcast(I32))
 
         def c_finish(k):
@@ -174,8 +176,10 @@ def tile_list_desk_stress_results_kernel(tc, tab_words, tab_scales, tab2_words, 
             b = units[k][1]
             d_t[k] = ring.tile([P, PACK, JW], F32, name="d", tag="d")
             for t in range(PACK):
-                if k < UNITS - ON_SCALAR:
-                    nc.vector.tensor_scalar_mul(d_t[k][:, t, :], w_t[k][:, t, :], sz[:, b, t : t + 1])
+                if k not in ON_SCALAR:
+                    nc.vector.scalar_tensor_tensor(
+                        out=d_t[k][:, t, :], in0=y_t[k][:, t, :], scalar=sz[:, b, t : t + 1], in1=y_t[k][:, t, :], op0=MULT, op1=MULT
+                    )
                 else:
                     nc.scalar.activation(d_t[k][:, t, :], w_t[k][:, t, :], ACT.Copy, scale=sz[:, b, t : t + 1])
 
@@ -253,7 +257,7 @@ def tile_list_desk_stress_results_kernel(tc, tab_words, tab_scales, tab2_words, 
 
         wd_cast(chunks[0])
         wd_cast(chunks[1])
-        w4s = keep.tile([P, IB, N], U8, name="w4s", tag="v2w0", align_bytes=64)
+        w4s = keep.tile([P, IB, N], U8, name="w4s", tag="staged", align_bytes=64)
         nc.vector.memset(w4s[:].rearrange("p b n -> p (b n)").bitcast(I32), 0)
         for quadrant in range(QUADRANTS):
             nc.sync.dma_start(
@@ -270,7 +274,8 @@ def tile_list_desk_stress_results_kernel(tc, tab_words, tab_scales, tab2_words, 
                 s_root(k)
                 if k + 1 < UNITS:
                     s_abs(k + 1)
-                s_square(k)
+                if k in ON_SCALAR:
+                    s_square(k)
                 size_product(k)
             if k == 0:
                 wd_quant(chunks[1])

@@ -161,7 +161,7 @@ def tile_list_desk_stress_results_kernel(tc, tab_words, tab_scales, tab2_words, 
         r_t, y_t, w_t, d_t, hg_t, hgw, hgs = {}, {}, {}, {}, {}, {}, {}
 
         def s_abs(k):
-            r_t[k] = ring.tile([P, PACK, JW], F32, name="r", tag="r", bufs=4)
+            r_t[k] = ring.tile([P, PACK, JW], F32, name="r", tag="r", bufs=6)
             nc.scalar.activation(r_t[k][:], banks[k][:], ACT.Abs)
 
         def s_root(k):
@@ -186,15 +186,15 @@ def tile_list_desk_stress_results_kernel(tc, tab_words, tab_scales, tab2_words, 
         def by_runs(src):
             return src.rearrange("p t (c i) -> p c t i", i=RUN)
 
-        def v_products(k):
-            hg_t[k] = ring.tile([P, 2, JW * PACK], BF16, name="hg", tag="hg", align_bytes=64)
-            for which, src in enumerate((banks[k], r_t[k])):
-                nc.vector.tensor_tensor(
-                    hg_t[k][:, which, :].rearrange("p (c i t) -> p c t i", i=RUN, t=PACK),
-                    by_runs(src[:]),
-                    by_runs(d_t[k][:]),
-                    MULT,
-                )
+        def v_product(k, which):
+            if which == 0:
+                hg_t[k] = ring.tile([P, 2, JW * PACK], BF16, name="hg", tag="hg", align_bytes=64)
+            nc.vector.tensor_tensor(
+                hg_t[k][:, which, :].rearrange("p (c i t) -> p c t i", i=RUN, t=PACK),
+                by_runs((banks[k], r_t[k])[which][:]),
+                by_runs(d_t[k][:]),
+                MULT,
+            )
 
         def v_quant(k):
             hgw[k] = ring.tile([P, 2 * JW], U32, name="hgw", tag="hgw", bufs=6, align_bytes=64)
@@ -265,29 +265,40 @@ def tile_list_desk_stress_results_kernel(tc, tab_words, tab_scales, tab2_words, 
                 w4_scales[:, 4 * quadrant : 4 * quadrant + 4, :].rearrange("b r n -> r b n").bitcast(I32),
             )
         wd_quant(chunks[0])
-        c_finish(0)
-        s_abs(0)
-        for k in range(UNITS + 1):
-            if k + 1 < UNITS:
-                c_finish(k + 1)
-            if k < UNITS:
-                s_root(k)
-                if k + 1 < UNITS:
-                    s_abs(k + 1)
-                if k in ON_SCALAR:
-                    s_square(k)
-                size_product(k)
-            if k == 0:
+        for k in range(IB):
+            c_finish(k)
+            s_abs(k)
+        for jb in range(JB):
+            x, z = jb * IB, jb * IB + 1
+            ahead = [k for k in (x + IB, z + IB) if k < UNITS]
+            for k in ahead:
+                c_finish(k)
+            s_root(x)
+            s_root(z)
+            for k in ahead[:1]:
+                s_abs(k)
+            s_square(z)
+            for k in ahead[1:]:
+                s_abs(k)
+            size_product(z)
+            size_product(x)
+            if jb == 0:
                 wd_quant(chunks[1])
             else:
-                v_quant(k - 1)
-            if k < UNITS:
-                v_products(k)
-            if 2 + k < len(chunks):
-                wd_cast(chunks[2 + k])
-            if 2 <= 1 + k < len(chunks):
-                wd_quant(chunks[1 + k])
-            if k == UNITS:
-                last_block()
-            elif k > 0 and k % IB == 0:
-                out_block(k // IB - 1)
+                v_quant(x - 1)
+            if jb == 1:
+                wd_quant(chunks[3])
+            v_product(x, 0)
+            v_product(x, 1)
+            if jb == 0:
+                wd_cast(chunks[2])
+            else:
+                out_block(jb - 1)
+            v_product(z, 0)
+            v_quant(x)
+            v_product(z, 1)
+            if jb == 0:
+                wd_quant(chunks[2])
+                wd_cast(chunks[3])
+        v_quant(UNITS - 1)
+        last_block()

@@ -115,10 +115,12 @@ def tile_list_desk_stress_results_kernel(tc, tab_words, tab_scales, tab2_words, 
         for a, quadrant in moves[:PLACED_FIRST]:
             place_rows(a, quadrant)
         load_words(tab2w, tab2_words, 1, "picked", (0, T2))
-        for a, quadrant in moves[PLACED_FIRST:]:
+        for a, quadrant in moves[PLACED_FIRST : 2 * QUADRANTS]:
             place_rows(a, quadrant)
         gather_v(0)
         load_words(tabw, tab_words, 2, "tabw0", (0, T))
+        for a, quadrant in moves[2 * QUADRANTS :]:
+            place_rows(a, quadrant)
         gather_v(1)
         load_words(tab2w, tab2_words, 2, "tab2w0", (0, T2))
         gather_v2(1, 0, S2, "v2w1")
@@ -257,8 +259,8 @@ def tile_list_desk_stress_results_kernel(tc, tab_words, tab_scales, tab2_words, 
 
         wd_cast(chunks[0])
         wd_cast(chunks[1])
-        w4s = keep.tile([P, IB, N], U8, name="w4s", tag="staged", align_bytes=64)
-        nc.vector.memset(w4s[:].rearrange("p b n -> p (b n)").bitcast(I32), 0)
+        w4s = keep.tile([P, IB, N], U8, name="w4s", tag="v2w0", align_bytes=64)
+        nc.gpsimd.memset(w4s[:].rearrange("p b n -> p (b n)").bitcast(I32), 0)
         for quadrant in range(QUADRANTS):
             nc.sync.dma_start(
                 w4s[32 * quadrant : 32 * quadrant + 4, :, :].bitcast(I32),

@@ -108,8 +108,8 @@ def tile_list_desk_stress_results_kernel(tc, tab_words, tab_scales, tab2_words, 
         nc.vector.tensor_copy(picked[:, :S], tabs[:].indirect(idx[:]))
         nc.vector.tensor_copy(staged[:, S:].bitcast(I32), picked[:, S:].bitcast(I32))
         nc.vector.tensor_copy(
-            staged[:, :S].rearrange("p (b t m) -> p b m t", b=IB, t=PACK),
-            picked[:, :S].rearrange("p (b m t) -> p b m t", b=IB, t=PACK),
+            staged[:, :S].rearrange("p (b t m) -> p b t m", b=IB, t=PACK),
+            picked[:, :S].rearrange("p (b m t) -> p b t m", b=IB, t=PACK),
         )
         moves = [(a, quadrant) for a in range(KP) for quadrant in range(QUADRANTS)]
         for a, quadrant in moves[:PLACED_FIRST]:

@@ -74,11 +74,11 @@ def tile_list_desk_stress_results_kernel(tc, tab_words, tab_scales, tab2_words, 
             nc.sync.dma_start(dst[0:P:ROW_STEP, :].bitcast(I32), scales[0:2].rearrange("a r t -> (a r) t").bitcast(I32))
             nc.sync.dma_start(dst[FIRST_ROW[2] : FIRST_ROW[2] + 16 * ROW_STEP : ROW_STEP, :].bitcast(I32), scales[2].bitcast(I32))
 
-        def place_rows(a, quadrant):
-            src = FIRST_ROW[a] + 4 * quadrant * ROW_STEP
+        def place_rows(a, r):
+            src = FIRST_ROW[a] + r * ROW_STEP
             nc.sync.dma_start(
-                planes[a][32 * quadrant : 32 * quadrant + 4, :].bitcast(I32),
-                staged[src : src + 3 * ROW_STEP + 1 : ROW_STEP, :].bitcast(I32),
+                planes[a][4 * a + r : P : 32, :].bitcast(I32),
+                staged[src : src + 12 * ROW_STEP + 1 : 4 * ROW_STEP, :].bitcast(I32),
             )
 
         def gather_v(a):
@@ -139,9 +139,9 @@ def tile_list_desk_stress_results_kernel(tc, tab_words, tab_scales, tab2_words, 
                 nc.tensor.matmul_mx(
                     out=banks[k][:, t, :],
                     lhsT=vw[a][:, icols].bitcast(FP8X4),
-                    lhsT_scale=planes[a][:, icols],
+                    lhsT_scale=planes[a][4 * a :, icols],
                     rhs=v2w[a, jb].bitcast(FP8X4),
-                    rhs_scale=planes[a][:, S + jb * JW : S + (jb + 1) * JW],
+                    rhs_scale=planes[a][4 * a :, S + jb * JW : S + (jb + 1) * JW],
                     start=(a == 0 and t == 0),
                     stop=(a == KP - 1 and t == PACK - 1),
                 )

@@ -39,6 +39,7 @@ def tile_list_desk_stress_results_kernel(tc, tab_words, tab_scales, tab2_words, 
     nc = tc.nc
     with ExitStack() as ctx:
         keep = ctx.enter_context(tc.tile_pool(name="keep", bufs=1))
+        laid = ctx.enter_context(tc.tile_pool(name="laid", bufs=1))
         ring = ctx.enter_context(tc.tile_pool(name="ring", bufs=3))
         psum = ctx.enter_context(tc.psum_pool(name="psum", bufs=UNITS))
 
@@ -46,7 +47,7 @@ def tile_list_desk_stress_results_kernel(tc, tab_words, tab_scales, tab2_words, 
         idx2 = keep.tile([P, S2 // LIST_ROWS], U16, name="idx2")
         tabs = keep.tile([P, T], U8, name="tabs", align_bytes=64)
         tab2s = keep.tile([P, T2], U8, name="tab2s", align_bytes=64)
-        picked = keep.tile([P, S + S2], U8, name="picked", tag="picked", align_bytes=64)
+        picked = laid.tile([P, S + S2], U8, name="picked", offset=4 * T2 - (S + S2) // 2)
         staged = keep.tile([P, S + S2], U8, name="staged", tag="staged", align_bytes=64)
         planes = [keep.tile([P, S + S2], U8, name="planes%d" % a, align_bytes=64) for a in range(KP)]
         sz = keep.tile([P, IB, PACK], F32, name="sz")
@@ -66,7 +67,10 @@ def tile_list_desk_stress_results_kernel(tc, tab_words, tab_scales, tab2_words, 
         nc.scalar.activation(one[:], one_in[:], ACT.Abs_reciprocal_sqrt)
 
         def load_words(dst, words, a, tag, cuts):
-            dst[a] = keep.tile([P, cuts[-1]], I32, name="words_%d_%d" % (a, cuts[-1]), tag=tag, align_bytes=64)
+            if isinstance(tag, int):
+                dst[a] = laid.tile([P, cuts[-1]], I32, name="words_%d_%d" % (a, cuts[-1]), offset=tag)
+            else:
+                dst[a] = keep.tile([P, cuts[-1]], I32, name="words_%d_%d" % (a, cuts[-1]), tag=tag, align_bytes=64)
             for lo, hi in zip(cuts[:-1], cuts[1:]):
                 nc.sync.dma_start(dst[a][:, lo:hi], words[a, :, lo:hi, :].rearrange("p t i -> p (t i)").bitcast(I32))
 
@@ -114,19 +118,19 @@ def tile_list_desk_stress_results_kernel(tc, tab_words, tab_scales, tab2_words, 
         moves = [(a, quadrant) for a in range(KP) for quadrant in range(QUADRANTS)]
         for a, quadrant in moves[:PLACED_FIRST]:
             place_rows(a, quadrant)
-        load_words(tab2w, tab2_words, 1, "picked", (0, T2))
+        load_words(tab2w, tab2_words, 1, 0, (0, T2))
         for a, quadrant in moves[PLACED_FIRST : 2 * QUADRANTS]:
             place_rows(a, quadrant)
         gather_v(0)
-        load_words(tabw, tab_words, 2, "tabw0", (0, T))
+        load_words(tabw, tab_words, 2, 4 * T2, (0, T))
         for a, quadrant in moves[2 * QUADRANTS :]:
             place_rows(a, quadrant)
         gather_v(1)
         load_words(tab2w, tab2_words, 2, "tab2w0", (0, T2))
         gather_v2(1, 0, S2, "v2w1")
         gather_v(2)
-        for b, tag in enumerate(("picked", "tabw0")):
-            wdraw[b] = keep.tile([P, PACK, N], F32, name="wdraw%d" % b, tag=tag, align_bytes=64)
+        for b in range(IB):
+            wdraw[b] = laid.tile([P, PACK, N], F32, name="wdraw%d" % b, offset=b * 4 * T2)
             for lo in range(0, N, NW):
                 nc.sync.dma_start(wdraw[b][:, :, lo : lo + NW], wd[b * PASS : (b + 1) * PASS, lo : lo + NW].rearrange("(p t) n -> p t n", t=PACK))
 

@@ -50,7 +50,6 @@ def tile_list_desk_stress_results_kernel(tc, tab_words, tab_scales, tab2_words, 
         picked = laid.tile([P, S + S2], U8, name="picked", offset=4 * T2 - (S + S2) // 2)
         staged = keep.tile([P, S + S2], U8, name="staged", tag="staged", align_bytes=64)
         planes = [keep.tile([P, S + S2], U8, name="planes%d" % a, align_bytes=64) for a in range(KP)]
-        sz = keep.tile([P, IB, PACK], F32, name="sz")
         chunks = [(b, u) for b in range(IB) for u in range(N // NW)]
         wdbf = {c: keep.tile([P, NW, PACK], BF16, name="wdbf%d_%d" % c, align_bytes=64) for c in chunks}
         wdw = {c: keep.tile([P, NW], U32, name="wdw%d_%d" % c, align_bytes=64) for c in chunks}
@@ -98,10 +97,9 @@ def tile_list_desk_stress_results_kernel(tc, tab_words, tab_scales, tab2_words, 
             for jb in range(lo // JW, hi // JW):
                 v2w[a, jb] = picks[:, jb * JW - lo : (jb + 1) * JW - lo]
 
-        nc.sync.dma_start(idx2[:], offs2)
         load_words(tab2w, tab2_words, 0, "tab2w0", (0, T2))
+        nc.sync.dma_start(idx2[:], offs2)
         nc.sync.dma_start(idx[:], offs)
-        nc.sync.dma_start(sz[:], size.rearrange("(b p t) -> p b t", b=IB, t=PACK))
         load_scale_rows(tab2s, tab2_scales)
         load_scale_rows(tabs, tab_scales)
         load_words(tabw, tab_words, 0, "tabw0", (0, T))
@@ -122,15 +120,17 @@ def tile_list_desk_stress_results_kernel(tc, tab_words, tab_scales, tab2_words, 
         for a, quadrant in moves[PLACED_FIRST : 2 * QUADRANTS]:
             place_rows(a, quadrant)
         gather_v(0)
-        load_words(tabw, tab_words, 2, 4 * T2, (0, T))
+        load_words(tabw, tab_words, 2, 4 * T2 + 64, (0, T))
         for a, quadrant in moves[2 * QUADRANTS :]:
             place_rows(a, quadrant)
+        sz = laid.tile([P, IB, PACK], F32, name="sz", offset=4 * T2)
+        nc.sync.dma_start(sz[:], size.rearrange("(b p t) -> p b t", b=IB, t=PACK))
         gather_v(1)
         load_words(tab2w, tab2_words, 2, "tab2w0", (0, T2))
         gather_v2(1, 0, S2, "v2w1")
         gather_v(2)
         for b in range(IB):
-            wdraw[b] = laid.tile([P, PACK, N], F32, name="wdraw%d" % b, offset=b * 4 * T2)
+            wdraw[b] = laid.tile([P, PACK, N], F32, name="wdraw%d" % b, offset=b * (4 * T2 + 64))
             for lo in range(0, N, NW):
                 nc.sync.dma_start(wdraw[b][:, :, lo : lo + NW], wd[b * PASS : (b + 1) * PASS, lo : lo + NW].rearrange("(p t) n -> p t n", t=PACK))
 

@@ -25,14 +25,26 @@ JW = 128
 JB = S2 // JW
 NT = N // P
 UNITS = JB * IB
+LAST = UNITS - 1
 NW = 256
-QUADRANTS = 4
+QUADRANT = 32
+ROWS = 4
 LIST_ROWS = 16
 RUN = 4
-FIRST_ROW = (0, 64, 33)
+H, G = 0, 1
 ROW_STEP = 4
-PLACED_FIRST = 6
-ON_SCALAR = (1, 3, 5, 7)
+PASS2_ROW = 33
+LAP = 64
+AT_TAB2_1 = 0
+AT_TAB2_0 = 4 * T2 - LAP
+AT_TAB_1 = 8 * T2 - 2 * LAP
+AT_TAB2_2 = 4 * (2 * T2 + T)
+AT_SIZE = AT_TAB2_2 + 4 * T2
+AT_TAB_2 = AT_SIZE + LAP
+AT_DEALT = AT_SIZE - S2
+ON_VECTOR = 3
+SQUARED = 2
+HG_BUFS = 3
 
 
 def tile_list_desk_stress_results_kernel(tc, tab_words, tab_scales, tab2_words, tab2_scales, offs, offs2, size, wd, w4_words, w4_scales, out):
@@ -40,49 +52,41 @@ def tile_list_desk_stress_results_kernel(tc, tab_words, tab_scales, tab2_words, 
     with ExitStack() as ctx:
         keep = ctx.enter_context(tc.tile_pool(name="keep", bufs=1))
         laid = ctx.enter_context(tc.tile_pool(name="laid", bufs=1))
-        ring = ctx.enter_context(tc.tile_pool(name="ring", bufs=3))
+        ring = ctx.enter_context(tc.tile_pool(name="ring", bufs=HG_BUFS))
         psum = ctx.enter_context(tc.psum_pool(name="psum", bufs=UNITS))
 
         idx = keep.tile([P, S // LIST_ROWS], U16, name="idx")
         idx2 = keep.tile([P, S2 // LIST_ROWS], U16, name="idx2")
         tabs = keep.tile([P, T], U8, name="tabs", align_bytes=64)
         tab2s = keep.tile([P, T2], U8, name="tab2s", align_bytes=64)
-        picked = laid.tile([P, S + S2], U8, name="picked", offset=4 * T2 - (S + S2) // 2)
-        staged = keep.tile([P, S + S2], U8, name="staged", tag="staged", align_bytes=64)
-        planes = [keep.tile([P, S + S2], U8, name="planes%d" % a, align_bytes=64) for a in range(KP)]
+        picked = keep.tile([P, S + S2], U8, name="picked", align_bytes=64)
+        dealt = laid.tile([P, S + S2], U8, name="dealt", offset=AT_DEALT)
+        staged = keep.tile([P, S + S2], U8, name="staged", align_bytes=64)
+        early = keep.tile([P, S + S2], U8, name="early", align_bytes=64)
+        late = keep.tile([P, S + S2], U8, name="late", align_bytes=64)
+        planes = [early, early, late]
         chunks = [(b, u) for b in range(IB) for u in range(N // NW)]
-        wdbf = {c: keep.tile([P, NW, PACK], BF16, name="wdbf%d_%d" % c, align_bytes=64) for c in chunks}
-        wdw = {c: keep.tile([P, NW], U32, name="wdw%d_%d" % c, align_bytes=64) for c in chunks}
-        wds = {c: keep.tile([P, NW], U8, name="wds%d_%d" % c, align_bytes=64) for c in chunks}
-        tabw, tab2w, vw, v2w, wdraw = {}, {}, {}, {}, {}
+        wds = {ch: keep.tile([P, NW], U8, name="wds%d_%d" % ch, align_bytes=64) for ch in chunks}
+        tabw, tab2w, vw, v2w, wdraw, wdbf, wdw = {}, {}, {}, {}, {}, {}, {}
         one_in = keep.tile([P, 1], F32, name="one_in", tag="tabw0", align_bytes=64)
         one = keep.tile([P, 1], F32, name="one")
 
         nc.vector.memset(tab2s[:].bitcast(I32), 0)
         nc.vector.memset(tabs[:].bitcast(I32), 0)
-        for a in range(KP):
-            nc.vector.memset(planes[a][:].bitcast(I32), 0)
+        nc.vector.memset(late[:].bitcast(I32), 0)
         nc.gpsimd.memset(one_in[:], 1.0)
         nc.scalar.activation(one[:], one_in[:], ACT.Abs_reciprocal_sqrt)
 
-        def load_words(dst, words, a, tag, cuts):
-            if isinstance(tag, int):
-                dst[a] = laid.tile([P, cuts[-1]], I32, name="words_%d_%d" % (a, cuts[-1]), offset=tag)
-            else:
-                dst[a] = keep.tile([P, cuts[-1]], I32, name="words_%d_%d" % (a, cuts[-1]), tag=tag, align_bytes=64)
-            for lo, hi in zip(cuts[:-1], cuts[1:]):
-                nc.sync.dma_start(dst[a][:, lo:hi], words[a, :, lo:hi, :].rearrange("p t i -> p (t i)").bitcast(I32))
+        def load_words(tile, words):
+            nc.sync.dma_start(tile[:], words.rearrange("p t i -> p (t i)").bitcast(I32))
+            return tile
 
         def load_scale_rows(dst, scales):
-            nc.sync.dma_start(dst[0:P:ROW_STEP, :].bitcast(I32), scales[0:2].rearrange("a r t -> (a r) t").bitcast(I32))
-            nc.sync.dma_start(dst[FIRST_ROW[2] : FIRST_ROW[2] + 16 * ROW_STEP : ROW_STEP, :].bitcast(I32), scales[2].bitcast(I32))
+            nc.sync.dma_start(dst[0:P:ROW_STEP, :].bitcast(I32), scales[0:2].rearrange("a q t -> q a t").bitcast(I32))
+            nc.sync.dma_start(dst[PASS2_ROW : PASS2_ROW + 16 * ROW_STEP : ROW_STEP, :].bitcast(I32), scales[2].bitcast(I32))
 
-        def place_rows(a, r):
-            src = FIRST_ROW[a] + r * ROW_STEP
-            nc.sync.dma_start(
-                planes[a][4 * a + r : P : 32, :].bitcast(I32),
-                staged[src : src + 12 * ROW_STEP + 1 : 4 * ROW_STEP, :].bitcast(I32),
-            )
+        def place_rows(a, row, src):
+            nc.sync.dma_start(planes[a][ROWS * a + row : P : QUADRANT, :].bitcast(I32), src.bitcast(I32))
 
         def gather_v(a):
             vw[a] = keep.tile([P, S], U32, name="vw%d" % a, align_bytes=64)
@@ -91,149 +95,157 @@ def tile_list_desk_stress_results_kernel(tc, tab_words, tab_scales, tab2_words, 
                 tabw[a][:].bitcast(U32).indirect(idx[:]),
             )
 
-        def gather_v2(a, lo, hi, tag):
-            picks = keep.tile([P, hi - lo], U32, name="v2w%d_%d" % (a, lo), tag=tag, align_bytes=64)
+        def gather_v2(a, lo, hi):
+            picks = keep.tile([P, hi - lo], U32, name="v2w%d_%d" % (a, lo), align_bytes=64)
             nc.vector.tensor_copy(picks[:], tab2w[a][:].bitcast(U32).indirect(idx2[:, lo // LIST_ROWS : hi // LIST_ROWS]))
             for jb in range(lo // JW, hi // JW):
                 v2w[a, jb] = picks[:, jb * JW - lo : (jb + 1) * JW - lo]
 
-        load_words(tab2w, tab2_words, 0, "tab2w0", (0, T2))
+        tab2w[0] = load_words(laid.tile([P, T2], I32, name="tab2w0", offset=AT_TAB2_0), tab2_words[0])
         nc.sync.dma_start(idx2[:], offs2)
         nc.sync.dma_start(idx[:], offs)
         load_scale_rows(tab2s, tab2_scales)
         load_scale_rows(tabs, tab_scales)
-        load_words(tabw, tab_words, 0, "tabw0", (0, T))
+        tabw[0] = load_words(keep.tile([P, T], I32, name="tabw0", tag="tabw0", align_bytes=64), tab_words[0])
 
-        gather_v2(0, 0, S2, "v2w0")
-        load_words(tabw, tab_words, 1, "tab2w0", (0, T))
+        gather_v2(0, 0, S2)
+        tab2w[1] = load_words(laid.tile([P, T2], I32, name="tab2w1", offset=AT_TAB2_1), tab2_words[1])
+        tabw[1] = load_words(laid.tile([P, T], I32, name="tabw1", offset=AT_TAB_1), tab_words[1])
         nc.vector.tensor_copy(picked[:, S:], tab2s[:].indirect(idx2[:]))
         nc.vector.tensor_copy(picked[:, :S], tabs[:].indirect(idx[:]))
-        nc.vector.tensor_copy(staged[:, S:].bitcast(I32), picked[:, S:].bitcast(I32))
+        nc.vector.tensor_copy(dealt[:, S:].bitcast(I32), picked[:, S:].bitcast(I32))
         nc.vector.tensor_copy(
-            staged[:, :S].rearrange("p (b t m) -> p b t m", b=IB, t=PACK),
+            dealt[:, :S].rearrange("p (b t m) -> p b t m", b=IB, t=PACK),
             picked[:, :S].rearrange("p (b m t) -> p b t m", b=IB, t=PACK),
         )
-        moves = [(a, quadrant) for a in range(KP) for quadrant in range(QUADRANTS)]
-        for a, quadrant in moves[:PLACED_FIRST]:
-            place_rows(a, quadrant)
-        load_words(tab2w, tab2_words, 1, 0, (0, T2))
-        for a, quadrant in moves[PLACED_FIRST : 2 * QUADRANTS]:
-            place_rows(a, quadrant)
-        gather_v(0)
-        load_words(tabw, tab_words, 2, 4 * T2 + 64, (0, T))
-        for a, quadrant in moves[2 * QUADRANTS :]:
-            place_rows(a, quadrant)
-        sz = laid.tile([P, IB, PACK], F32, name="sz", offset=4 * T2)
+        nc.vector.tensor_copy(early[:].bitcast(I32), dealt[:].bitcast(I32))
+        nc.vector.tensor_copy(staged[:].bitcast(I32), dealt[:].bitcast(I32))
+        for a in range(KP - 1):
+            for row in range(1, ROWS):
+                place_rows(a, row, staged[ROW_STEP * (2 * row + a) : P : QUADRANT, :])
+        tabw[2] = load_words(laid.tile([P, T], I32, name="tabw2", offset=AT_TAB_2), tab_words[2])
+        tab2w[2] = load_words(laid.tile([P, T2], I32, name="tab2w2", offset=AT_TAB2_2), tab2_words[2])
+        for row in range(ROWS):
+            src = PASS2_ROW + row * ROW_STEP
+            place_rows(KP - 1, row, staged[src : src + 3 * ROWS * ROW_STEP + 1 : ROWS * ROW_STEP, :])
+        sz = laid.tile([P, IB, PACK], F32, name="sz", offset=AT_SIZE)
         nc.sync.dma_start(sz[:], size.rearrange("(b p t) -> p b t", b=IB, t=PACK))
+        gather_v(0)
+        gather_v2(1, 0, S2)
         gather_v(1)
-        load_words(tab2w, tab2_words, 2, "tab2w0", (0, T2))
-        gather_v2(1, 0, S2, "v2w1")
         gather_v(2)
         for b in range(IB):
-            wdraw[b] = laid.tile([P, PACK, N], F32, name="wdraw%d" % b, offset=b * (4 * T2 + 64))
+            wdraw[b] = laid.tile([P, PACK, N], F32, name="wdraw%d" % b, offset=AT_TAB_1 + b * 4 * PACK * N)
             for lo in range(0, N, NW):
                 nc.sync.dma_start(wdraw[b][:, :, lo : lo + NW], wd[b * PASS : (b + 1) * PASS, lo : lo + NW].rearrange("(p t) n -> p t n", t=PACK))
 
         units = [(jb, b) for jb in range(JB) for b in range(IB)]
 
-        def c_pass(k, a):
-            jb, b = units[k]
+        def c_pass(u, a):
+            jb, b = units[u]
             for t in range(PACK):
                 icols = slice(b * PASS + t * P, b * PASS + (t + 1) * P)
                 nc.tensor.matmul_mx(
-                    out=banks[k][:, t, :],
+                    out=banks[u][:, t, :],
                     lhsT=vw[a][:, icols].bitcast(FP8X4),
-                    lhsT_scale=planes[a][4 * a :, icols],
+                    lhsT_scale=planes[a][ROWS * a :, icols],
                     rhs=v2w[a, jb].bitcast(FP8X4),
-                    rhs_scale=planes[a][4 * a :, S + jb * JW : S + (jb + 1) * JW],
+                    rhs_scale=planes[a][ROWS * a :, S + jb * JW : S + (jb + 1) * JW],
                     start=(a == 0 and t == 0),
                     stop=(a == KP - 1 and t == PACK - 1),
                 )
 
-        banks = [psum.tile([P, PACK, JW], F32, name="bank", tag="bank") for k in range(UNITS)]
-        for k in range(UNITS):
-            c_pass(k, 0)
-        for k in range(UNITS):
-            c_pass(k, 1)
+        banks = [psum.tile([P, PACK, JW], F32, name="bank", tag="bank") for u in range(UNITS)]
+        for a in range(KP - 1):
+            for u in range(UNITS):
+                c_pass(u, a)
 
-        gather_v2(2, 0, S2 // 2, "v2w2")
-        gather_v2(2, S2 // 2, S2, "v2w2_late")
-        w4w = keep.tile([P, IB, 2 * N], U8, name="w4w", tag="tab2w0", align_bytes=64)
+        gather_v2(KP - 1, 0, S2 // 2)
+        gather_v2(KP - 1, S2 // 2, S2)
+        w4w = laid.tile([P, IB, 2 * N], U8, name="w4w", offset=AT_TAB2_2, align_bytes=64)
         nc.sync.dma_start(w4w[:].bitcast(I32), w4_words.rearrange("b p e -> p b e").bitcast(I32))
-
-        def c_finish(k):
-            c_pass(k, KP - 1)
 
         r_t, y_t, w_t, d_t, hg_t, hgw, hgs = {}, {}, {}, {}, {}, {}, {}
 
-        def s_abs(k):
-            r_t[k] = ring.tile([P, PACK, JW], F32, name="r", tag="r", bufs=6)
-            nc.scalar.activation(r_t[k][:], banks[k][:], ACT.Abs)
+        def in_turn(shape, dtype):
+            return ring.tile(shape, dtype, name="turn", tag="turn", bufs=UNITS + len(chunks) - 1, align_bytes=64)
 
-        def s_root(k):
-            y_t[k] = ring.tile([P, PACK, JW], F32, name="y", tag="y")
-            nc.scalar.activation(y_t[k][:], r_t[k][:], ACT.Abs_reciprocal_sqrt, bias=one[:])
+        def activate(name, src, count, parts, func, **operands):
+            dst = keep.tile([P, count, JW], F32, name=name)
+            for lo in range(0, count, count // parts):
+                ts = slice(lo, lo + count // parts)
+                nc.scalar.activation(dst[:, ts, :], src[:, ts, :], func, **operands)
+            return dst
 
-        def s_square(k):
-            w_t[k] = ring.tile([P, PACK, JW], F32, name="w", tag="w")
-            nc.scalar.activation(w_t[k][:], y_t[k][:], ACT.Square)
+        def s_abs(u, parts=1):
+            r_t[u] = activate("r%d" % u, banks[u], PACK, parts, ACT.Abs)
 
-        def size_product(k):
-            b = units[k][1]
-            d_t[k] = ring.tile([P, PACK, JW], F32, name="d", tag="d")
+        def s_root(u, parts=1):
+            y_t[u] = activate("y%d" % u, r_t[u], PACK, parts, ACT.Abs_reciprocal_sqrt, bias=one[:])
+
+        def s_square(u, parts=1):
+            w_t[u] = activate("w%d" % u, y_t[u], SQUARED if u < ON_VECTOR else PACK, parts, ACT.Square)
+
+        def size_product(u):
+            d_t[u] = in_turn([P, PACK, JW], F32)
             for t in range(PACK):
-                if k not in ON_SCALAR:
-                    nc.vector.scalar_tensor_tensor(
-                        out=d_t[k][:, t, :], in0=y_t[k][:, t, :], scalar=sz[:, b, t : t + 1], in1=y_t[k][:, t, :], op0=MULT, op1=MULT
-                    )
+                scale = sz[:, units[u][1], t : t + 1]
+                if u >= ON_VECTOR:
+                    nc.scalar.activation(d_t[u][:, t, :], w_t[u][:, t, :], ACT.Copy, scale=scale)
+                elif u == ON_VECTOR - 1 and t < SQUARED:
+                    nc.vector.tensor_scalar(out=d_t[u][:, t, :], in0=w_t[u][:, t, :], scalar1=scale, scalar2=None, op0=MULT)
                 else:
-                    nc.scalar.activation(d_t[k][:, t, :], w_t[k][:, t, :], ACT.Copy, scale=sz[:, b, t : t + 1])
+                    nc.vector.scalar_tensor_tensor(
+                        out=d_t[u][:, t, :], in0=y_t[u][:, t, :], scalar=scale, in1=y_t[u][:, t, :], op0=MULT, op1=MULT
+                    )
 
         def by_runs(src):
             return src.rearrange("p t (c i) -> p c t i", i=RUN)
 
-        def v_product(k, which):
-            if which == 0:
-                hg_t[k] = ring.tile([P, 2, JW * PACK], BF16, name="hg", tag="hg", align_bytes=64)
+        def v_product(u, half):
+            if u not in hg_t:
+                hg_t[u] = ring.tile([P, 2, JW * PACK], BF16, name="hg", tag="hg", align_bytes=64)
             nc.vector.tensor_tensor(
-                hg_t[k][:, which, :].rearrange("p (c i t) -> p c t i", i=RUN, t=PACK),
-                by_runs((banks[k], r_t[k])[which][:]),
-                by_runs(d_t[k][:]),
+                hg_t[u][:, half, :].rearrange("p (c i t) -> p c t i", i=RUN, t=PACK),
+                by_runs((banks[u], r_t[u])[half][:]),
+                by_runs(d_t[u][:]),
                 MULT,
             )
 
-        def v_quant(k):
-            hgw[k] = ring.tile([P, 2 * JW], U32, name="hgw", tag="hgw", bufs=6, align_bytes=64)
-            hgs[k] = ring.tile([P, 2 * JW], U8, name="hgs", tag="hgs", bufs=6, align_bytes=64)
-            if k < UNITS - 1:
-                nc.vector.quantize_mx(out=hgw[k][:].bitcast(FP8X4), scales=hgs[k][:], in_=hg_t[k][:].rearrange("p w c -> p (w c)"))
+        def v_quant(u, halves=None):
+            hgw[u] = ring.tile([P, 2 * JW], U32, name="hgw", tag="hgw", bufs=UNITS, align_bytes=64)
+            hgs[u] = ring.tile([P, 2 * JW], U8, name="hgs", tag="hgs", bufs=UNITS, align_bytes=64)
+            if halves is None:
+                nc.vector.quantize_mx(out=hgw[u][:].bitcast(FP8X4), scales=hgs[u][:], in_=hg_t[u][:].rearrange("p w c -> p (w c)"))
             else:
-                for which in range(2):
-                    cols = slice(which * JW, (which + 1) * JW)
-                    nc.vector.quantize_mx(out=hgw[k][:, cols].bitcast(FP8X4), scales=hgs[k][:, cols], in_=hg_t[k][:, which, :])
+                for half in halves:
+                    cols = slice(half * JW, (half + 1) * JW)
+                    nc.vector.quantize_mx(out=hgw[u][:, cols].bitcast(FP8X4), scales=hgs[u][:, cols], in_=hg_t[u][:, half, :])
 
-        def wd_cast(c):
+        def wd_cast(ch, tile):
+            wdbf[ch] = tile
             nc.vector.tensor_copy(
-                wdbf[c][:].rearrange("p (c i) t -> p c t i", i=RUN),
-                by_runs(wdraw[c[0]][:, :, c[1] * NW : (c[1] + 1) * NW]),
+                tile[:].rearrange("p (c i) t -> p c t i", i=RUN),
+                by_runs(wdraw[ch[0]][:, :, ch[1] * NW : (ch[1] + 1) * NW]),
             )
 
-        def wd_quant(c):
-            nc.vector.quantize_mx(out=wdw[c][:].bitcast(FP8X4), scales=wds[c][:], in_=wdbf[c][:].rearrange("p n t -> p (n t)"))
+        def wd_quant(ch):
+            wdw[ch] = keep.tile([P, NW], U32, name="wdw%d_%d" % ch, align_bytes=64)
+            nc.vector.quantize_mx(out=wdw[ch][:].bitcast(FP8X4), scales=wds[ch][:], in_=wdbf[ch][:].rearrange("p n t -> p (n t)"))
 
-        def linear_pass(dst, nt, k, first):
-            c = (units[k][1], nt * P // NW)
-            wcols = slice(nt * P % NW, nt * P % NW + P)
-            nc.tensor.matmul_mx(
-                out=dst, lhsT=wdw[c][:, wcols].bitcast(FP8X4), lhsT_scale=wds[c][:, wcols],
-                rhs=hgw[k][:, 0:JW].bitcast(FP8X4), rhs_scale=hgs[k][:, 0:JW], start=first, stop=False,
-            )
-
-        def option_pass(dst, nt, k, final):
-            b = units[k][1]
+        def option_pass(dst, nt, u, start):
+            b = units[u][1]
             nc.tensor.matmul_mx(
                 out=dst, lhsT=w4w[:, b, 2 * nt * P : 2 * (nt + 1) * P].bitcast(FP4X4), lhsT_scale=w4s[:, b, nt * P : (nt + 1) * P],
-                rhs=hgw[k][:, JW : 2 * JW].bitcast(FP8X4), rhs_scale=hgs[k][:, JW : 2 * JW], start=False, stop=final,
+                rhs=hgw[u][:, JW : 2 * JW].bitcast(FP8X4), rhs_scale=hgs[u][:, JW : 2 * JW], start=start, stop=False,
+            )
+
+        def linear_pass(dst, nt, u, stop):
+            ch = (units[u][1], nt * P // NW)
+            wcols = slice(nt * P % NW, nt * P % NW + P)
+            nc.tensor.matmul_mx(
+                out=dst, lhsT=wdw[ch][:, wcols].bitcast(FP8X4), lhsT_scale=wds[ch][:, wcols],
+                rhs=hgw[u][:, 0:JW].bitcast(FP8X4), rhs_scale=hgs[u][:, 0:JW], start=False, stop=stop,
             )
 
         out_v = out.rearrange("(nt p) j -> p nt j", p=P)
@@ -242,69 +254,72 @@ def tile_list_desk_stress_results_kernel(tc, tab_words, tab_scales, tab2_words, 
             accs = [psum.tile([P, NT, JW], F32, name="bank", tag="bank") for part in range(NT // per_bank)]
             for b in range(IB):
                 for nt in range(NT):
-                    linear_pass(accs[nt // per_bank][:, nt % per_bank, :], nt, jb * IB + b, b == 0 and nt % per_bank == 0)
+                    option_pass(accs[nt // per_bank][:, nt % per_bank, :], nt, jb * IB + b, b == 0 and nt % per_bank == 0)
                 for nt in range(NT):
-                    option_pass(accs[nt // per_bank][:, nt % per_bank, :], nt, jb * IB + b, b == IB - 1 and nt % per_bank == per_bank - 1)
+                    linear_pass(accs[nt // per_bank][:, nt % per_bank, :], nt, jb * IB + b, b == IB - 1 and nt % per_bank == per_bank - 1)
             return accs
 
-        def out_block(jb):
-            accs = out_sums(jb, NT)
-            res = ring.tile([P, NT, JW], F32, name="res", tag="res")
-            nc.scalar.copy(res[:], accs[0][:])
-            nc.sync.dma_start(out_v[:, :, jb * JW : (jb + 1) * JW], res[:])
-
-        def last_block():
-            half_nt = NT // 2
-            accs = out_sums(JB - 1, half_nt)
-            for half, copy, queue in ((0, nc.vector.tensor_copy, nc.sync), (1, nc.scalar.copy, nc.scalar)):
-                res = keep.tile([P, half_nt, JW], F32, name="res_last%d" % half)
-                copy(res[:], accs[half][:, 0:half_nt, :])
-                queue.dma_start(out_v[:, half * half_nt : (half + 1) * half_nt, (JB - 1) * JW : JB * JW], res[:])
-
-        wd_cast(chunks[0])
-        wd_cast(chunks[1])
-        w4s = keep.tile([P, IB, N], U8, name="w4s", tag="v2w0", align_bytes=64)
-        nc.gpsimd.memset(w4s[:].rearrange("p b n -> p (b n)").bitcast(I32), 0)
-        for quadrant in range(QUADRANTS):
+        wd_cast(chunks[0], keep.tile([P, NW, PACK], BF16, name="wdbf0", align_bytes=64))
+        for u in range(UNITS):
+            c_pass(u, KP - 1)
+        w4s = late[:, 0 : IB * N].rearrange("p (b n) -> p b n", b=IB)
+        for quadrant in range(P // QUADRANT):
             nc.sync.dma_start(
-                w4s[32 * quadrant : 32 * quadrant + 4, :, :].bitcast(I32),
-                w4_scales[:, 4 * quadrant : 4 * quadrant + 4, :].rearrange("b r n -> r b n").bitcast(I32),
+                w4s[QUADRANT * quadrant : QUADRANT * quadrant + ROWS, :, :].bitcast(I32),
+                w4_scales[:, ROWS * quadrant : ROWS * (quadrant + 1), :].rearrange("b r n -> r b n").bitcast(I32),
             )
+
+        s_abs(0, 2)
+        s_root(0, 2)
+        for step in (s_abs, s_root):
+            for u in range(1, ON_VECTOR):
+                step(u)
+        for u in range(ON_VECTOR - 1, LAST - 1):
+            s_abs(u + 1)
+            s_square(u)
+            s_root(u + 1)
+            if u >= ON_VECTOR:
+                size_product(u)
+        s_square(LAST - 1, 2)
+        size_product(LAST - 1)
+        for step in (s_abs, s_root, s_square):
+            step(LAST, 2)
+        size_product(LAST)
+
         wd_quant(chunks[0])
-        for k in range(IB):
-            c_finish(k)
-            s_abs(k)
-        for jb in range(JB):
-            x, z = jb * IB, jb * IB + 1
-            ahead = [k for k in (x + IB, z + IB) if k < UNITS]
-            for k in ahead:
-                c_finish(k)
-            s_root(x)
-            s_root(z)
-            for k in ahead[:1]:
-                s_abs(k)
-            s_square(z)
-            for k in ahead[1:]:
-                s_abs(k)
-            size_product(z)
-            size_product(x)
-            if jb == 0:
-                wd_quant(chunks[1])
+        size_product(0)
+        wd_cast(chunks[1], in_turn([P, NW, PACK], BF16))
+        v_product(0, H)
+        wd_quant(chunks[1])
+        v_product(0, G)
+        sums = []
+        for u in range(1, LAST):
+            if u < ON_VECTOR:
+                size_product(u)
+                v_quant(u - 1)
+                v_product(u, H)
             else:
-                v_quant(x - 1)
-            if jb == 1:
-                wd_quant(chunks[3])
-            v_product(x, 0)
-            v_product(x, 1)
-            if jb == 0:
-                wd_cast(chunks[2])
-            else:
-                out_block(jb - 1)
-            v_product(z, 0)
-            v_quant(x)
-            v_product(z, 1)
-            if jb == 0:
-                wd_quant(chunks[2])
-                wd_cast(chunks[3])
-        v_quant(UNITS - 1)
-        last_block()
+                v_product(u, H)
+                v_quant(u - 1)
+            if u + 1 < len(chunks):
+                wd_cast(chunks[u + 1], in_turn([P, NW, PACK], BF16))
+            v_product(u, G)
+            if u + 1 < len(chunks):
+                wd_quant(chunks[u + 1])
+            if u % IB == 0:
+                sums.append(out_sums(u // IB - 1, NT)[0])
+        v_quant(LAST - 1, (H, G))
+        v_product(LAST, G)
+        v_product(LAST, H)
+        for jb, acc in enumerate(sums):
+            res = ring.tile([P, NT, JW], F32, name="res", tag="res", bufs=JB - 1)
+            nc.scalar.copy(res[:], acc[:])
+            nc.sync.dma_start(out_v[:, :, jb * JW : (jb + 1) * JW], res[:])
+        v_quant(LAST, (G, H))
+
+        half_nt = NT // 2
+        accs = out_sums(JB - 1, half_nt)
+        for part, copy, queue in ((0, nc.vector.tensor_copy, nc.sync), (1, nc.scalar.copy, nc.scalar)):
+            res = keep.tile([P, half_nt, JW], F32, name="res_last%d" % part)
+            copy(res[:], accs[part][:, 0:half_nt, :])
+            queue.dma_start(out_v[:, part * half_nt : (part + 1) * half_nt, (JB - 1) * JW : JB * JW], res[:])

@@ -15,6 +15,7 @@ FP8X4 = mybir.dt.float8_e4m3fn_x4
 FP4X4 = mybir.dt.float4_e2m1fn_x4
 ACT = mybir.ActivationFunctionType
 MULT = mybir.AluOpType.mult
+ADD = mybir.AluOpType.add
 
 P = 128
 PACK = 4
@@ -43,8 +44,8 @@ AT_SIZE = AT_TAB2_2 + 4 * T2
 AT_TAB_2 = AT_SIZE + LAP
 AT_DEALT = AT_SIZE - S2
 ON_VECTOR = 3
-SQUARED = 2
-HG_BUFS = 3
+HG_BUFS = UNITS + 1
+POOL_DESKS = 192
 
 
 def tile_list_desk_stress_results_kernel(tc, tab_words, tab_scales, tab2_words, tab2_scales, offs, offs2, size, wd, w4_words, w4_scales, out):
@@ -168,10 +169,10 @@ def tile_list_desk_stress_results_kernel(tc, tab_words, tab_scales, tab2_words, 
         r_t, y_t, w_t, d_t, hg_t, hgw, hgs = {}, {}, {}, {}, {}, {}, {}
 
         def in_turn(shape, dtype):
-            return ring.tile(shape, dtype, name="turn", tag="turn", bufs=UNITS + len(chunks) - 1, align_bytes=64)
+            return ring.tile(shape, dtype, name="turn", tag="turn", bufs=UNITS + 1, align_bytes=64)
 
         def activate(name, src, count, parts, func, **operands):
-            dst = keep.tile([P, count, JW], F32, name=name)
+            dst = keep.tile([P, count, JW], F32, name=name, tag=name, align_bytes=64)
             for lo in range(0, count, count // parts):
                 ts = slice(lo, lo + count // parts)
                 nc.scalar.activation(dst[:, ts, :], src[:, ts, :], func, **operands)
@@ -184,7 +185,7 @@ def tile_list_desk_stress_results_kernel(tc, tab_words, tab_scales, tab2_words, 
             y_t[u] = activate("y%d" % u, r_t[u], PACK, parts, ACT.Abs_reciprocal_sqrt, bias=one[:])
 
         def s_square(u, parts=1):
-            w_t[u] = activate("w%d" % u, y_t[u], SQUARED if u < ON_VECTOR else PACK, parts, ACT.Square)
+            w_t[u] = activate("w%d" % u, y_t[u], PACK, parts, ACT.Square)
 
         def size_product(u):
             d_t[u] = in_turn([P, PACK, JW], F32)
@@ -192,8 +193,6 @@ def tile_list_desk_stress_results_kernel(tc, tab_words, tab_scales, tab2_words, 
                 scale = sz[:, units[u][1], t : t + 1]
                 if u >= ON_VECTOR:
                     nc.scalar.activation(d_t[u][:, t, :], w_t[u][:, t, :], ACT.Copy, scale=scale)
-                elif u == ON_VECTOR - 1 and t < SQUARED:
-                    nc.vector.tensor_scalar(out=d_t[u][:, t, :], in0=w_t[u][:, t, :], scalar1=scale, scalar2=None, op0=MULT)
                 else:
                     nc.vector.scalar_tensor_tensor(
                         out=d_t[u][:, t, :], in0=y_t[u][:, t, :], scalar=scale, in1=y_t[u][:, t, :], op0=MULT, op1=MULT
@@ -222,15 +221,22 @@ def tile_list_desk_stress_results_kernel(tc, tab_words, tab_scales, tab2_words, 
                     cols = slice(half * JW, (half + 1) * JW)
                     nc.vector.quantize_mx(out=hgw[u][:, cols].bitcast(FP8X4), scales=hgs[u][:, cols], in_=hg_t[u][:, half, :])
 
-        def wd_cast(ch, tile):
-            wdbf[ch] = tile
-            nc.vector.tensor_copy(
-                tile[:].rearrange("p (c i) t -> p c t i", i=RUN),
-                by_runs(wdraw[ch[0]][:, :, ch[1] * NW : (ch[1] + 1) * NW]),
-            )
+        def cast_views(ch, lo, hi):
+            src = wdraw[ch[0]][:, :, ch[1] * NW + lo : ch[1] * NW + hi]
+            return wdbf[ch][:, lo:hi, :].rearrange("p (c i) t -> p c t i", i=RUN), by_runs(src)
+
+        def wd_cast(ch, lo, hi):
+            nc.vector.tensor_copy(*cast_views(ch, lo, hi))
+
+        def wd_cast_pool(ch, lo, hi):
+            dst, src = cast_views(ch, lo, hi)
+            nc.gpsimd.tensor_scalar(out=dst, in0=src, scalar1=1.0, scalar2=0.0, op0=MULT, op1=ADD)
 
         def wd_quant(ch):
-            wdw[ch] = keep.tile([P, NW], U32, name="wdw%d_%d" % ch, align_bytes=64)
+            if ch == chunks[-1]:
+                wdw[ch] = ring.tile([P, NW], U32, name="hg", tag="hg", align_bytes=64)
+            else:
+                wdw[ch] = keep.tile([P, NW], U32, name="wdw%d_%d" % ch, align_bytes=64)
             nc.vector.quantize_mx(out=wdw[ch][:].bitcast(FP8X4), scales=wds[ch][:], in_=wdbf[ch][:].rearrange("p n t -> p (n t)"))
 
         def option_pass(dst, nt, u, start):
@@ -259,7 +265,8 @@ def tile_list_desk_stress_results_kernel(tc, tab_words, tab_scales, tab2_words, 
                     linear_pass(accs[nt // per_bank][:, nt % per_bank, :], nt, jb * IB + b, b == IB - 1 and nt % per_bank == per_bank - 1)
             return accs
 
-        wd_cast(chunks[0], keep.tile([P, NW, PACK], BF16, name="wdbf0", align_bytes=64))
+        wdbf[chunks[0]] = keep.tile([P, NW, PACK], BF16, name="wdbf0", align_bytes=64)
+        wd_cast(chunks[0], 0, NW)
         for u in range(UNITS):
             c_pass(u, KP - 1)
         w4s = late[:, 0 : IB * N].rearrange("p (b n) -> p b n", b=IB)
@@ -271,43 +278,59 @@ def tile_list_desk_stress_results_kernel(tc, tab_words, tab_scales, tab2_words, 
 
         s_abs(0, 2)
         s_root(0, 2)
-        for step in (s_abs, s_root):
-            for u in range(1, ON_VECTOR):
-                step(u)
-        for u in range(ON_VECTOR - 1, LAST - 1):
-            s_abs(u + 1)
-            s_square(u)
-            s_root(u + 1)
-            if u >= ON_VECTOR:
-                size_product(u)
-        s_square(LAST - 1, 2)
-        size_product(LAST - 1)
-        for step in (s_abs, s_root, s_square):
-            step(LAST, 2)
-        size_product(LAST)
+        s_abs(1)
+        s_abs(2)
+        s_root(1)
+        s_abs(3)
+        s_root(2)
+        s_root(3, 2)
+        s_square(3, 2)
+        size_product(3)
+        for step in (s_abs, s_root, s_square, size_product):
+            step(4)
+            step(5)
+        s_abs(6)
+        s_abs(7)
+        for u in (6, 7):
+            s_root(u, 2)
+            s_square(u, 2)
+            size_product(u)
 
         wd_quant(chunks[0])
         size_product(0)
-        wd_cast(chunks[1], in_turn([P, NW, PACK], BF16))
+        wdbf[chunks[1]] = in_turn([P, NW, PACK], BF16)
+        wd_cast(chunks[1], 0, NW)
         v_product(0, H)
         wd_quant(chunks[1])
         v_product(0, G)
-        sums = []
-        for u in range(1, LAST):
-            if u < ON_VECTOR:
-                size_product(u)
-                v_quant(u - 1)
-                v_product(u, H)
-            else:
-                v_product(u, H)
-                v_quant(u - 1)
-            if u + 1 < len(chunks):
-                wd_cast(chunks[u + 1], in_turn([P, NW, PACK], BF16))
-            v_product(u, G)
-            if u + 1 < len(chunks):
-                wd_quant(chunks[u + 1])
-            if u % IB == 0:
-                sums.append(out_sums(u // IB - 1, NT)[0])
+        size_product(1)
+        v_quant(0)
+        size_product(2)
+        wdbf[chunks[2]] = keep.tile([P, NW, PACK], BF16, name="wdbf2", tag="y2", align_bytes=64)
+        wd_cast_pool(chunks[2], 0, NW)
+        for u in (1, 2, 3):
+            v_product(u, H)
+        v_product(1, G)
+        v_product(2, G)
+        v_quant(1)
+        v_quant(2)
+        v_product(3, G)
+        wdbf[chunks[3]] = keep.tile([P, NW, PACK], BF16, name="wdbf3", tag="r3", align_bytes=64)
+        wd_cast_pool(chunks[3], 0, POOL_DESKS)
+        v_product(4, H)
+        v_product(5, H)
+        v_quant(3)
+        wd_quant(chunks[2])
+        wd_cast(chunks[3], POOL_DESKS, NW)
+        v_product(4, G)
+        v_product(5, G)
+        v_quant(4)
+        wd_quant(chunks[3])
+        sums = [out_sums(jb, NT)[0] for jb in range(2)]
+        v_product(6, H)
+        v_quant(5)
+        v_product(6, G)
+        sums.append(out_sums(2, NT)[0])
         v_quant(LAST - 1, (H, G))
         v_product(LAST, G)
         v_product(LAST, H)

@@ -45,7 +45,7 @@ AT_TAB_2 = AT_SIZE + LAP
 AT_DEALT = AT_SIZE - S2
 ON_VECTOR = 3
 HG_BUFS = UNITS + 1
-POOL_DESKS = 192
+POOL_DESKS = 128
 
 
 def tile_list_desk_stress_results_kernel(tc, tab_words, tab_scales, tab2_words, tab2_scales, offs, offs2, size, wd, w4_words, w4_scales, out):
@@ -313,14 +313,14 @@ def tile_list_desk_stress_results_kernel(tc, tab_words, tab_scales, tab2_words, 
         v_product(1, G)
         v_product(2, G)
         v_quant(1)
-        v_quant(2)
         v_product(3, G)
-        wdbf[chunks[3]] = keep.tile([P, NW, PACK], BF16, name="wdbf3", tag="r3", align_bytes=64)
+        v_quant(2)
+        v_quant(3)
+        wd_quant(chunks[2])
+        wdbf[chunks[3]] = keep.tile([P, NW, PACK], BF16, name="wdbf3", tag="y2", align_bytes=64)
         wd_cast_pool(chunks[3], 0, POOL_DESKS)
         v_product(4, H)
         v_product(5, H)
-        v_quant(3)
-        wd_quant(chunks[2])
         wd_cast(chunks[3], POOL_DESKS, NW)
         v_product(4, G)
         v_product(5, G)

@@ -44,8 +44,9 @@ AT_SIZE = AT_TAB2_2 + 4 * T2
 AT_TAB_2 = AT_SIZE + LAP
 AT_DEALT = AT_SIZE - S2
 ON_VECTOR = 3
+SQUARED = 4
 HG_BUFS = UNITS + 1
-POOL_DESKS = 128
+POOL_DESKS = 192
 
 
 def tile_list_desk_stress_results_kernel(tc, tab_words, tab_scales, tab2_words, tab2_scales, offs, offs2, size, wd, w4_words, w4_scales, out):
@@ -129,16 +130,17 @@ def tile_list_desk_stress_results_kernel(tc, tab_words, tab_scales, tab2_words, 
         for row in range(ROWS):
             src = PASS2_ROW + row * ROW_STEP
             place_rows(KP - 1, row, staged[src : src + 3 * ROWS * ROW_STEP + 1 : ROWS * ROW_STEP, :])
-        sz = laid.tile([P, IB, PACK], F32, name="sz", offset=AT_SIZE)
-        nc.sync.dma_start(sz[:], size.rearrange("(b p t) -> p b t", b=IB, t=PACK))
         gather_v(0)
         gather_v2(1, 0, S2)
         gather_v(1)
         gather_v(2)
         for b in range(IB):
-            wdraw[b] = laid.tile([P, PACK, N], F32, name="wdraw%d" % b, offset=AT_TAB_1 + b * 4 * PACK * N)
+            wdraw[b] = laid.tile([P, PACK, N], F32, name="wdraw%d" % b, offset=AT_TAB_1 - LAP + b * 4 * PACK * N)
             for lo in range(0, N, NW):
                 nc.sync.dma_start(wdraw[b][:, :, lo : lo + NW], wd[b * PASS : (b + 1) * PASS, lo : lo + NW].rearrange("(p t) n -> p t n", t=PACK))
+                if (b, lo) == (0, 0):
+                    sz = laid.tile([P, IB, PACK], F32, name="sz", offset=AT_TAB_1 + 4 * T - LAP)
+                    nc.sync.dma_start(sz[:], size.rearrange("(b p t) -> p b t", b=IB, t=PACK))
 
         units = [(jb, b) for jb in range(JB) for b in range(IB)]
 
@@ -191,7 +193,9 @@ def tile_list_desk_stress_results_kernel(tc, tab_words, tab_scales, tab2_words, 
             d_t[u] = in_turn([P, PACK, JW], F32)
             for t in range(PACK):
                 scale = sz[:, units[u][1], t : t + 1]
-                if u >= ON_VECTOR:
+                if u == SQUARED:
+                    nc.vector.tensor_scalar(out=d_t[u][:, t, :], in0=w_t[u][:, t, :], scalar1=scale, scalar2=None, op0=MULT)
+                elif u >= ON_VECTOR:
                     nc.scalar.activation(d_t[u][:, t, :], w_t[u][:, t, :], ACT.Copy, scale=scale)
                 else:
                     nc.vector.scalar_tensor_tensor(
@@ -286,15 +290,18 @@ def tile_list_desk_stress_results_kernel(tc, tab_words, tab_scales, tab2_words, 
         s_root(3, 2)
         s_square(3, 2)
         size_product(3)
-        for step in (s_abs, s_root, s_square, size_product):
+        for step in (s_abs, s_root, s_square):
             step(4)
             step(5)
         s_abs(6)
+        size_product(5)
+        s_root(6)
         s_abs(7)
-        for u in (6, 7):
-            s_root(u, 2)
-            s_square(u, 2)
-            size_product(u)
+        s_square(6)
+        s_root(7)
+        size_product(6)
+        s_square(7, 2)
+        size_product(7)
 
         wd_quant(chunks[0])
         size_product(0)
@@ -315,6 +322,7 @@ def tile_list_desk_stress_results_kernel(tc, tab_words, tab_scales, tab2_words, 
         v_quant(1)
         v_product(3, G)
         v_quant(2)
+        size_product(4)
         v_quant(3)
         wd_quant(chunks[2])
         wdbf[chunks[3]] = keep.tile([P, NW, PACK], BF16, name="wdbf3", tag="y2", align_bytes=64)

@@ -39,13 +39,15 @@ LAP = 64
 AT_TAB2_1 = 0
 AT_TAB2_0 = 4 * T2 - LAP
 AT_TAB_1 = 8 * T2 - 2 * LAP
+AT_WD = AT_TAB_1 - LAP
+AT_SIZE = AT_WD + 4 * T
 AT_TAB2_2 = 4 * (2 * T2 + T)
-AT_SIZE = AT_TAB2_2 + 4 * T2
-AT_TAB_2 = AT_SIZE + LAP
-AT_DEALT = AT_SIZE - S2
+AT_TAB_2 = AT_TAB2_2 + 4 * T2 + LAP
+AT_DEALT = AT_TAB2_2 + 4 * T2 - S2
 ON_VECTOR = 3
-SQUARED = 4
-HG_BUFS = UNITS + 1
+SHARED = 4
+FIRST_RUN = (1, 2, 3)
+SECOND_RUN = (4, 5)
 POOL_DESKS = 192
 
 
@@ -54,7 +56,7 @@ def tile_list_desk_stress_results_kernel(tc, tab_words, tab_scales, tab2_words, 
     with ExitStack() as ctx:
         keep = ctx.enter_context(tc.tile_pool(name="keep", bufs=1))
         laid = ctx.enter_context(tc.tile_pool(name="laid", bufs=1))
-        ring = ctx.enter_context(tc.tile_pool(name="ring", bufs=HG_BUFS))
+        ring = ctx.enter_context(tc.tile_pool(name="ring", bufs=UNITS + 1))
         psum = ctx.enter_context(tc.psum_pool(name="psum", bufs=UNITS))
 
         idx = keep.tile([P, S // LIST_ROWS], U16, name="idx")
@@ -135,11 +137,11 @@ def tile_list_desk_stress_results_kernel(tc, tab_words, tab_scales, tab2_words, 
         gather_v(1)
         gather_v(2)
         for b in range(IB):
-            wdraw[b] = laid.tile([P, PACK, N], F32, name="wdraw%d" % b, offset=AT_TAB_1 - LAP + b * 4 * PACK * N)
+            wdraw[b] = laid.tile([P, PACK, N], F32, name="wdraw%d" % b, offset=AT_WD + b * 4 * PACK * N)
             for lo in range(0, N, NW):
                 nc.sync.dma_start(wdraw[b][:, :, lo : lo + NW], wd[b * PASS : (b + 1) * PASS, lo : lo + NW].rearrange("(p t) n -> p t n", t=PACK))
                 if (b, lo) == (0, 0):
-                    sz = laid.tile([P, IB, PACK], F32, name="sz", offset=AT_TAB_1 + 4 * T - LAP)
+                    sz = laid.tile([P, IB, PACK], F32, name="sz", offset=AT_SIZE)
                     nc.sync.dma_start(sz[:], size.rearrange("(b p t) -> p b t", b=IB, t=PACK))
 
         units = [(jb, b) for jb in range(JB) for b in range(IB)]
@@ -171,29 +173,29 @@ def tile_list_desk_stress_results_kernel(tc, tab_words, tab_scales, tab2_words, 
         r_t, y_t, w_t, d_t, hg_t, hgw, hgs = {}, {}, {}, {}, {}, {}, {}
 
         def in_turn(shape, dtype):
-            return ring.tile(shape, dtype, name="turn", tag="turn", bufs=UNITS + 1, align_bytes=64)
+            return ring.tile(shape, dtype, name="turn", tag="turn", align_bytes=64)
 
-        def activate(name, src, count, parts, func, **operands):
-            dst = keep.tile([P, count, JW], F32, name=name, tag=name, align_bytes=64)
-            for lo in range(0, count, count // parts):
-                ts = slice(lo, lo + count // parts)
+        def activate(name, src, parts, func, **operands):
+            dst = keep.tile([P, PACK, JW], F32, name=name, tag=name, align_bytes=64)
+            for lo in range(0, PACK, PACK // parts):
+                ts = slice(lo, lo + PACK // parts)
                 nc.scalar.activation(dst[:, ts, :], src[:, ts, :], func, **operands)
             return dst
 
         def s_abs(u, parts=1):
-            r_t[u] = activate("r%d" % u, banks[u], PACK, parts, ACT.Abs)
+            r_t[u] = activate("r%d" % u, banks[u], parts, ACT.Abs)
 
         def s_root(u, parts=1):
-            y_t[u] = activate("y%d" % u, r_t[u], PACK, parts, ACT.Abs_reciprocal_sqrt, bias=one[:])
+            y_t[u] = activate("y%d" % u, r_t[u], parts, ACT.Abs_reciprocal_sqrt, bias=one[:])
 
         def s_square(u, parts=1):
-            w_t[u] = activate("w%d" % u, y_t[u], PACK, parts, ACT.Square)
+            w_t[u] = activate("w%d" % u, y_t[u], parts, ACT.Square)
 
         def size_product(u):
             d_t[u] = in_turn([P, PACK, JW], F32)
             for t in range(PACK):
                 scale = sz[:, units[u][1], t : t + 1]
-                if u == SQUARED:
+                if u == SHARED:
                     nc.vector.tensor_scalar(out=d_t[u][:, t, :], in0=w_t[u][:, t, :], scalar1=scale, scalar2=None, op0=MULT)
                 elif u >= ON_VECTOR:
                     nc.scalar.activation(d_t[u][:, t, :], w_t[u][:, t, :], ACT.Copy, scale=scale)
@@ -283,25 +285,18 @@ def tile_list_desk_stress_results_kernel(tc, tab_words, tab_scales, tab2_words, 
         s_abs(0, 2)
         s_root(0, 2)
         s_abs(1)
-        s_abs(2)
-        s_root(1)
-        s_abs(3)
-        s_root(2)
-        s_root(3, 2)
-        s_square(3, 2)
-        size_product(3)
-        for step in (s_abs, s_root, s_square):
-            step(4)
-            step(5)
-        s_abs(6)
-        size_product(5)
-        s_root(6)
-        s_abs(7)
-        s_square(6)
-        s_root(7)
-        size_product(6)
-        s_square(7, 2)
-        size_product(7)
+        for u in range(1, ON_VECTOR):
+            s_abs(u + 1)
+            s_root(u)
+        s_root(ON_VECTOR)
+        for u in range(ON_VECTOR, LAST):
+            s_abs(u + 1)
+            s_square(u)
+            s_root(u + 1)
+            if u != SHARED:
+                size_product(u)
+        s_square(LAST, 2)
+        size_product(LAST)
 
         wd_quant(chunks[0])
         size_product(0)
@@ -313,30 +308,29 @@ def tile_list_desk_stress_results_kernel(tc, tab_words, tab_scales, tab2_words, 
         size_product(1)
         v_quant(0)
         size_product(2)
-        wdbf[chunks[2]] = keep.tile([P, NW, PACK], BF16, name="wdbf2", tag="y2", align_bytes=64)
-        wd_cast_pool(chunks[2], 0, NW)
-        for u in (1, 2, 3):
-            v_product(u, H)
         v_product(1, G)
-        v_product(2, G)
-        v_quant(1)
-        v_product(3, G)
-        v_quant(2)
-        size_product(4)
+        wdbf[chunks[2]] = keep.tile([P, NW, PACK], BF16, name="wdbf2", tag="r1", align_bytes=64)
+        wd_cast_pool(chunks[2], 0, NW)
+        for u in FIRST_RUN:
+            v_product(u, H)
+        for u in FIRST_RUN[1:]:
+            v_product(u, G)
+            v_quant(u - 1)
+        size_product(SHARED)
         v_quant(3)
-        wd_quant(chunks[2])
-        wdbf[chunks[3]] = keep.tile([P, NW, PACK], BF16, name="wdbf3", tag="y2", align_bytes=64)
-        wd_cast_pool(chunks[3], 0, POOL_DESKS)
-        v_product(4, H)
-        v_product(5, H)
-        wd_cast(chunks[3], POOL_DESKS, NW)
         v_product(4, G)
+        wd_quant(chunks[2])
+        wdbf[chunks[3]] = keep.tile([P, NW, PACK], BF16, name="wdbf3", tag="r1", align_bytes=64)
+        wd_cast_pool(chunks[3], 0, POOL_DESKS)
+        for u in SECOND_RUN:
+            v_product(u, H)
+        wd_cast(chunks[3], POOL_DESKS, NW)
         v_product(5, G)
-        v_quant(4)
+        for u in SECOND_RUN:
+            v_quant(u)
         wd_quant(chunks[3])
         sums = [out_sums(jb, NT)[0] for jb in range(2)]
         v_product(6, H)
-        v_quant(5)
         v_product(6, G)
         sums.append(out_sums(2, NT)[0])
         v_quant(LAST - 1, (H, G))

@@ -308,9 +308,9 @@ def tile_list_desk_stress_results_kernel(tc, tab_words, tab_scales, tab2_words, 
         size_product(1)
         v_quant(0)
         size_product(2)
-        v_product(1, G)
-        wdbf[chunks[2]] = keep.tile([P, NW, PACK], BF16, name="wdbf2", tag="r1", align_bytes=64)
+        wdbf[chunks[2]] = keep.tile([P, NW, PACK], BF16, name="wdbf2", tag="y2", align_bytes=64)
         wd_cast_pool(chunks[2], 0, NW)
+        v_product(1, G)
         for u in FIRST_RUN:
             v_product(u, H)
         for u in FIRST_RUN[1:]:
@@ -318,10 +318,10 @@ def tile_list_desk_stress_results_kernel(tc, tab_words, tab_scales, tab2_words, 
             v_quant(u - 1)
         size_product(SHARED)
         v_quant(3)
-        v_product(4, G)
         wd_quant(chunks[2])
-        wdbf[chunks[3]] = keep.tile([P, NW, PACK], BF16, name="wdbf3", tag="r1", align_bytes=64)
+        wdbf[chunks[3]] = keep.tile([P, NW, PACK], BF16, name="wdbf3", tag="y2", align_bytes=64)
         wd_cast_pool(chunks[3], 0, POOL_DESKS)
+        v_product(4, G)
         for u in SECOND_RUN:
             v_product(u, H)
         wd_cast(chunks[3], POOL_DESKS, NW)

@@ -44,11 +44,9 @@ AT_SIZE = AT_WD + 4 * T
 AT_TAB2_2 = 4 * (2 * T2 + T)
 AT_TAB_2 = AT_TAB2_2 + 4 * T2 + LAP
 AT_DEALT = AT_TAB2_2 + 4 * T2 - S2
-ON_VECTOR = 3
-SHARED = 4
-FIRST_RUN = (1, 2, 3)
-SECOND_RUN = (4, 5)
-POOL_DESKS = 192
+FUSED, SCALED, ON_SCALAR = 0, 1, 2
+OWN_DESKS = 64
+TURNS = 30
 
 
 def tile_list_desk_stress_results_kernel(tc, tab_words, tab_scales, tab2_words, tab2_scales, offs, offs2, size, wd, w4_words, w4_scales, out):
@@ -56,7 +54,7 @@ def tile_list_desk_stress_results_kernel(tc, tab_words, tab_scales, tab2_words, 
     with ExitStack() as ctx:
         keep = ctx.enter_context(tc.tile_pool(name="keep", bufs=1))
         laid = ctx.enter_context(tc.tile_pool(name="laid", bufs=1))
-        ring = ctx.enter_context(tc.tile_pool(name="ring", bufs=UNITS + 1))
+        ring = ctx.enter_context(tc.tile_pool(name="ring", bufs=TURNS))
         psum = ctx.enter_context(tc.psum_pool(name="psum", bufs=UNITS))
 
         idx = keep.tile([P, S // LIST_ROWS], U16, name="idx")
@@ -69,9 +67,9 @@ def tile_list_desk_stress_results_kernel(tc, tab_words, tab_scales, tab2_words, 
         early = keep.tile([P, S + S2], U8, name="early", align_bytes=64)
         late = keep.tile([P, S + S2], U8, name="late", align_bytes=64)
         planes = [early, early, late]
-        chunks = [(b, u) for b in range(IB) for u in range(N // NW)]
+        chunks = [(b, half) for b in range(IB) for half in range(N // NW)]
         wds = {ch: keep.tile([P, NW], U8, name="wds%d_%d" % ch, align_bytes=64) for ch in chunks}
-        tabw, tab2w, vw, v2w, wdraw, wdbf, wdw = {}, {}, {}, {}, {}, {}, {}
+        tabw, tab2w, vw, v2w, wdraw, wdw = {}, {}, {}, {}, {}, {}
         one_in = keep.tile([P, 1], F32, name="one_in", tag="tabw0", align_bytes=64)
         one = keep.tile([P, 1], F32, name="one")
 
@@ -136,15 +134,19 @@ def tile_list_desk_stress_results_kernel(tc, tab_words, tab_scales, tab2_words, 
         gather_v2(1, 0, S2)
         gather_v(1)
         gather_v(2)
+
+        def wd_rows(b):
+            return wd[b * PASS : (b + 1) * PASS, :].rearrange("(p t) n -> p t n", t=PACK)
+
         for b in range(IB):
             wdraw[b] = laid.tile([P, PACK, N], F32, name="wdraw%d" % b, offset=AT_WD + b * 4 * PACK * N)
-            for lo in range(0, N, NW):
-                nc.sync.dma_start(wdraw[b][:, :, lo : lo + NW], wd[b * PASS : (b + 1) * PASS, lo : lo + NW].rearrange("(p t) n -> p t n", t=PACK))
-                if (b, lo) == (0, 0):
-                    sz = laid.tile([P, IB, PACK], F32, name="sz", offset=AT_SIZE)
-                    nc.sync.dma_start(sz[:], size.rearrange("(b p t) -> p b t", b=IB, t=PACK))
+        nc.sync.dma_start(wdraw[0][:, :, :NW], wd_rows(0)[:, :, :NW])
+        sz = laid.tile([P, IB, PACK], F32, name="sz", offset=AT_SIZE)
+        nc.sync.dma_start(sz[:], size.rearrange("(b p t) -> p b t", b=IB, t=PACK))
+        nc.sync.dma_start(wdraw[0][:, :, NW:], wd_rows(0)[:, :, NW:])
+        nc.sync.dma_start(wdraw[1][:], wd_rows(1))
 
-        units = [(jb, b) for jb in range(JB) for b in range(IB)]
+        units = [(0, 0), (0, 1), (1, 0), (2, 0), (1, 1), (2, 1), (3, 1), (3, 0)]
 
         def c_pass(u, a):
             jb, b = units[u]
@@ -165,8 +167,8 @@ def tile_list_desk_stress_results_kernel(tc, tab_words, tab_scales, tab2_words, 
             for u in range(UNITS):
                 c_pass(u, a)
 
-        gather_v2(KP - 1, 0, S2 // 2)
-        gather_v2(KP - 1, S2 // 2, S2)
+        gather_v2(KP - 1, 0, JW)
+        gather_v2(KP - 1, JW, S2)
         w4w = laid.tile([P, IB, 2 * N], U8, name="w4w", offset=AT_TAB2_2, align_bytes=64)
         nc.sync.dma_start(w4w[:].bitcast(I32), w4_words.rearrange("b p e -> p b e").bitcast(I32))
 
@@ -175,51 +177,65 @@ def tile_list_desk_stress_results_kernel(tc, tab_words, tab_scales, tab2_words, 
         def in_turn(shape, dtype):
             return ring.tile(shape, dtype, name="turn", tag="turn", align_bytes=64)
 
-        def activate(name, src, parts, func, **operands):
-            dst = keep.tile([P, PACK, JW], F32, name=name, tag=name, align_bytes=64)
-            for lo in range(0, PACK, PACK // parts):
-                ts = slice(lo, lo + PACK // parts)
-                nc.scalar.activation(dst[:, ts, :], src[:, ts, :], func, **operands)
-            return dst
+        def wide(name, us):
+            return keep.tile([P, PACK, len(us) * JW], F32, name=name, tag=name, align_bytes=64)
 
-        def s_abs(u, parts=1):
-            r_t[u] = activate("r%d" % u, banks[u], parts, ACT.Abs)
+        def activate(dst, src, parts, func, ts=range(PACK), **operands):
+            step = len(ts) // parts
+            for lo in range(ts[0], ts[-1] + 1, step):
+                nc.scalar.activation(dst[:, lo : lo + step, :], src[:, lo : lo + step, :], func, **operands)
 
-        def s_root(u, parts=1):
-            y_t[u] = activate("y%d" % u, r_t[u], parts, ACT.Abs_reciprocal_sqrt, bias=one[:])
+        def s_abs(us, u, parts=1):
+            if us not in r_t:
+                r_t[us] = wide("r%d" % us[0], us)
+            lo = us.index(u) * JW
+            activate(r_t[us][:, :, lo : lo + JW], banks[u], parts, ACT.Abs)
 
-        def s_square(u, parts=1):
-            w_t[u] = activate("w%d" % u, y_t[u], parts, ACT.Square)
+        def s_root(us, parts=1):
+            y_t[us] = wide("y%d" % us[0], us)
+            activate(y_t[us], r_t[us], parts, ACT.Abs_reciprocal_sqrt, bias=one[:])
 
-        def size_product(u):
-            d_t[u] = in_turn([P, PACK, JW], F32)
-            for t in range(PACK):
-                scale = sz[:, units[u][1], t : t + 1]
-                if u == SHARED:
-                    nc.vector.tensor_scalar(out=d_t[u][:, t, :], in0=w_t[u][:, t, :], scalar1=scale, scalar2=None, op0=MULT)
-                elif u >= ON_VECTOR:
-                    nc.scalar.activation(d_t[u][:, t, :], w_t[u][:, t, :], ACT.Copy, scale=scale)
+        def s_square(us, parts=1, ts=range(PACK)):
+            w_t[us] = wide("w%d" % us[0], us)
+            activate(w_t[us], y_t[us], parts, ACT.Square, ts)
+
+        def size_product(us, how, ts=range(PACK)):
+            if len(us) > 1 and us not in d_t:
+                d_t[us] = wide("r0", us)
+            if us not in d_t:
+                d_t[us] = in_turn([P, PACK, len(us) * JW], F32)
+            for t in ts:
+                scale = sz[:, units[us[0]][1], t : t + 1]
+                if how == SCALED:
+                    nc.vector.tensor_scalar(out=d_t[us][:, t, :], in0=w_t[us][:, t, :], scalar1=scale, scalar2=None, op0=MULT)
+                elif how == ON_SCALAR:
+                    nc.scalar.activation(d_t[us][:, t, :], w_t[us][:, t, :], ACT.Copy, scale=scale)
                 else:
                     nc.vector.scalar_tensor_tensor(
-                        out=d_t[u][:, t, :], in0=y_t[u][:, t, :], scalar=scale, in1=y_t[u][:, t, :], op0=MULT, op1=MULT
+                        out=d_t[us][:, t, :], in0=y_t[us][:, t, :], scalar=scale, in1=y_t[us][:, t, :], op0=MULT, op1=MULT
                     )
+
+        def of_unit(tiles, u):
+            us = [us for us in tiles if u in us][0]
+            lo = us.index(u) * JW
+            return tiles[us][:, :, lo : lo + JW]
 
         def by_runs(src):
             return src.rearrange("p t (c i) -> p c t i", i=RUN)
 
         def v_product(u, half):
             if u not in hg_t:
-                hg_t[u] = ring.tile([P, 2, JW * PACK], BF16, name="hg", tag="hg", align_bytes=64)
+                hg_t[u] = in_turn([P, 2, JW * PACK], BF16)
             nc.vector.tensor_tensor(
                 hg_t[u][:, half, :].rearrange("p (c i t) -> p c t i", i=RUN, t=PACK),
-                by_runs((banks[u], r_t[u])[half][:]),
-                by_runs(d_t[u][:]),
+                by_runs(banks[u][:] if half == H else of_unit(r_t, u)),
+                by_runs(of_unit(d_t, u)),
                 MULT,
             )
 
         def v_quant(u, halves=None):
-            hgw[u] = ring.tile([P, 2 * JW], U32, name="hgw", tag="hgw", bufs=UNITS, align_bytes=64)
-            hgs[u] = ring.tile([P, 2 * JW], U8, name="hgs", tag="hgs", bufs=UNITS, align_bytes=64)
+            hgw[u] = in_turn([P, 2 * JW], U32)
+            hgs[u] = keep.tile([P, 2 * JW], U8, name="hgs%d" % u, align_bytes=64)
             if halves is None:
                 nc.vector.quantize_mx(out=hgw[u][:].bitcast(FP8X4), scales=hgs[u][:], in_=hg_t[u][:].rearrange("p w c -> p (w c)"))
             else:
@@ -227,23 +243,21 @@ def tile_list_desk_stress_results_kernel(tc, tab_words, tab_scales, tab2_words, 
                     cols = slice(half * JW, (half + 1) * JW)
                     nc.vector.quantize_mx(out=hgw[u][:, cols].bitcast(FP8X4), scales=hgs[u][:, cols], in_=hg_t[u][:, half, :])
 
-        def cast_views(ch, lo, hi):
+        def cast_views(dst, ch, lo, hi):
             src = wdraw[ch[0]][:, :, ch[1] * NW + lo : ch[1] * NW + hi]
-            return wdbf[ch][:, lo:hi, :].rearrange("p (c i) t -> p c t i", i=RUN), by_runs(src)
+            return dst.rearrange("p (c i) t -> p c t i", i=RUN), by_runs(src)
 
-        def wd_cast(ch, lo, hi):
-            nc.vector.tensor_copy(*cast_views(ch, lo, hi))
+        def wd_cast(dst, ch, lo, hi):
+            nc.vector.tensor_copy(*cast_views(dst, ch, lo, hi))
 
-        def wd_cast_pool(ch, lo, hi):
-            dst, src = cast_views(ch, lo, hi)
+        def wd_cast_pool(dst, ch, lo, hi):
+            dst, src = cast_views(dst, ch, lo, hi)
             nc.gpsimd.tensor_scalar(out=dst, in0=src, scalar1=1.0, scalar2=0.0, op0=MULT, op1=ADD)
 
-        def wd_quant(ch):
-            if ch == chunks[-1]:
-                wdw[ch] = ring.tile([P, NW], U32, name="hg", tag="hg", align_bytes=64)
-            else:
-                wdw[ch] = keep.tile([P, NW], U32, name="wdw%d_%d" % ch, align_bytes=64)
-            nc.vector.quantize_mx(out=wdw[ch][:].bitcast(FP8X4), scales=wds[ch][:], in_=wdbf[ch][:].rearrange("p n t -> p (n t)"))
+        def wd_quant(ch, src, lo, hi):
+            if ch not in wdw:
+                wdw[ch] = in_turn([P, NW], U32)
+            nc.vector.quantize_mx(out=wdw[ch][:, lo:hi].bitcast(FP8X4), scales=wds[ch][:, lo:hi], in_=src.rearrange("p n t -> p (n t)"))
 
         def option_pass(dst, nt, u, start):
             b = units[u][1]
@@ -261,18 +275,31 @@ def tile_list_desk_stress_results_kernel(tc, tab_words, tab_scales, tab2_words, 
             )
 
         out_v = out.rearrange("(nt p) j -> p nt j", p=P)
+        half_nt = NT // 2
 
-        def out_sums(jb, per_bank):
-            accs = [psum.tile([P, NT, JW], F32, name="bank", tag="bank") for part in range(NT // per_bank)]
-            for b in range(IB):
-                for nt in range(NT):
-                    option_pass(accs[nt // per_bank][:, nt % per_bank, :], nt, jb * IB + b, b == 0 and nt % per_bank == 0)
-                for nt in range(NT):
-                    linear_pass(accs[nt // per_bank][:, nt % per_bank, :], nt, jb * IB + b, b == IB - 1 and nt % per_bank == per_bank - 1)
-            return accs
+        def out_sum(half, jbs, linear_last):
+            acc = psum.tile([P, half_nt, 2 * JW], F32, name="bank", tag="bank")
+            steps = [(u, kind) for u in range(UNITS) if units[u][0] in jbs for kind in (G, H)]
+            if linear_last:
+                steps = [s for s in steps if s[1] == G or units[s[0]][1] == 0] + [s for s in steps if s[1] == H and units[s[0]][1] == 1]
+            for k, (u, kind) in enumerate(steps):
+                for n in range(half_nt):
+                    lo = (units[u][0] - jbs[0]) * JW
+                    dst = acc[:, n, lo : lo + JW]
+                    if kind == G:
+                        option_pass(dst, half * half_nt + n, u, k == 0 and n == 0)
+                    else:
+                        linear_pass(dst, half * half_nt + n, u, k == len(steps) - 1 and n == half_nt - 1)
+            return acc
 
-        wdbf[chunks[0]] = keep.tile([P, NW, PACK], BF16, name="wdbf0", align_bytes=64)
-        wd_cast(chunks[0], 0, NW)
+        def store(acc, half, jbs, copy, queue):
+            width = len(jbs) * JW
+            res = keep.tile([P, half_nt, width], F32, name="res%d_%d" % (half, jbs[0]))
+            copy(res[:], acc[:, :, :width])
+            queue.dma_start(out_v[:, half * half_nt : (half + 1) * half_nt, jbs[0] * JW : jbs[0] * JW + width], res[:])
+
+        bf0 = keep.tile([P, NW, PACK], BF16, name="bf0", align_bytes=64)
+        wd_cast(bf0[:], chunks[0], 0, NW)
         for u in range(UNITS):
             c_pass(u, KP - 1)
         w4s = late[:, 0 : IB * N].rearrange("p (b n) -> p b n", b=IB)
@@ -282,69 +309,83 @@ def tile_list_desk_stress_results_kernel(tc, tab_words, tab_scales, tab2_words, 
                 w4_scales[:, ROWS * quadrant : ROWS * (quadrant + 1), :].rearrange("b r n -> r b n").bitcast(I32),
             )
 
-        s_abs(0, 2)
-        s_root(0, 2)
-        s_abs(1)
-        for u in range(1, ON_VECTOR):
-            s_abs(u + 1)
-            s_root(u)
-        s_root(ON_VECTOR)
-        for u in range(ON_VECTOR, LAST):
-            s_abs(u + 1)
-            s_square(u)
-            s_root(u + 1)
-            if u != SHARED:
-                size_product(u)
-        s_square(LAST, 2)
-        size_product(LAST)
+        pair = (2, 3)
+        low, high = range(0, PACK // 2), range(PACK // 2, PACK)
+        for u in (0, 1):
+            s_abs((u,), u, 2)
+            s_root((u,), 2)
+        s_abs(pair, 2)
+        s_abs(pair, 3)
+        s_abs((4,), 4)
+        s_root(pair)
+        s_root((4,))
+        s_square(pair, 1, high)
+        s_square((4,))
+        s_abs((5,), 5)
+        size_product((4,), ON_SCALAR)
+        s_root((5,))
+        s_abs((6,), 6)
+        s_square((5,))
+        s_root((6,))
+        size_product((5,), ON_SCALAR)
+        s_square((6,))
+        s_abs((7,), 7)
+        size_product((6,), ON_SCALAR)
+        s_root((7,), 2)
+        s_square((7,), 2)
+        size_product((7,), ON_SCALAR)
 
-        wd_quant(chunks[0])
-        size_product(0)
-        wdbf[chunks[1]] = in_turn([P, NW, PACK], BF16)
-        wd_cast(chunks[1], 0, NW)
-        v_product(0, H)
-        wd_quant(chunks[1])
+        pool_desks = NW - OWN_DESKS
+        size_product((0,), FUSED, low)
+        wd_quant(chunks[0], bf0[:], 0, NW)
+        size_product((0,), FUSED, high)
+        bf1_own = in_turn([P, OWN_DESKS, PACK], BF16)
+        wd_cast(bf1_own[:], chunks[1], 0, OWN_DESKS)
+        size_product((1,), FUSED)
+        bf1_pool = keep.tile([P, pool_desks, PACK], BF16, name="bf1_pool", tag="y1", align_bytes=64)
+        wd_cast_pool(bf1_pool[:], chunks[1], OWN_DESKS, NW)
         v_product(0, G)
-        size_product(1)
-        v_quant(0)
-        size_product(2)
-        wdbf[chunks[2]] = keep.tile([P, NW, PACK], BF16, name="wdbf2", tag="y2", align_bytes=64)
-        wd_cast_pool(chunks[2], 0, NW)
+        v_product(1, H)
+        v_product(0, H)
         v_product(1, G)
-        for u in FIRST_RUN:
-            v_product(u, H)
-        for u in FIRST_RUN[1:]:
-            v_product(u, G)
-            v_quant(u - 1)
-        size_product(SHARED)
-        v_quant(3)
-        wd_quant(chunks[2])
-        wdbf[chunks[3]] = keep.tile([P, NW, PACK], BF16, name="wdbf3", tag="y2", align_bytes=64)
-        wd_cast_pool(chunks[3], 0, POOL_DESKS)
+        wd_quant(chunks[1], bf1_own[:], 0, OWN_DESKS)
+        size_product(pair, FUSED, low)
+        v_quant(0)
+        wd_quant(chunks[1], bf1_pool[:, :OWN_DESKS, :], OWN_DESKS, 2 * OWN_DESKS)
+        wd_quant(chunks[1], bf1_pool[:, OWN_DESKS:, :], 2 * OWN_DESKS, NW)
+        size_product(pair, SCALED, high)
+        v_quant(1)
+        v_product(2, G)
+        v_product(3, G)
+        bf2 = keep.tile([P, NW, PACK], BF16, name="bf2", tag="r2", align_bytes=64)
+        wd_cast_pool(bf2[:], chunks[2], 0, NW)
         v_product(4, G)
-        for u in SECOND_RUN:
+        for u in (2, 3, 4):
             v_product(u, H)
-        wd_cast(chunks[3], POOL_DESKS, NW)
-        v_product(5, G)
-        for u in SECOND_RUN:
+        for u in (2, 3, 4):
             v_quant(u)
-        wd_quant(chunks[3])
-        sums = [out_sums(jb, NT)[0] for jb in range(2)]
-        v_product(6, H)
+        bf3_own = in_turn([P, OWN_DESKS, PACK], BF16)
+        wd_cast(bf3_own[:], chunks[3], 0, OWN_DESKS)
+        v_product(5, G)
+        bf3_pool = keep.tile([P, pool_desks, PACK], BF16, name="bf3_pool", tag="r5", align_bytes=64)
+        wd_cast_pool(bf3_pool[:], chunks[3], OWN_DESKS, NW)
+        wd_quant(chunks[2], bf2[:], 0, NW)
+        for u in (5, 6):
+            v_product(u, H)
+        wd_quant(chunks[3], bf3_own[:], 0, OWN_DESKS)
+        v_quant(5)
         v_product(6, G)
-        sums.append(out_sums(2, NT)[0])
-        v_quant(LAST - 1, (H, G))
+        wd_quant(chunks[3], bf3_pool[:, :OWN_DESKS, :], OWN_DESKS, 2 * OWN_DESKS)
+        wd_quant(chunks[3], bf3_pool[:, OWN_DESKS:, :], 2 * OWN_DESKS, NW)
+        v_quant(6)
         v_product(LAST, G)
         v_product(LAST, H)
-        for jb, acc in enumerate(sums):
-            res = ring.tile([P, NT, JW], F32, name="res", tag="res", bufs=JB - 1)
-            nc.scalar.copy(res[:], acc[:])
-            nc.sync.dma_start(out_v[:, :, jb * JW : (jb + 1) * JW], res[:])
         v_quant(LAST, (G, H))
 
-        half_nt = NT // 2
-        accs = out_sums(JB - 1, half_nt)
-        for part, copy, queue in ((0, nc.vector.tensor_copy, nc.sync), (1, nc.scalar.copy, nc.scalar)):
-            res = keep.tile([P, half_nt, JW], F32, name="res_last%d" % part)
-            copy(res[:], accs[part][:, 0:half_nt, :])
-            queue.dma_start(out_v[:, part * half_nt : (part + 1) * half_nt, (JB - 1) * JW : JB * JW], res[:])
+        groups = [(0, (0, 1)), (0, (2,)), (1, (0, 1)), (1, (2,))]
+        sums = [out_sum(half, jbs, True) for half, jbs in groups]
+        last = [out_sum(half, (JB - 1,), False) for half in range(2)]
+        for acc, (half, jbs) in zip(sums, groups):
+            store(acc, half, jbs, nc.scalar.copy, nc.sync)
+        store(last[0], 0, (JB - 1,), nc.vector.tensor_copy, nc.sync)
+        store(last[1], 1, (JB - 1,), nc.scalar.copy, nc.scalar)

@@ -311,9 +311,10 @@ def tile_list_desk_stress_results_kernel(tc, tab_words, tab_scales, tab2_words, 
 
         pair = (2, 3)
         low, high = range(0, PACK // 2), range(PACK // 2, PACK)
-        for u in (0, 1):
-            s_abs((u,), u, 2)
-            s_root((u,), 2)
+        s_abs((0,), 0)
+        s_abs((1,), 1)
+        s_root((0,))
+        s_root((1,))
         s_abs(pair, 2)
         s_abs(pair, 3)
         s_abs((4,), 4)
@@ -324,21 +325,17 @@ def tile_list_desk_stress_results_kernel(tc, tab_words, tab_scales, tab2_words, 
         s_abs((5,), 5)
         size_product((4,), ON_SCALAR)
         s_root((5,))
-        s_abs((6,), 6)
-        s_square((5,))
-        s_root((6,))
-        size_product((5,), ON_SCALAR)
-        s_square((6,))
-        s_abs((7,), 7)
-        size_product((6,), ON_SCALAR)
-        s_root((7,), 2)
+        for u in (5, 6):
+            s_abs((u + 1,), u + 1)
+            s_square((u,))
+            s_root((u + 1,))
+            size_product((u,), ON_SCALAR)
         s_square((7,), 2)
         size_product((7,), ON_SCALAR)
 
         pool_desks = NW - OWN_DESKS
-        size_product((0,), FUSED, low)
         wd_quant(chunks[0], bf0[:], 0, NW)
-        size_product((0,), FUSED, high)
+        size_product((0,), FUSED)
         bf1_own = in_turn([P, OWN_DESKS, PACK], BF16)
         wd_cast(bf1_own[:], chunks[1], 0, OWN_DESKS)
         size_product((1,), FUSED)

@@ -251,7 +251,7 @@ def tile_list_desk_stress_results_kernel(tc, tab_words, tab_scales, tab2_words, 
             nc.vector.tensor_copy(*cast_views(dst, ch, lo, hi))
 
         def wd_cast_pool(dst, ch, lo, hi):
-            dst, src = cast_views(dst, ch, lo, hi)
+            src = wdraw[ch[0]][:, :, ch[1] * NW + lo : ch[1] * NW + hi].rearrange("p t n -> p n t")
             nc.gpsimd.tensor_scalar(out=dst, in0=src, scalar1=1.0, scalar2=0.0, op0=MULT, op1=ADD)
 
         def wd_quant(ch, src, lo, hi):
@@ -336,8 +336,6 @@ def tile_list_desk_stress_results_kernel(tc, tab_words, tab_scales, tab2_words, 
         pool_desks = NW - OWN_DESKS
         wd_quant(chunks[0], bf0[:], 0, NW)
         size_product((0,), FUSED)
-        bf1_own = in_turn([P, OWN_DESKS, PACK], BF16)
-        wd_cast(bf1_own[:], chunks[1], 0, OWN_DESKS)
         size_product((1,), FUSED)
         bf1_pool = keep.tile([P, pool_desks, PACK], BF16, name="bf1_pool", tag="y1", align_bytes=64)
         wd_cast_pool(bf1_pool[:], chunks[1], OWN_DESKS, NW)
@@ -345,9 +343,11 @@ def tile_list_desk_stress_results_kernel(tc, tab_words, tab_scales, tab2_words, 
         v_product(1, H)
         v_product(0, H)
         v_product(1, G)
-        wd_quant(chunks[1], bf1_own[:], 0, OWN_DESKS)
+        bf1_own = in_turn([P, OWN_DESKS, PACK], BF16)
+        wd_cast(bf1_own[:], chunks[1], 0, OWN_DESKS)
         size_product(pair, FUSED, low)
         v_quant(0)
+        wd_quant(chunks[1], bf1_own[:], 0, OWN_DESKS)
         wd_quant(chunks[1], bf1_pool[:, :OWN_DESKS, :], OWN_DESKS, 2 * OWN_DESKS)
         wd_quant(chunks[1], bf1_pool[:, OWN_DESKS:, :], 2 * OWN_DESKS, NW)
         size_product(pair, SCALED, high)

@@ -55,7 +55,7 @@ def tile_list_desk_stress_results_kernel(tc, tab_words, tab_scales, tab2_words, 
         keep = ctx.enter_context(tc.tile_pool(name="keep", bufs=1))
         laid = ctx.enter_context(tc.tile_pool(name="laid", bufs=1))
         ring = ctx.enter_context(tc.tile_pool(name="ring", bufs=TURNS))
-        psum = ctx.enter_context(tc.psum_pool(name="psum", bufs=UNITS))
+        psum = ctx.enter_context(tc.psum_pool(name="psum", bufs=1))
 
         idx = keep.tile([P, S // LIST_ROWS], U16, name="idx")
         idx2 = keep.tile([P, S2 // LIST_ROWS], U16, name="idx2")
@@ -162,7 +162,7 @@ def tile_list_desk_stress_results_kernel(tc, tab_words, tab_scales, tab2_words, 
                     stop=(a == KP - 1 and t == PACK - 1),
                 )
 
-        banks = [psum.tile([P, PACK, JW], F32, name="bank", tag="bank") for u in range(UNITS)]
+        banks = [psum.tile([P, PACK, JW], F32, name="bank%d" % u, tag="bank%d" % u) for u in range(UNITS)]
         for a in range(KP - 1):
             for u in range(UNITS):
                 c_pass(u, a)
@@ -277,26 +277,25 @@ def tile_list_desk_stress_results_kernel(tc, tab_words, tab_scales, tab2_words, 
         out_v = out.rearrange("(nt p) j -> p nt j", p=P)
         half_nt = NT // 2
 
-        def out_sum(half, jbs, linear_last):
-            acc = psum.tile([P, half_nt, 2 * JW], F32, name="bank", tag="bank")
+        def out_sum(nts, jbs, bank):
+            acc = psum.tile([P, len(nts), len(jbs) * JW], F32, name="out%d" % bank, tag="bank%d" % bank)
             steps = [(u, kind) for u in range(UNITS) if units[u][0] in jbs for kind in (G, H)]
-            if linear_last:
+            if LAST not in [u for u, kind in steps]:
                 steps = [s for s in steps if s[1] == G or units[s[0]][1] == 0] + [s for s in steps if s[1] == H and units[s[0]][1] == 1]
             for k, (u, kind) in enumerate(steps):
-                for n in range(half_nt):
+                for n, nt in enumerate(nts):
                     lo = (units[u][0] - jbs[0]) * JW
                     dst = acc[:, n, lo : lo + JW]
                     if kind == G:
-                        option_pass(dst, half * half_nt + n, u, k == 0 and n == 0)
+                        option_pass(dst, nt, u, k == 0 and n == 0)
                     else:
-                        linear_pass(dst, half * half_nt + n, u, k == len(steps) - 1 and n == half_nt - 1)
+                        linear_pass(dst, nt, u, k == len(steps) - 1 and n == len(nts) - 1)
             return acc
 
-        def store(acc, half, jbs, copy, queue):
-            width = len(jbs) * JW
-            res = keep.tile([P, half_nt, width], F32, name="res%d_%d" % (half, jbs[0]))
-            copy(res[:], acc[:, :, :width])
-            queue.dma_start(out_v[:, half * half_nt : (half + 1) * half_nt, jbs[0] * JW : jbs[0] * JW + width], res[:])
+        def store(acc, nts, jbs, copy, queue):
+            res = keep.tile([P, len(nts), len(jbs) * JW], F32, name="res%d_%d" % (nts[0], jbs[0]))
+            copy(res[:], acc[:])
+            queue.dma_start(out_v[:, nts[0] : nts[-1] + 1, jbs[0] * JW : (jbs[-1] + 1) * JW], res[:])
 
         bf0 = keep.tile([P, NW, PACK], BF16, name="bf0", align_bytes=64)
         wd_cast(bf0[:], chunks[0], 0, NW)
@@ -379,10 +378,11 @@ def tile_list_desk_stress_results_kernel(tc, tab_words, tab_scales, tab2_words, 
         v_product(LAST, H)
         v_quant(LAST, (G, H))
 
-        groups = [(0, (0, 1)), (0, (2,)), (1, (0, 1)), (1, (2,))]
-        sums = [out_sum(half, jbs, True) for half, jbs in groups]
-        last = [out_sum(half, (JB - 1,), False) for half in range(2)]
-        for acc, (half, jbs) in zip(sums, groups):
-            store(acc, half, jbs, nc.scalar.copy, nc.sync)
-        store(last[0], 0, (JB - 1,), nc.vector.tensor_copy, nc.sync)
-        store(last[1], 1, (JB - 1,), nc.scalar.copy, nc.scalar)
+        groups = [((0, 1), (0, 1), 1), ((0, 1), (2,), 0), ((2, 3), (0, 1), 5), ((2, 3), (2,), 2)]
+        sums = [out_sum(*group) for group in groups]
+        for acc, (nts, jbs, bank) in zip(sums, groups):
+            store(acc, nts, jbs, nc.scalar.copy, nc.sync)
+        last = [out_sum((nt,), (JB - 1,), bank) for nt, bank in enumerate((3, 4, 6, 1))]
+        for nt, acc in enumerate(last):
+            copy = (nc.vector.tensor_copy, nc.scalar.copy)[nt % 2]
+            store(acc, (nt,), (JB - 1,), copy, nc.scalar if nt == NT - 1 else nc.sync)

@@ -27,7 +27,6 @@ JB = S2 // JW
 NT = N // P
 UNITS = JB * IB
 LAST = UNITS - 1
-NW = 256
 QUADRANT = 32
 ROWS = 4
 LIST_ROWS = 16
@@ -45,7 +44,9 @@ AT_TAB2_2 = 4 * (2 * T2 + T)
 AT_TAB_2 = AT_TAB2_2 + 4 * T2 + LAP
 AT_DEALT = AT_TAB2_2 + 4 * T2 - S2
 FUSED, SCALED, ON_SCALAR = 0, 1, 2
-OWN_DESKS = 64
+FIRST = 128
+CUT = 320
+WIDTHS = (256, 128, 64)
 TURNS = 30
 
 
@@ -67,8 +68,7 @@ def tile_list_desk_stress_results_kernel(tc, tab_words, tab_scales, tab2_words, 
         early = keep.tile([P, S + S2], U8, name="early", align_bytes=64)
         late = keep.tile([P, S + S2], U8, name="late", align_bytes=64)
         planes = [early, early, late]
-        chunks = [(b, half) for b in range(IB) for half in range(N // NW)]
-        wds = {ch: keep.tile([P, NW], U8, name="wds%d_%d" % ch, align_bytes=64) for ch in chunks}
+        wds = [keep.tile([P, N], U8, name="wds%d" % b, align_bytes=64) for b in range(IB)]
         tabw, tab2w, vw, v2w, wdraw, wdw = {}, {}, {}, {}, {}, {}
         one_in = keep.tile([P, 1], F32, name="one_in", tag="tabw0", align_bytes=64)
         one = keep.tile([P, 1], F32, name="one")
@@ -140,10 +140,11 @@ def tile_list_desk_stress_results_kernel(tc, tab_words, tab_scales, tab2_words, 
 
         for b in range(IB):
             wdraw[b] = laid.tile([P, PACK, N], F32, name="wdraw%d" % b, offset=AT_WD + b * 4 * PACK * N)
-        nc.sync.dma_start(wdraw[0][:, :, :NW], wd_rows(0)[:, :, :NW])
+        nc.sync.dma_start(wdraw[0][:, :, :FIRST], wd_rows(0)[:, :, :FIRST])
         sz = laid.tile([P, IB, PACK], F32, name="sz", offset=AT_SIZE)
         nc.sync.dma_start(sz[:], size.rearrange("(b p t) -> p b t", b=IB, t=PACK))
-        nc.sync.dma_start(wdraw[0][:, :, NW:], wd_rows(0)[:, :, NW:])
+        nc.sync.dma_start(wdraw[0][:, :, FIRST:CUT], wd_rows(0)[:, :, FIRST:CUT])
+        nc.sync.dma_start(wdraw[0][:, :, CUT:], wd_rows(0)[:, :, CUT:])
         nc.sync.dma_start(wdraw[1][:], wd_rows(1))
 
         units = [(0, 0), (0, 1), (1, 0), (2, 0), (1, 1), (2, 1), (3, 1), (3, 0)]
@@ -172,7 +173,7 @@ def tile_list_desk_stress_results_kernel(tc, tab_words, tab_scales, tab2_words, 
         w4w = laid.tile([P, IB, 2 * N], U8, name="w4w", offset=AT_TAB2_2, align_bytes=64)
         nc.sync.dma_start(w4w[:].bitcast(I32), w4_words.rearrange("b p e -> p b e").bitcast(I32))
 
-        r_t, y_t, w_t, d_t, hg_t, hgw, hgs = {}, {}, {}, {}, {}, {}, {}
+        r_t, y_t, w_t, d_t, hg_t, hgw, hgs, bf_t = {}, {}, {}, {}, {}, {}, {}, {}
 
         def in_turn(shape, dtype):
             return ring.tile(shape, dtype, name="turn", tag="turn", align_bytes=64)
@@ -185,15 +186,15 @@ def tile_list_desk_stress_results_kernel(tc, tab_words, tab_scales, tab2_words, 
             for lo in range(ts[0], ts[-1] + 1, step):
                 nc.scalar.activation(dst[:, lo : lo + step, :], src[:, lo : lo + step, :], func, **operands)
 
-        def s_abs(us, u, parts=1):
-            if us not in r_t:
-                r_t[us] = wide("r%d" % us[0], us)
-            lo = us.index(u) * JW
-            activate(r_t[us][:, :, lo : lo + JW], banks[u], parts, ACT.Abs)
+        def s_abs(u, parts=1):
+            r_t[u] = keep.tile([P, PACK, JW], F32, name="r%d" % u, tag="r%d" % u, align_bytes=64)
+            activate(r_t[u], banks[u], parts, ACT.Abs)
 
-        def s_root(us, parts=1):
-            y_t[us] = wide("y%d" % us[0], us)
-            activate(y_t[us], r_t[us], parts, ACT.Abs_reciprocal_sqrt, bias=one[:])
+        def s_root(us, u, parts=1):
+            if us not in y_t:
+                y_t[us] = wide("y%d" % us[0], us)
+            lo = us.index(u) * JW
+            activate(y_t[us][:, :, lo : lo + JW], r_t[u], parts, ACT.Abs_reciprocal_sqrt, bias=one[:])
 
         def s_square(us, parts=1, ts=range(PACK)):
             w_t[us] = wide("w%d" % us[0], us)
@@ -228,7 +229,7 @@ def tile_list_desk_stress_results_kernel(tc, tab_words, tab_scales, tab2_words, 
                 hg_t[u] = in_turn([P, 2, JW * PACK], BF16)
             nc.vector.tensor_tensor(
                 hg_t[u][:, half, :].rearrange("p (c i t) -> p c t i", i=RUN, t=PACK),
-                by_runs(banks[u][:] if half == H else of_unit(r_t, u)),
+                by_runs((banks[u], r_t[u])[half][:]),
                 by_runs(of_unit(d_t, u)),
                 MULT,
             )
@@ -243,21 +244,25 @@ def tile_list_desk_stress_results_kernel(tc, tab_words, tab_scales, tab2_words, 
                     cols = slice(half * JW, (half + 1) * JW)
                     nc.vector.quantize_mx(out=hgw[u][:, cols].bitcast(FP8X4), scales=hgs[u][:, cols], in_=hg_t[u][:, half, :])
 
-        def cast_views(dst, ch, lo, hi):
-            src = wdraw[ch[0]][:, :, ch[1] * NW + lo : ch[1] * NW + hi]
-            return dst.rearrange("p (c i) t -> p c t i", i=RUN), by_runs(src)
+        def wd_cast(dst, b, lo, hi):
+            nc.vector.tensor_copy(dst[:].rearrange("p (c i) t -> p c t i", i=RUN), by_runs(wdraw[b][:, :, lo:hi]))
+            bf_t[b, lo] = dst
 
-        def wd_cast(dst, ch, lo, hi):
-            nc.vector.tensor_copy(*cast_views(dst, ch, lo, hi))
+        def wd_cast_pool(tag, b, lo, hi):
+            dst = keep.tile([P, hi - lo, PACK], BF16, name="bf" + tag, tag=tag, align_bytes=64)
+            src = wdraw[b][:, :, lo:hi].rearrange("p t n -> p n t")
+            nc.gpsimd.tensor_scalar(out=dst[:], in0=src, scalar1=1.0, scalar2=0.0, op0=MULT, op1=ADD)
+            bf_t[b, lo] = dst
 
-        def wd_cast_pool(dst, ch, lo, hi):
-            src = wdraw[ch[0]][:, :, ch[1] * NW + lo : ch[1] * NW + hi].rearrange("p t n -> p n t")
-            nc.gpsimd.tensor_scalar(out=dst, in0=src, scalar1=1.0, scalar2=0.0, op0=MULT, op1=ADD)
-
-        def wd_quant(ch, src, lo, hi):
-            if ch not in wdw:
-                wdw[ch] = in_turn([P, NW], U32)
-            nc.vector.quantize_mx(out=wdw[ch][:, lo:hi].bitcast(FP8X4), scales=wds[ch][:, lo:hi], in_=src.rearrange("p n t -> p (n t)"))
+        def wd_quant(b, lo, hi):
+            if b not in wdw:
+                wdw[b] = in_turn([P, N], U32)
+            at = lo
+            for width in WIDTHS:
+                if hi - at >= width:
+                    src = bf_t[b, lo][:, at - lo : at - lo + width, :].rearrange("p n t -> p (n t)")
+                    nc.vector.quantize_mx(out=wdw[b][:, at : at + width].bitcast(FP8X4), scales=wds[b][:, at : at + width], in_=src)
+                    at = at + width
 
         def option_pass(dst, nt, u, start):
             b = units[u][1]
@@ -267,8 +272,8 @@ def tile_list_desk_stress_results_kernel(tc, tab_words, tab_scales, tab2_words, 
             )
 
         def linear_pass(dst, nt, u, stop):
-            ch = (units[u][1], nt * P // NW)
-            wcols = slice(nt * P % NW, nt * P % NW + P)
+            ch = units[u][1]
+            wcols = slice(nt * P, (nt + 1) * P)
             nc.tensor.matmul_mx(
                 out=dst, lhsT=wdw[ch][:, wcols].bitcast(FP8X4), lhsT_scale=wds[ch][:, wcols],
                 rhs=hgw[u][:, 0:JW].bitcast(FP8X4), rhs_scale=hgs[u][:, 0:JW], start=False, stop=stop,
@@ -297,8 +302,7 @@ def tile_list_desk_stress_results_kernel(tc, tab_words, tab_scales, tab2_words, 
             copy(res[:], acc[:])
             queue.dma_start(out_v[:, nts[0] : nts[-1] + 1, jbs[0] * JW : (jbs[-1] + 1) * JW], res[:])
 
-        bf0 = keep.tile([P, NW, PACK], BF16, name="bf0", align_bytes=64)
-        wd_cast(bf0[:], chunks[0], 0, NW)
+        wd_cast(keep.tile([P, FIRST, PACK], BF16, name="bf0", align_bytes=64), 0, 0, FIRST)
         for u in range(UNITS):
             c_pass(u, KP - 1)
         w4s = late[:, 0 : IB * N].rearrange("p (b n) -> p b n", b=IB)
@@ -310,69 +314,62 @@ def tile_list_desk_stress_results_kernel(tc, tab_words, tab_scales, tab2_words, 
 
         pair = (2, 3)
         low, high = range(0, PACK // 2), range(PACK // 2, PACK)
-        s_abs((0,), 0)
-        s_abs((1,), 1)
-        s_root((0,))
-        s_root((1,))
-        s_abs(pair, 2)
-        s_abs(pair, 3)
-        s_abs((4,), 4)
-        s_root(pair)
-        s_root((4,))
-        s_square(pair, 1, high)
-        s_square((4,))
-        s_abs((5,), 5)
-        size_product((4,), ON_SCALAR)
-        s_root((5,))
-        for u in (5, 6):
-            s_abs((u + 1,), u + 1)
+        for u in (0, 1):
+            s_abs(u, 2)
+            s_root((u,), u, 2)
+        for u in pair:
+            s_abs(u)
+        for u in pair:
+            s_root(pair, u)
+        for u in (4, 5):
+            s_abs(u)
+        for u in (4, 5):
+            s_root((u,), u)
+        for u in (4, 5):
             s_square((u,))
-            s_root((u + 1,))
-            size_product((u,), ON_SCALAR)
+        size_product((4,), ON_SCALAR)
+        s_abs(6)
+        size_product((5,), ON_SCALAR)
+        s_root((6,), 6)
+        s_abs(7)
+        s_square((6,), 2)
+        size_product((6,), ON_SCALAR)
+        s_root((7,), 7, 2)
         s_square((7,), 2)
         size_product((7,), ON_SCALAR)
 
-        pool_desks = NW - OWN_DESKS
-        wd_quant(chunks[0], bf0[:], 0, NW)
-        size_product((0,), FUSED)
+        wd_quant(0, 0, FIRST)
+        size_product((0,), FUSED, low)
+        wd_cast(in_turn([P, CUT - FIRST, PACK], BF16), 0, FIRST, CUT)
+        size_product((0,), FUSED, high)
+        wd_quant(0, FIRST, CUT)
         size_product((1,), FUSED)
-        bf1_pool = keep.tile([P, pool_desks, PACK], BF16, name="bf1_pool", tag="y1", align_bytes=64)
-        wd_cast_pool(bf1_pool[:], chunks[1], OWN_DESKS, NW)
+        wd_cast_pool("y1", 0, CUT, N)
         v_product(0, G)
         v_product(1, H)
         v_product(0, H)
         v_product(1, G)
-        bf1_own = in_turn([P, OWN_DESKS, PACK], BF16)
-        wd_cast(bf1_own[:], chunks[1], 0, OWN_DESKS)
-        size_product(pair, FUSED, low)
+        size_product(pair, FUSED)
         v_quant(0)
-        wd_quant(chunks[1], bf1_own[:], 0, OWN_DESKS)
-        wd_quant(chunks[1], bf1_pool[:, :OWN_DESKS, :], OWN_DESKS, 2 * OWN_DESKS)
-        wd_quant(chunks[1], bf1_pool[:, OWN_DESKS:, :], 2 * OWN_DESKS, NW)
-        size_product(pair, SCALED, high)
+        wd_quant(0, CUT, N)
         v_quant(1)
         v_product(2, G)
+        wd_cast_pool("r2", 1, 0, CUT)
         v_product(3, G)
-        bf2 = keep.tile([P, NW, PACK], BF16, name="bf2", tag="r2", align_bytes=64)
-        wd_cast_pool(bf2[:], chunks[2], 0, NW)
-        v_product(4, G)
         for u in (2, 3, 4):
             v_product(u, H)
-        for u in (2, 3, 4):
+        v_product(4, G)
+        for u in (2, 3):
             v_quant(u)
-        bf3_own = in_turn([P, OWN_DESKS, PACK], BF16)
-        wd_cast(bf3_own[:], chunks[3], 0, OWN_DESKS)
+        wd_quant(1, 0, CUT)
         v_product(5, G)
-        bf3_pool = keep.tile([P, pool_desks, PACK], BF16, name="bf3_pool", tag="r5", align_bytes=64)
-        wd_cast_pool(bf3_pool[:], chunks[3], OWN_DESKS, NW)
-        wd_quant(chunks[2], bf2[:], 0, NW)
+        wd_cast_pool("r5", 1, CUT, N)
+        v_quant(4)
         for u in (5, 6):
             v_product(u, H)
-        wd_quant(chunks[3], bf3_own[:], 0, OWN_DESKS)
         v_quant(5)
         v_product(6, G)
-        wd_quant(chunks[3], bf3_pool[:, :OWN_DESKS, :], OWN_DESKS, 2 * OWN_DESKS)
-        wd_quant(chunks[3], bf3_pool[:, OWN_DESKS:, :], 2 * OWN_DESKS, NW)
+        wd_quant(1, CUT, N)
         v_quant(6)
         v_product(LAST, G)
         v_product(LAST, H)

@@ -379,7 +379,6 @@ def tile_list_desk_stress_results_kernel(tc, tab_words, tab_scales, tab2_words, 
         sums = [out_sum(*group) for group in groups]
         for acc, (nts, jbs, bank) in zip(sums, groups):
             store(acc, nts, jbs, nc.scalar.copy, nc.sync)
-        last = [out_sum((nt,), (JB - 1,), bank) for nt, bank in enumerate((3, 4, 6, 1))]
-        for nt, acc in enumerate(last):
-            copy = (nc.vector.tensor_copy, nc.scalar.copy)[nt % 2]
-            store(acc, (nt,), (JB - 1,), copy, nc.scalar if nt == NT - 1 else nc.sync)
+        last = [out_sum(nts, (JB - 1,), bank) for nts, bank in (((0, 1), 3), ((2, 3), 4))]
+        store(last[0], (0, 1), (JB - 1,), nc.vector.tensor_copy, nc.sync)
+        store(last[1], (2, 3), (JB - 1,), nc.scalar.copy, nc.scalar)

@@ -299,7 +299,7 @@ def tile_list_desk_stress_results_kernel(tc, tab_words, tab_scales, tab2_words, 
 
         def store(acc, nts, jbs, copy, queue):
             res = keep.tile([P, len(nts), len(jbs) * JW], F32, name="res%d_%d" % (nts[0], jbs[0]))
-            copy(res[:], acc[:])
+            copy(res[:], acc)
             queue.dma_start(out_v[:, nts[0] : nts[-1] + 1, jbs[0] * JW : (jbs[-1] + 1) * JW], res[:])
 
         wd_cast(keep.tile([P, FIRST, PACK], BF16, name="bf0", align_bytes=64), 0, 0, FIRST)
@@ -375,10 +375,12 @@ def tile_list_desk_stress_results_kernel(tc, tab_words, tab_scales, tab2_words, 
         v_product(LAST, H)
         v_quant(LAST, (G, H))
 
-        groups = [((0, 1), (0, 1), 1), ((0, 1), (2,), 0), ((2, 3), (0, 1), 5), ((2, 3), (2,), 2)]
+        groups = [((0, 1), (0, 1), 1), ((0, 1), (2,), 2), ((2, 3), (0, 1), 0), ((2, 3), (2,), 3)]
         sums = [out_sum(*group) for group in groups]
-        for acc, (nts, jbs, bank) in zip(sums, groups):
-            store(acc, nts, jbs, nc.scalar.copy, nc.sync)
-        last = [out_sum(nts, (JB - 1,), bank) for nts, bank in (((0, 1), 3), ((2, 3), 4))]
-        store(last[0], (0, 1), (JB - 1,), nc.vector.tensor_copy, nc.sync)
-        store(last[1], (2, 3), (JB - 1,), nc.scalar.copy, nc.scalar)
+        for n in range(half_nt):
+            store(sums[0][:, n : n + 1, :], (n,), groups[0][1], nc.scalar.copy, nc.sync)
+        for acc, (nts, jbs, bank) in list(zip(sums, groups))[1:]:
+            store(acc[:], nts, jbs, nc.scalar.copy, nc.sync)
+        last = [out_sum(nts, (JB - 1,), bank) for nts, bank in (((0, 1), 4), ((2, 3), 5))]
+        store(last[0][:], (0, 1), (JB - 1,), nc.vector.tensor_copy, nc.sync)
+        store(last[1][:], (2, 3), (JB - 1,), nc.scalar.copy, nc.scalar)

@@ -359,12 +359,12 @@ def tile_list_desk_stress_results_kernel(tc, tab_words, tab_scales, tab2_words, 
         for u in (2, 3, 4):
             v_product(u, H)
         v_product(4, G)
-        for u in (2, 3):
+        for u in (2, 4):
             v_quant(u)
         wd_quant(1, 0, CUT)
         v_product(5, G)
         wd_cast_pool("r5", 1, CUT, N)
-        v_quant(4)
+        v_quant(3)
         for u in (5, 6):
             v_product(u, H)
         v_quant(5)

@@ -34,15 +34,19 @@ RUN = 4
 H, G = 0, 1
 ROW_STEP = 4
 PASS2_ROW = 33
-LAP = 64
-AT_TAB2_1 = 0
-AT_TAB2_0 = 4 * T2 - LAP
-AT_TAB_1 = 8 * T2 - 2 * LAP
+LAP = 256
+LINE = 256
+AT_TAB2_0 = 0
+AT_TAB_1 = 4 * T2 - LAP
 AT_WD = AT_TAB_1 - LAP
 AT_SIZE = AT_WD + 4 * T
-AT_TAB2_2 = 4 * (2 * T2 + T)
-AT_TAB_2 = AT_TAB2_2 + 4 * T2 + LAP
-AT_DEALT = AT_TAB2_2 + 4 * T2 - S2
+AT_LATE = AT_TAB_1 + 4 * T
+AT_TAB_0 = AT_LATE + S + S2 - LAP
+AT_TAB2_1 = AT_TAB_0 + LAP
+AT_TAB2_2 = AT_TAB2_1 + 4 * T2
+AT_DEALT = AT_TAB2_2 + 4 * T2
+AT_TAB_2 = AT_DEALT + S + S2 - LAP
+AHEAD = 4
 FUSED, SCALED, ON_SCALAR = 0, 1, 2
 FIRST = 128
 CUT = 320
@@ -60,22 +64,20 @@ def tile_list_desk_stress_results_kernel(tc, tab_words, tab_scales, tab2_words, 
 
         idx = keep.tile([P, S // LIST_ROWS], U16, name="idx")
         idx2 = keep.tile([P, S2 // LIST_ROWS], U16, name="idx2")
-        tabs = keep.tile([P, T], U8, name="tabs", align_bytes=64)
-        tab2s = keep.tile([P, T2], U8, name="tab2s", align_bytes=64)
+        tabs = keep.tile([P, T], U8, name="tabs", align_bytes=LINE)
+        tab2s = keep.tile([P, T2], U8, name="tab2s", align_bytes=LINE)
         picked = keep.tile([P, S + S2], U8, name="picked", align_bytes=64)
         dealt = laid.tile([P, S + S2], U8, name="dealt", offset=AT_DEALT)
-        staged = keep.tile([P, S + S2], U8, name="staged", align_bytes=64)
-        early = keep.tile([P, S + S2], U8, name="early", align_bytes=64)
-        late = keep.tile([P, S + S2], U8, name="late", align_bytes=64)
-        planes = [early, early, late]
+        staged = keep.tile([P, S + S2], U8, name="staged", align_bytes=LINE)
+        early = keep.tile([P, S + S2], U8, name="early", align_bytes=LINE)
+        planes = {0: early, 1: early}
         wds = [keep.tile([P, N], U8, name="wds%d" % b, align_bytes=64) for b in range(IB)]
         tabw, tab2w, vw, v2w, wdraw, wdw = {}, {}, {}, {}, {}, {}
-        one_in = keep.tile([P, 1], F32, name="one_in", tag="tabw0", align_bytes=64)
+        one_in = laid.tile([P, 1], F32, name="one_in", offset=AT_TAB_0)
         one = keep.tile([P, 1], F32, name="one")
 
         nc.vector.memset(tab2s[:].bitcast(I32), 0)
         nc.vector.memset(tabs[:].bitcast(I32), 0)
-        nc.vector.memset(late[:].bitcast(I32), 0)
         nc.gpsimd.memset(one_in[:], 1.0)
         nc.scalar.activation(one[:], one_in[:], ACT.Abs_reciprocal_sqrt)
 
@@ -108,10 +110,9 @@ def tile_list_desk_stress_results_kernel(tc, tab_words, tab_scales, tab2_words, 
         nc.sync.dma_start(idx[:], offs)
         load_scale_rows(tab2s, tab2_scales)
         load_scale_rows(tabs, tab_scales)
-        tabw[0] = load_words(keep.tile([P, T], I32, name="tabw0", tag="tabw0", align_bytes=64), tab_words[0])
+        tabw[0] = load_words(laid.tile([P, T], I32, name="tabw0", offset=AT_TAB_0), tab_words[0])
 
         gather_v2(0, 0, S2)
-        tab2w[1] = load_words(laid.tile([P, T2], I32, name="tab2w1", offset=AT_TAB2_1), tab2_words[1])
         tabw[1] = load_words(laid.tile([P, T], I32, name="tabw1", offset=AT_TAB_1), tab_words[1])
         nc.vector.tensor_copy(picked[:, S:], tab2s[:].indirect(idx2[:]))
         nc.vector.tensor_copy(picked[:, :S], tabs[:].indirect(idx[:]))
@@ -126,14 +127,19 @@ def tile_list_desk_stress_results_kernel(tc, tab_words, tab_scales, tab2_words, 
             for row in range(1, ROWS):
                 place_rows(a, row, staged[ROW_STEP * (2 * row + a) : P : QUADRANT, :])
         tabw[2] = load_words(laid.tile([P, T], I32, name="tabw2", offset=AT_TAB_2), tab_words[2])
+        gather_v(0)
+        tab2w[1] = load_words(laid.tile([P, T2], I32, name="tab2w1", offset=AT_TAB2_1), tab2_words[1])
         tab2w[2] = load_words(laid.tile([P, T2], I32, name="tab2w2", offset=AT_TAB2_2), tab2_words[2])
+        late = laid.tile([P, S + S2], U8, name="late", offset=AT_LATE)
+        planes[KP - 1] = late
+        nc.vector.memset(late[:].bitcast(I32), 0)
         for row in range(ROWS):
             src = PASS2_ROW + row * ROW_STEP
             place_rows(KP - 1, row, staged[src : src + 3 * ROWS * ROW_STEP + 1 : ROWS * ROW_STEP, :])
-        gather_v(0)
-        gather_v2(1, 0, S2)
         gather_v(1)
         gather_v(2)
+        gather_v2(1, 0, JW)
+        gather_v2(1, JW, S2)
 
         def wd_rows(b):
             return wd[b * PASS : (b + 1) * PASS, :].rearrange("(p t) n -> p t n", t=PACK)
@@ -149,7 +155,7 @@ def tile_list_desk_stress_results_kernel(tc, tab_words, tab_scales, tab2_words, 
 
         units = [(0, 0), (0, 1), (1, 0), (2, 0), (1, 1), (2, 1), (3, 1), (3, 0)]
 
-        def c_pass(u, a):
+        def c_pass(u, a, stop):
             jb, b = units[u]
             for t in range(PACK):
                 icols = slice(b * PASS + t * P, b * PASS + (t + 1) * P)
@@ -160,17 +166,18 @@ def tile_list_desk_stress_results_kernel(tc, tab_words, tab_scales, tab2_words, 
                     rhs=v2w[a, jb].bitcast(FP8X4),
                     rhs_scale=planes[a][ROWS * a :, S + jb * JW : S + (jb + 1) * JW],
                     start=(a == 0 and t == 0),
-                    stop=(a == KP - 1 and t == PACK - 1),
+                    stop=(stop and t == PACK - 1),
                 )
 
         banks = [psum.tile([P, PACK, JW], F32, name="bank%d" % u, tag="bank%d" % u) for u in range(UNITS)]
-        for a in range(KP - 1):
-            for u in range(UNITS):
-                c_pass(u, a)
+        for u in range(UNITS):
+            c_pass(u, 0, False)
+        for u in range(AHEAD):
+            c_pass(u, 1, False)
 
         gather_v2(KP - 1, 0, JW)
         gather_v2(KP - 1, JW, S2)
-        w4w = laid.tile([P, IB, 2 * N], U8, name="w4w", offset=AT_TAB2_2, align_bytes=64)
+        w4w = laid.tile([P, IB, 2 * N], U8, name="w4w", offset=AT_TAB2_2, align_bytes=LINE)
         nc.sync.dma_start(w4w[:].bitcast(I32), w4_words.rearrange("b p e -> p b e").bitcast(I32))
 
         r_t, y_t, w_t, d_t, hg_t, hgw, hgs, bf_t = {}, {}, {}, {}, {}, {}, {}, {}
@@ -298,13 +305,15 @@ def tile_list_desk_stress_results_kernel(tc, tab_words, tab_scales, tab2_words, 
             return acc
 
         def store(acc, nts, jbs, copy, queue):
-            res = keep.tile([P, len(nts), len(jbs) * JW], F32, name="res%d_%d" % (nts[0], jbs[0]))
+            res = keep.tile([P, len(nts), len(jbs) * JW], F32, name="res%d_%d" % (nts[0], jbs[0]), align_bytes=LINE)
             copy(res[:], acc)
             queue.dma_start(out_v[:, nts[0] : nts[-1] + 1, jbs[0] * JW : (jbs[-1] + 1) * JW], res[:])
 
         wd_cast(keep.tile([P, FIRST, PACK], BF16, name="bf0", align_bytes=64), 0, 0, FIRST)
         for u in range(UNITS):
-            c_pass(u, KP - 1)
+            c_pass(u, KP - 1, u < AHEAD)
+            if u >= AHEAD:
+                c_pass(u, 1, True)
         w4s = late[:, 0 : IB * N].rearrange("p (b n) -> p b n", b=IB)
         for quadrant in range(P // QUADRANT):
             nc.sync.dma_start(

@@ -36,17 +36,17 @@ ROW_STEP = 4
 PASS2_ROW = 33
 LAP = 256
 LINE = 256
-AT_TAB2_0 = 0
-AT_TAB_1 = 4 * T2 - LAP
-AT_WD = AT_TAB_1 - LAP
+AT_SCALES2 = 0
+AT_TAB_2 = T2 - LAP
+AT_WD = AT_TAB_2 - LAP
 AT_SIZE = AT_WD + 4 * T
-AT_LATE = AT_TAB_1 + 4 * T
-AT_TAB_0 = AT_LATE + S + S2 - LAP
-AT_TAB2_1 = AT_TAB_0 + LAP
+AT_LATE = AT_TAB_2 + 4 * T
+AT_TAB_1 = AT_LATE + S + S2 - LAP
+AT_TAB2_1 = AT_TAB_1 + LAP
 AT_TAB2_2 = AT_TAB2_1 + 4 * T2
 AT_DEALT = AT_TAB2_2 + 4 * T2
-AT_TAB_2 = AT_DEALT + S + S2 - LAP
-AHEAD = 4
+AT_TAB2_0 = AT_DEALT + 4 * S2
+AT_TAB_0 = AT_TAB2_0 + 4 * T2 - LAP
 FUSED, SCALED, ON_SCALAR = 0, 1, 2
 FIRST = 128
 CUT = 320
@@ -65,7 +65,7 @@ def tile_list_desk_stress_results_kernel(tc, tab_words, tab_scales, tab2_words, 
         idx = keep.tile([P, S // LIST_ROWS], U16, name="idx")
         idx2 = keep.tile([P, S2 // LIST_ROWS], U16, name="idx2")
         tabs = keep.tile([P, T], U8, name="tabs", align_bytes=LINE)
-        tab2s = keep.tile([P, T2], U8, name="tab2s", align_bytes=LINE)
+        tab2s = laid.tile([P, T2], U8, name="tab2s", offset=AT_SCALES2)
         picked = keep.tile([P, S + S2], U8, name="picked", align_bytes=64)
         dealt = laid.tile([P, S + S2], U8, name="dealt", offset=AT_DEALT)
         staged = keep.tile([P, S + S2], U8, name="staged", align_bytes=LINE)
@@ -73,7 +73,7 @@ def tile_list_desk_stress_results_kernel(tc, tab_words, tab_scales, tab2_words, 
         planes = {0: early, 1: early}
         wds = [keep.tile([P, N], U8, name="wds%d" % b, align_bytes=64) for b in range(IB)]
         tabw, tab2w, vw, v2w, wdraw, wdw = {}, {}, {}, {}, {}, {}
-        one_in = laid.tile([P, 1], F32, name="one_in", offset=AT_TAB_0)
+        one_in = laid.tile([P, 1], F32, name="one_in", offset=AT_TAB_1)
         one = keep.tile([P, 1], F32, name="one")
 
         nc.vector.memset(tab2s[:].bitcast(I32), 0)
@@ -89,18 +89,21 @@ def tile_list_desk_stress_results_kernel(tc, tab_words, tab_scales, tab2_words, 
             nc.sync.dma_start(dst[0:P:ROW_STEP, :].bitcast(I32), scales[0:2].rearrange("a q t -> q a t").bitcast(I32))
             nc.sync.dma_start(dst[PASS2_ROW : PASS2_ROW + 16 * ROW_STEP : ROW_STEP, :].bitcast(I32), scales[2].bitcast(I32))
 
-        def place_rows(a, row, src):
-            nc.sync.dma_start(planes[a][ROWS * a + row : P : QUADRANT, :].bitcast(I32), src.bitcast(I32))
+        def place_rows(a, row, src, queue):
+            queue.dma_start(planes[a][ROWS * a + row : P : QUADRANT, :].bitcast(I32), src.bitcast(I32))
 
-        def gather_v(a):
-            vw[a] = keep.tile([P, S], U32, name="vw%d" % a, align_bytes=64)
+        def gather_v(a, lo, hi):
+            picks = keep.tile([P, (hi - lo) * PASS], U32, name="vw%d_%d" % (a, lo), align_bytes=64)
             nc.vector.tensor_copy(
-                vw[a][:].rearrange("p (b t m) -> p b m t", b=IB, t=PACK),
-                tabw[a][:].bitcast(U32).indirect(idx[:]),
+                picks[:].rearrange("p (b t m) -> p b m t", m=P, t=PACK),
+                tabw[a][:].bitcast(U32).indirect(idx[:, lo * PASS // LIST_ROWS : hi * PASS // LIST_ROWS]),
             )
+            for b in range(lo, hi):
+                vw[a, b] = picks[:, (b - lo) * PASS : (b - lo + 1) * PASS]
 
-        def gather_v2(a, lo, hi):
-            picks = keep.tile([P, hi - lo], U32, name="v2w%d_%d" % (a, lo), align_bytes=64)
+        def gather_v2(a, lo, hi, picks=None):
+            if picks is None:
+                picks = keep.tile([P, hi - lo], U32, name="v2w%d_%d" % (a, lo), align_bytes=64)
             nc.vector.tensor_copy(picks[:], tab2w[a][:].bitcast(U32).indirect(idx2[:, lo // LIST_ROWS : hi // LIST_ROWS]))
             for jb in range(lo // JW, hi // JW):
                 v2w[a, jb] = picks[:, jb * JW - lo : (jb + 1) * JW - lo]
@@ -110,11 +113,10 @@ def tile_list_desk_stress_results_kernel(tc, tab_words, tab_scales, tab2_words, 
         nc.sync.dma_start(idx[:], offs)
         load_scale_rows(tab2s, tab2_scales)
         load_scale_rows(tabs, tab_scales)
-        tabw[0] = load_words(laid.tile([P, T], I32, name="tabw0", offset=AT_TAB_0), tab_words[0])
-
-        gather_v2(0, 0, S2)
         tabw[1] = load_words(laid.tile([P, T], I32, name="tabw1", offset=AT_TAB_1), tab_words[1])
+
         nc.vector.tensor_copy(picked[:, S:], tab2s[:].indirect(idx2[:]))
+        tabw[2] = load_words(laid.tile([P, T], I32, name="tabw2", offset=AT_TAB_2), tab_words[2])
         nc.vector.tensor_copy(picked[:, :S], tabs[:].indirect(idx[:]))
         nc.vector.tensor_copy(dealt[:, S:].bitcast(I32), picked[:, S:].bitcast(I32))
         nc.vector.tensor_copy(
@@ -125,9 +127,10 @@ def tile_list_desk_stress_results_kernel(tc, tab_words, tab_scales, tab2_words, 
         nc.vector.tensor_copy(staged[:].bitcast(I32), dealt[:].bitcast(I32))
         for a in range(KP - 1):
             for row in range(1, ROWS):
-                place_rows(a, row, staged[ROW_STEP * (2 * row + a) : P : QUADRANT, :])
-        tabw[2] = load_words(laid.tile([P, T], I32, name="tabw2", offset=AT_TAB_2), tab_words[2])
-        gather_v(0)
+                place_rows(a, row, staged[ROW_STEP * (2 * row + a) : P : QUADRANT, :], nc.scalar)
+        gather_v2(0, 0, S2, laid.tile([P, S2], U32, name="v2w0", offset=AT_DEALT))
+        tabw[0] = load_words(laid.tile([P, T], I32, name="tabw0", offset=AT_TAB_0), tab_words[0])
+        gather_v(1, 0, IB)
         tab2w[1] = load_words(laid.tile([P, T2], I32, name="tab2w1", offset=AT_TAB2_1), tab2_words[1])
         tab2w[2] = load_words(laid.tile([P, T2], I32, name="tab2w2", offset=AT_TAB2_2), tab2_words[2])
         late = laid.tile([P, S + S2], U8, name="late", offset=AT_LATE)
@@ -135,9 +138,10 @@ def tile_list_desk_stress_results_kernel(tc, tab_words, tab_scales, tab2_words, 
         nc.vector.memset(late[:].bitcast(I32), 0)
         for row in range(ROWS):
             src = PASS2_ROW + row * ROW_STEP
-            place_rows(KP - 1, row, staged[src : src + 3 * ROWS * ROW_STEP + 1 : ROWS * ROW_STEP, :])
-        gather_v(1)
-        gather_v(2)
+            place_rows(KP - 1, row, staged[src : src + 3 * ROWS * ROW_STEP + 1 : ROWS * ROW_STEP, :], nc.sync)
+        gather_v(2, 0, IB)
+        for b in range(IB):
+            gather_v(0, b, b + 1)
         gather_v2(1, 0, JW)
         gather_v2(1, JW, S2)
 
@@ -155,25 +159,27 @@ def tile_list_desk_stress_results_kernel(tc, tab_words, tab_scales, tab2_words, 
 
         units = [(0, 0), (0, 1), (1, 0), (2, 0), (1, 1), (2, 1), (3, 1), (3, 0)]
 
-        def c_pass(u, a, stop):
+        def c_pass(u, a):
             jb, b = units[u]
             for t in range(PACK):
                 icols = slice(b * PASS + t * P, b * PASS + (t + 1) * P)
                 nc.tensor.matmul_mx(
                     out=banks[u][:, t, :],
-                    lhsT=vw[a][:, icols].bitcast(FP8X4),
+                    lhsT=vw[a, b][:, t * P : (t + 1) * P].bitcast(FP8X4),
                     lhsT_scale=planes[a][ROWS * a :, icols],
                     rhs=v2w[a, jb].bitcast(FP8X4),
                     rhs_scale=planes[a][ROWS * a :, S + jb * JW : S + (jb + 1) * JW],
-                    start=(a == 0 and t == 0),
-                    stop=(stop and t == PACK - 1),
+                    start=(a == orders[u][0] and t == 0),
+                    stop=(a == orders[u][-1] and t == PACK - 1),
                 )
 
         banks = [psum.tile([P, PACK, JW], F32, name="bank%d" % u, tag="bank%d" % u) for u in range(UNITS)]
-        for u in range(UNITS):
-            c_pass(u, 0, False)
-        for u in range(AHEAD):
-            c_pass(u, 1, False)
+        ahead = {0: (0, 1), 1: (0, 1), 2: (0,), 3: (0,)}
+        orders = [ahead.get(u, ()) + (KP - 1,) + tuple(a for a in range(KP - 1) if a not in ahead.get(u, ())) for u in range(UNITS)]
+        for u in (0, 2, 3, 1):
+            c_pass(u, 0)
+        for u in (0, 1):
+            c_pass(u, 1)
 
         gather_v2(KP - 1, 0, JW)
         gather_v2(KP - 1, JW, S2)
@@ -311,9 +317,8 @@ def tile_list_desk_stress_results_kernel(tc, tab_words, tab_scales, tab2_words, 
 
         wd_cast(keep.tile([P, FIRST, PACK], BF16, name="bf0", align_bytes=64), 0, 0, FIRST)
         for u in range(UNITS):
-            c_pass(u, KP - 1, u < AHEAD)
-            if u >= AHEAD:
-                c_pass(u, 1, True)
+            for a in orders[u][len(ahead.get(u, ())) :]:
+                c_pass(u, a)
         w4s = late[:, 0 : IB * N].rearrange("p (b n) -> p b n", b=IB)
         for quadrant in range(P // QUADRANT):
             nc.sync.dma_start(

@@ -335,8 +335,9 @@ def tile_list_desk_stress_results_kernel(tc, tab_words, tab_scales, tab2_words, 
             s_abs(u)
         for u in pair:
             s_root(pair, u)
-        for u in (4, 5):
-            s_abs(u)
+        s_abs(4)
+        s_square(pair, 1, high)
+        s_abs(5)
         for u in (4, 5):
             s_root((u,), u)
         for u in (4, 5):
@@ -363,7 +364,8 @@ def tile_list_desk_stress_results_kernel(tc, tab_words, tab_scales, tab2_words, 
         v_product(1, H)
         v_product(0, H)
         v_product(1, G)
-        size_product(pair, FUSED)
+        size_product(pair, FUSED, low)
+        size_product(pair, SCALED, high)
         v_quant(0)
         wd_quant(0, CUT, N)
         v_quant(1)
@@ -395,6 +397,9 @@ def tile_list_desk_stress_results_kernel(tc, tab_words, tab_scales, tab2_words, 
             store(sums[0][:, n : n + 1, :], (n,), groups[0][1], nc.scalar.copy, nc.sync)
         for acc, (nts, jbs, bank) in list(zip(sums, groups))[1:]:
             store(acc[:], nts, jbs, nc.scalar.copy, nc.sync)
-        last = [out_sum(nts, (JB - 1,), bank) for nts, bank in (((0, 1), 4), ((2, 3), 5))]
-        store(last[0][:], (0, 1), (JB - 1,), nc.vector.tensor_copy, nc.sync)
-        store(last[1][:], (2, 3), (JB - 1,), nc.scalar.copy, nc.scalar)
+        last = [out_sum((nt,), (JB - 1,), bank) for nt, bank in enumerate((4, 5, 6, 1))]
+        for lo, queue in ((0, nc.sync), (half_nt, nc.scalar)):
+            res = keep.tile([P, half_nt, JW], F32, name="res_last%d" % lo, align_bytes=LINE)
+            nc.vector.tensor_copy(res[:, 0:1, :], last[lo][:])
+            nc.scalar.copy(res[:, 1:2, :], last[lo + 1][:])
+            queue.dma_start(out_v[:, lo : lo + half_nt, (JB - 1) * JW :], res[:])

@@ -31,6 +31,7 @@ QUADRANT = 32
 ROWS = 4
 LIST_ROWS = 16
 RUN = 4
+LONG_RUN = 8
 H, G = 0, 1
 ROW_STEP = 4
 PASS2_ROW = 33
@@ -234,16 +235,16 @@ def tile_list_desk_stress_results_kernel(tc, tab_words, tab_scales, tab2_words, 
             lo = us.index(u) * JW
             return tiles[us][:, :, lo : lo + JW]
 
-        def by_runs(src):
-            return src.rearrange("p t (c i) -> p c t i", i=RUN)
+        def by_runs(src, run=RUN):
+            return src.rearrange("p t (c i) -> p c t i", i=run)
 
         def v_product(u, half):
             if u not in hg_t:
                 hg_t[u] = in_turn([P, 2, JW * PACK], BF16)
             nc.vector.tensor_tensor(
-                hg_t[u][:, half, :].rearrange("p (c i t) -> p c t i", i=RUN, t=PACK),
-                by_runs((banks[u], r_t[u])[half][:]),
-                by_runs(of_unit(d_t, u)),
+                hg_t[u][:, half, :].rearrange("p (c i t) -> p c t i", i=LONG_RUN, t=PACK),
+                by_runs((banks[u], r_t[u])[half][:], LONG_RUN),
+                by_runs(of_unit(d_t, u), LONG_RUN),
                 MULT,
             )
 
@@ -365,9 +366,9 @@ def tile_list_desk_stress_results_kernel(tc, tab_words, tab_scales, tab2_words, 
         v_product(0, H)
         v_product(1, G)
         size_product(pair, FUSED, low)
-        size_product(pair, SCALED, high)
         v_quant(0)
         wd_quant(0, CUT, N)
+        size_product(pair, SCALED, high)
         v_quant(1)
         v_product(2, G)
         wd_cast_pool("r2", 1, 0, CUT)

from contextlib import ExitStack

import concourse.mybir as mybir

K, T, S, T2, S2, N = 1536, 4096, 1024, 2048, 512, 512
FLOPS = 2 * K * S * S2 + 2 * 2 * S * N * S2

F32 = mybir.dt.float32
BF16 = mybir.dt.bfloat16
I32 = mybir.dt.int32
U32 = mybir.dt.uint32
U16 = mybir.dt.uint16
U8 = mybir.dt.uint8
FP8X4 = mybir.dt.float8_e4m3fn_x4
FP4X4 = mybir.dt.float4_e2m1fn_x4
ACT = mybir.ActivationFunctionType
MULT = mybir.AluOpType.mult
ADD = mybir.AluOpType.add

P = 128
PACK = 4
PASS = P * PACK
KP = K // PASS
IB = S // PASS
JW = 128
JB = S2 // JW
NT = N // P
UNITS = JB * IB
LAST = UNITS - 1
QUADRANT = 32
ROWS = 4
LIST_ROWS = 16
RUN = 4
LONG_RUN = 8
H, G = 0, 1
ROW_STEP = 4
PASS2_ROW = 33
LAP = 256
LINE = 256
AT_SCALES2 = 0
AT_TAB_2 = T2 - LAP
AT_WD = AT_TAB_2 - LAP
AT_SIZE = AT_WD + 4 * T
AT_LATE = AT_TAB_2 + 4 * T
AT_TAB_1 = AT_LATE + S + S2 - LAP
AT_TAB2_1 = AT_TAB_1 + LAP
AT_TAB2_2 = AT_TAB2_1 + 4 * T2
AT_DEALT = AT_TAB2_2 + 4 * T2
AT_TAB2_0 = AT_DEALT + 4 * S2
AT_TAB_0 = AT_TAB2_0 + 4 * T2 - LAP
FUSED, SCALED, ON_SCALAR = 0, 1, 2
FIRST = 128
CUT = 320
WIDTHS = (256, 128, 64)
TURNS = 30


def tile_list_desk_stress_results_kernel(tc, tab_words, tab_scales, tab2_words, tab2_scales, offs, offs2, size, wd, w4_words, w4_scales, out):
    nc = tc.nc
    with ExitStack() as ctx:
        keep = ctx.enter_context(tc.tile_pool(name="keep", bufs=1))
        laid = ctx.enter_context(tc.tile_pool(name="laid", bufs=1))
        ring = ctx.enter_context(tc.tile_pool(name="ring", bufs=TURNS))
        psum = ctx.enter_context(tc.psum_pool(name="psum", bufs=1))

        idx = keep.tile([P, S // LIST_ROWS], U16, name="idx")
        idx2 = keep.tile([P, S2 // LIST_ROWS], U16, name="idx2")
        tabs = keep.tile([P, T], U8, name="tabs", align_bytes=LINE)
        tab2s = laid.tile([P, T2], U8, name="tab2s", offset=AT_SCALES2)
        picked = keep.tile([P, S + S2], U8, name="picked", align_bytes=64)
        dealt = laid.tile([P, S + S2], U8, name="dealt", offset=AT_DEALT)
        staged = keep.tile([P, S + S2], U8, name="staged", align_bytes=LINE)
        early = keep.tile([P, S + S2], U8, name="early", align_bytes=LINE)
        planes = {0: early, 1: early}
        wds = [keep.tile([P, N], U8, name="wds%d" % b, align_bytes=64) for b in range(IB)]
        tabw, tab2w, vw, v2w, wdraw, wdw = {}, {}, {}, {}, {}, {}
        one_in = laid.tile([P, 1], F32, name="one_in", offset=AT_TAB_1)
        one = keep.tile([P, 1], F32, name="one")

        nc.vector.memset(tab2s[:].bitcast(I32), 0)
        nc.vector.memset(tabs[:].bitcast(I32), 0)
        nc.gpsimd.memset(one_in[:], 1.0)
        nc.scalar.activation(one[:], one_in[:], ACT.Abs_reciprocal_sqrt)

        def load_words(tile, words):
            nc.sync.dma_start(tile[:], words.rearrange("p t i -> p (t i)").bitcast(I32))
            return tile

        def load_scale_rows(dst, scales):
            nc.sync.dma_start(dst[0:P:ROW_STEP, :].bitcast(I32), scales[0:2].rearrange("a q t -> q a t").bitcast(I32))
            nc.sync.dma_start(dst[PASS2_ROW : PASS2_ROW + 16 * ROW_STEP : ROW_STEP, :].bitcast(I32), scales[2].bitcast(I32))

        def place_rows(a, row, src, queue):
            queue.dma_start(planes[a][ROWS * a + row : P : QUADRANT, :].bitcast(I32), src.bitcast(I32))

        def gather_v(a, lo, hi):
            picks = keep.tile([P, (hi - lo) * PASS], U32, name="vw%d_%d" % (a, lo), align_bytes=64)
            nc.vector.tensor_copy(
                picks[:].rearrange("p (b t m) -> p b m t", m=P, t=PACK),
                tabw[a][:].bitcast(U32).indirect(idx[:, lo * PASS // LIST_ROWS : hi * PASS // LIST_ROWS]),
            )
            for b in range(lo, hi):
                vw[a, b] = picks[:, (b - lo) * PASS : (b - lo + 1) * PASS]

        def gather_v2(a, lo, hi, picks=None):
            if picks is None:
                picks = keep.tile([P, hi - lo], U32, name="v2w%d_%d" % (a, lo), align_bytes=64)
            nc.vector.tensor_copy(picks[:], tab2w[a][:].bitcast(U32).indirect(idx2[:, lo // LIST_ROWS : hi // LIST_ROWS]))
            for jb in range(lo // JW, hi // JW):
                v2w[a, jb] = picks[:, jb * JW - lo : (jb + 1) * JW - lo]

        tab2w[0] = load_words(laid.tile([P, T2], I32, name="tab2w0", offset=AT_TAB2_0), tab2_words[0])
        nc.sync.dma_start(idx2[:], offs2)
        nc.sync.dma_start(idx[:], offs)
        load_scale_rows(tab2s, tab2_scales)
        load_scale_rows(tabs, tab_scales)
        tabw[1] = load_words(laid.tile([P, T], I32, name="tabw1", offset=AT_TAB_1), tab_words[1])

        nc.vector.tensor_copy(picked[:, S:], tab2s[:].indirect(idx2[:]))
        tabw[2] = load_words(laid.tile([P, T], I32, name="tabw2", offset=AT_TAB_2), tab_words[2])
        nc.vector.tensor_copy(picked[:, :S], tabs[:].indirect(idx[:]))
        nc.vector.tensor_copy(dealt[:, S:].bitcast(I32), picked[:, S:].bitcast(I32))
        nc.vector.tensor_copy(
            dealt[:, :S].rearrange("p (b t m) -> p b t m", b=IB, t=PACK),
            picked[:, :S].rearrange("p (b m t) -> p b t m", b=IB, t=PACK),
        )
        nc.vector.tensor_copy(early[:].bitcast(I32), dealt[:].bitcast(I32))
        nc.vector.tensor_copy(staged[:].bitcast(I32), dealt[:].bitcast(I32))
        for a in range(KP - 1):
            for row in range(1, ROWS):
                place_rows(a, row, staged[ROW_STEP * (2 * row + a) : P : QUADRANT, :], nc.scalar)
        gather_v2(0, 0, S2, laid.tile([P, S2], U32, name="v2w0", offset=AT_DEALT))
        tabw[0] = load_words(laid.tile([P, T], I32, name="tabw0", offset=AT_TAB_0), tab_words[0])
        gather_v(1, 0, IB)
        tab2w[1] = load_words(laid.tile([P, T2], I32, name="tab2w1", offset=AT_TAB2_1), tab2_words[1])
        tab2w[2] = load_words(laid.tile([P, T2], I32, name="tab2w2", offset=AT_TAB2_2), tab2_words[2])
        late = laid.tile([P, S + S2], U8, name="late", offset=AT_LATE)
        planes[KP - 1] = late
        nc.vector.memset(late[:].bitcast(I32), 0)
        for row in range(ROWS):
            src = PASS2_ROW + row * ROW_STEP
            place_rows(KP - 1, row, staged[src : src + 3 * ROWS * ROW_STEP + 1 : ROWS * ROW_STEP, :], nc.sync)
        gather_v(2, 0, IB)
        for b in range(IB):
            gather_v(0, b, b + 1)
        gather_v2(1, 0, JW)
        gather_v2(1, JW, S2)

        def wd_rows(b):
            return wd[b * PASS : (b + 1) * PASS, :].rearrange("(p t) n -> p t n", t=PACK)

        for b in range(IB):
            wdraw[b] = laid.tile([P, PACK, N], F32, name="wdraw%d" % b, offset=AT_WD + b * 4 * PACK * N)
        nc.sync.dma_start(wdraw[0][:, :, :FIRST], wd_rows(0)[:, :, :FIRST])
        sz = laid.tile([P, IB, PACK], F32, name="sz", offset=AT_SIZE)
        nc.sync.dma_start(sz[:], size.rearrange("(b p t) -> p b t", b=IB, t=PACK))
        nc.sync.dma_start(wdraw[0][:, :, FIRST:CUT], wd_rows(0)[:, :, FIRST:CUT])
        nc.sync.dma_start(wdraw[0][:, :, CUT:], wd_rows(0)[:, :, CUT:])
        nc.sync.dma_start(wdraw[1][:], wd_rows(1))

        units = [(0, 0), (0, 1), (1, 0), (2, 0), (1, 1), (2, 1), (3, 1), (3, 0)]

        def c_pass(u, a):
            jb, b = units[u]
            for t in range(PACK):
                icols = slice(b * PASS + t * P, b * PASS + (t + 1) * P)
                nc.tensor.matmul_mx(
                    out=banks[u][:, t, :],
                    lhsT=vw[a, b][:, t * P : (t + 1) * P].bitcast(FP8X4),
                    lhsT_scale=planes[a][ROWS * a :, icols],
                    rhs=v2w[a, jb].bitcast(FP8X4),
                    rhs_scale=planes[a][ROWS * a :, S + jb * JW : S + (jb + 1) * JW],
                    start=(a == orders[u][0] and t == 0),
                    stop=(a == orders[u][-1] and t == PACK - 1),
                )

        banks = [psum.tile([P, PACK, JW], F32, name="bank%d" % u, tag="bank%d" % u) for u in range(UNITS)]
        ahead = {0: (0, 1), 1: (0, 1), 2: (0,), 3: (0,)}
        orders = [ahead.get(u, ()) + (KP - 1,) + tuple(a for a in range(KP - 1) if a not in ahead.get(u, ())) for u in range(UNITS)]
        for u in (0, 2, 3, 1):
            c_pass(u, 0)
        for u in (0, 1):
            c_pass(u, 1)

        gather_v2(KP - 1, 0, JW)
        gather_v2(KP - 1, JW, S2)
        w4w = laid.tile([P, IB, 2 * N], U8, name="w4w", offset=AT_TAB2_2, align_bytes=LINE)
        nc.sync.dma_start(w4w[:].bitcast(I32), w4_words.rearrange("b p e -> p b e").bitcast(I32))

        r_t, y_t, w_t, d_t, hg_t, hgw, hgs, bf_t = {}, {}, {}, {}, {}, {}, {}, {}

        def in_turn(shape, dtype):
            return ring.tile(shape, dtype, name="turn", tag="turn", align_bytes=64)

        def wide(name, us):
            return keep.tile([P, PACK, len(us) * JW], F32, name=name, tag=name, align_bytes=64)

        def activate(dst, src, parts, func, ts=range(PACK), **operands):
            step = len(ts) // parts
            for lo in range(ts[0], ts[-1] + 1, step):
                nc.scalar.activation(dst[:, lo : lo + step, :], src[:, lo : lo + step, :], func, **operands)

        def s_abs(u, parts=1):
            r_t[u] = keep.tile([P, PACK, JW], F32, name="r%d" % u, tag="r%d" % u, align_bytes=64)
            activate(r_t[u], banks[u], parts, ACT.Abs)

        def s_root(us, u, parts=1):
            if us not in y_t:
                y_t[us] = wide("y%d" % us[0], us)
            lo = us.index(u) * JW
            activate(y_t[us][:, :, lo : lo + JW], r_t[u], parts, ACT.Abs_reciprocal_sqrt, bias=one[:])

        def s_square(us, parts=1, ts=range(PACK)):
            w_t[us] = wide("w%d" % us[0], us)
            activate(w_t[us], y_t[us], parts, ACT.Square, ts)

        def size_product(us, how, ts=range(PACK)):
            if len(us) > 1 and us not in d_t:
                d_t[us] = wide("r0", us)
            if us not in d_t:
                d_t[us] = in_turn([P, PACK, len(us) * JW], F32)
            for t in ts:
                scale = sz[:, units[us[0]][1], t : t + 1]
                if how == SCALED:
                    nc.vector.tensor_scalar(out=d_t[us][:, t, :], in0=w_t[us][:, t, :], scalar1=scale, scalar2=None, op0=MULT)
                elif how == ON_SCALAR:
                    nc.scalar.activation(d_t[us][:, t, :], w_t[us][:, t, :], ACT.Copy, scale=scale)
                else:
                    nc.vector.scalar_tensor_tensor(
                        out=d_t[us][:, t, :], in0=y_t[us][:, t, :], scalar=scale, in1=y_t[us][:, t, :], op0=MULT, op1=MULT
                    )

        def of_unit(tiles, u):
            us = [us for us in tiles if u in us][0]
            lo = us.index(u) * JW
            return tiles[us][:, :, lo : lo + JW]

        def by_runs(src, run=RUN):
            return src.rearrange("p t (c i) -> p c t i", i=run)

        def v_product(u, half):
            if u not in hg_t:
                hg_t[u] = in_turn([P, 2, JW * PACK], BF16)
            nc.vector.tensor_tensor(
                hg_t[u][:, half, :].rearrange("p (c i t) -> p c t i", i=LONG_RUN, t=PACK),
                by_runs((banks[u], r_t[u])[half][:], LONG_RUN),
                by_runs(of_unit(d_t, u), LONG_RUN),
                MULT,
            )

        def v_quant(u, halves=None):
            hgw[u] = in_turn([P, 2 * JW], U32)
            hgs[u] = keep.tile([P, 2 * JW], U8, name="hgs%d" % u, align_bytes=64)
            if halves is None:
                nc.vector.quantize_mx(out=hgw[u][:].bitcast(FP8X4), scales=hgs[u][:], in_=hg_t[u][:].rearrange("p w c -> p (w c)"))
            else:
                for half in halves:
                    cols = slice(half * JW, (half + 1) * JW)
                    nc.vector.quantize_mx(out=hgw[u][:, cols].bitcast(FP8X4), scales=hgs[u][:, cols], in_=hg_t[u][:, half, :])

        def wd_cast(dst, b, lo, hi):
            nc.vector.tensor_copy(dst[:].rearrange("p (c i) t -> p c t i", i=RUN), by_runs(wdraw[b][:, :, lo:hi]))
            bf_t[b, lo] = dst

        def wd_cast_pool(tag, b, lo, hi):
            dst = keep.tile([P, hi - lo, PACK], BF16, name="bf" + tag, tag=tag, align_bytes=64)
            src = wdraw[b][:, :, lo:hi].rearrange("p t n -> p n t")
            nc.gpsimd.tensor_scalar(out=dst[:], in0=src, scalar1=1.0, scalar2=0.0, op0=MULT, op1=ADD)
            bf_t[b, lo] = dst

        def wd_quant(b, lo, hi):
            if b not in wdw:
                wdw[b] = in_turn([P, N], U32)
            at = lo
            for width in WIDTHS:
                if hi - at >= width:
                    src = bf_t[b, lo][:, at - lo : at - lo + width, :].rearrange("p n t -> p (n t)")
                    nc.vector.quantize_mx(out=wdw[b][:, at : at + width].bitcast(FP8X4), scales=wds[b][:, at : at + width], in_=src)
                    at = at + width

        def option_pass(dst, nt, u, start):
            b = units[u][1]
            nc.tensor.matmul_mx(
                out=dst, lhsT=w4w[:, b, 2 * nt * P : 2 * (nt + 1) * P].bitcast(FP4X4), lhsT_scale=w4s[:, b, nt * P : (nt + 1) * P],
                rhs=hgw[u][:, JW : 2 * JW].bitcast(FP8X4), rhs_scale=hgs[u][:, JW : 2 * JW], start=start, stop=False,
            )

        def linear_pass(dst, nt, u, stop):
            ch = units[u][1]
            wcols = slice(nt * P, (nt + 1) * P)
            nc.tensor.matmul_mx(
                out=dst, lhsT=wdw[ch][:, wcols].bitcast(FP8X4), lhsT_scale=wds[ch][:, wcols],
                rhs=hgw[u][:, 0:JW].bitcast(FP8X4), rhs_scale=hgs[u][:, 0:JW], start=False, stop=stop,
            )

        out_v = out.rearrange("(nt p) j -> p nt j", p=P)
        half_nt = NT // 2

        def out_sum(nts, jbs, bank):
            acc = psum.tile([P, len(nts), len(jbs) * JW], F32, name="out%d" % bank, tag="bank%d" % bank)
            steps = [(u, kind) for u in range(UNITS) if units[u][0] in jbs for kind in (G, H)]
            if LAST not in [u for u, kind in steps]:
                steps = [s for s in steps if s[1] == G or units[s[0]][1] == 0] + [s for s in steps if s[1] == H and units[s[0]][1] == 1]
            for k, (u, kind) in enumerate(steps):
                for n, nt in enumerate(nts):
                    lo = (units[u][0] - jbs[0]) * JW
                    dst = acc[:, n, lo : lo + JW]
                    if kind == G:
                        option_pass(dst, nt, u, k == 0 and n == 0)
                    else:
                        linear_pass(dst, nt, u, k == len(steps) - 1 and n == len(nts) - 1)
            return acc

        def store(acc, nts, jbs, copy, queue):
            res = keep.tile([P, len(nts), len(jbs) * JW], F32, name="res%d_%d" % (nts[0], jbs[0]), align_bytes=LINE)
            copy(res[:], acc)
            queue.dma_start(out_v[:, nts[0] : nts[-1] + 1, jbs[0] * JW : (jbs[-1] + 1) * JW], res[:])

        wd_cast(keep.tile([P, FIRST, PACK], BF16, name="bf0", align_bytes=64), 0, 0, FIRST)
        for u in range(UNITS):
            for a in orders[u][len(ahead.get(u, ())) :]:
                c_pass(u, a)
        w4s = late[:, 0 : IB * N].rearrange("p (b n) -> p b n", b=IB)
        for quadrant in range(P // QUADRANT):
            nc.sync.dma_start(
                w4s[QUADRANT * quadrant : QUADRANT * quadrant + ROWS, :, :].bitcast(I32),
                w4_scales[:, ROWS * quadrant : ROWS * (quadrant + 1), :].rearrange("b r n -> r b n").bitcast(I32),
            )

        pair = (2, 3)
        low, high = range(0, PACK // 2), range(PACK // 2, PACK)
        for u in (0, 1):
            s_abs(u, 2)
            s_root((u,), u, 2)
        for u in pair:
            s_abs(u)
        for u in pair:
            s_root(pair, u)
        s_abs(4)
        s_square(pair, 1, high)
        s_abs(5)
        for u in (4, 5):
            s_root((u,), u)
        for u in (4, 5):
            s_square((u,))
        size_product((4,), ON_SCALAR)
        s_abs(6)
        size_product((5,), ON_SCALAR)
        s_root((6,), 6)
        s_abs(7)
        s_square((6,), 2)
        size_product((6,), ON_SCALAR)
        s_root((7,), 7, 2)
        s_square((7,), 2)
        size_product((7,), ON_SCALAR)

        wd_quant(0, 0, FIRST)
        size_product((0,), FUSED, low)
        wd_cast(in_turn([P, CUT - FIRST, PACK], BF16), 0, FIRST, CUT)
        size_product((0,), FUSED, high)
        wd_quant(0, FIRST, CUT)
        size_product((1,), FUSED)
        wd_cast_pool("y1", 0, CUT, N)
        v_product(0, G)
        v_product(1, H)
        v_product(0, H)
        v_product(1, G)
        size_product(pair, FUSED, low)
        v_quant(0)
        wd_quant(0, CUT, N)
        size_product(pair, SCALED, high)
        v_quant(1)
        v_product(2, G)
        wd_cast_pool("r2", 1, 0, CUT)
        v_product(3, G)
        for u in (2, 3, 4):
            v_product(u, H)
        v_product(4, G)
        for u in (2, 4):
            v_quant(u)
        wd_quant(1, 0, CUT)
        v_product(5, G)
        wd_cast_pool("r5", 1, CUT, N)
        v_quant(3)
        for u in (5, 6):
            v_product(u, H)
        v_quant(5)
        v_product(6, G)
        wd_quant(1, CUT, N)
        v_quant(6)
        v_product(LAST, G)
        v_product(LAST, H)
        v_quant(LAST, (G, H))

        groups = [((0, 1), (0, 1), 1), ((0, 1), (2,), 2), ((2, 3), (0, 1), 0), ((2, 3), (2,), 3)]
        sums = [out_sum(*group) for group in groups]
        for n in range(half_nt):
            store(sums[0][:, n : n + 1, :], (n,), groups[0][1], nc.scalar.copy, nc.sync)
        for acc, (nts, jbs, bank) in list(zip(sums, groups))[1:]:
            store(acc[:], nts, jbs, nc.scalar.copy, nc.sync)
        last = [out_sum((nt,), (JB - 1,), bank) for nt, bank in enumerate((4, 5, 6, 1))]
        for lo, queue in ((0, nc.sync), (half_nt, nc.scalar)):
            res = keep.tile([P, half_nt, JW], F32, name="res_last%d" % lo, align_bytes=LINE)
            nc.vector.tensor_copy(res[:, 0:1, :], last[lo][:])
            nc.scalar.copy(res[:, 1:2, :], last[lo + 1][:])
            queue.dma_start(out_v[:, lo : lo + half_nt, (JB - 1) * JW :], res[:])
